import numpy as np
import ml_dtypes


def mxq(x, axis, fmt="e4m3"):
    dtype, down = {"e4m3": (ml_dtypes.float8_e4m3fn, 7), "e5m2": (ml_dtypes.float8_e5m2, 14)}[fmt]
    v = np.moveaxis(np.asarray(x, np.float32).astype(ml_dtypes.bfloat16).astype(np.float64), axis, -1)
    blocks = v.reshape(v.shape[:-1] + (-1, 32))
    amax = np.abs(blocks).max(-1, keepdims=True)
    byte = np.maximum(np.where(amax > 0, np.frexp(amax)[1] - 1 + 127, 0) - down, 1)
    scale = np.exp2(byte - 127.0)
    codes = (blocks / scale).astype(np.float32).astype(dtype).astype(np.float64)
    return np.moveaxis((codes * scale).reshape(v.shape), -1, axis)


WIDE = False


def mx_kscale(k):
    if not WIDE:
        return np.ones(k)
    levels = np.array([24, -24, 12, -12, 0])
    if k % 512:
        return np.exp2(np.random.permutation(np.resize(levels, k // 32))).repeat(32)
    a = np.empty((k // 512, 16))
    for p in range(k // 512):
        a[p, :8] = np.random.permutation(np.resize(levels, 8))
        for g in range(8):
            far = levels[np.abs(levels - a[p, g]) >= 10]
            a[p, g + 8] = far[np.random.randint(len(far))]
    return np.exp2(a.ravel()).repeat(32)


def f64(x):
    return np.asarray(x).astype(np.float64)


def striped(idx):
    return np.tile(idx.reshape(-1, 16).T, (8, 1)).astype(np.uint16)


def unstriped(offs):
    return offs[:16].T.reshape(-1).astype(np.int64)


E2M1 = np.array([0.0, 0.5, 1.0, 1.5, 2.0, 3.0, 4.0, 6.0, -0.0, -0.5, -1.0, -1.5, -2.0, -3.0, -4.0, -6.0])


def pack_weight(w, fmt):
    k, n = w.shape
    w = f64(np.asarray(w, np.float32).astype(ml_dtypes.bfloat16)).reshape(k // 32, 32, n)
    amax = np.abs(w).max(1)
    if fmt == "e4m3":
        byte = np.frexp(amax)[1] - 1 + 127 - 7
    else:
        mant, ex = np.frexp(amax / 6.0)
        byte = np.where(mant > 0.5, ex, ex - 1) + 127
    byte = np.clip(np.where(amax > 0, byte, 1), 1, 254)
    scaled = (w * np.exp2(127.0 - byte)[:, None, :]).reshape(k, n).astype(np.float32)
    by_word = np.ascontiguousarray(scaled.reshape(k // 512, 128, 4, n).transpose(0, 1, 3, 2))
    if fmt == "e4m3":
        words = by_word.astype(ml_dtypes.float8_e4m3fn).view(np.uint8)
    else:
        c = by_word.astype(ml_dtypes.float4_e2m1fn).view(np.uint8) & 0xF
        words = (c[..., 0::2] | (c[..., 1::2] << 4)).reshape(k // 512, 128, 2 * n)
    return np.ascontiguousarray(words), np.ascontiguousarray(byte.astype(np.uint8).reshape(k // 512, 16, n))


def unpack_weight(words, scales, fmt):
    g, _, n = scales.shape
    words = np.ascontiguousarray(words).reshape(g, 128, n, -1)
    if fmt == "e4m3":
        vals = words.view(ml_dtypes.float8_e4m3fn).astype(np.float64)
    else:
        nib = np.empty((g, 128, n, 4), np.uint8)
        nib[..., 0::2] = words & 0xF
        nib[..., 1::2] = words >> 4
        vals = E2M1[nib]
    vals = vals * np.repeat(np.exp2(scales.astype(np.float64) - 127.0), 8, axis=1)[..., None]
    return vals.transpose(0, 1, 3, 2).reshape(g * 512, n)


def pack_table4(v):
    words, scales = pack_weight(v, "e2m1")
    g, t = words.shape[0] // 2, v.shape[1]
    return np.ascontiguousarray(words.reshape(g, 2, 128, t, 2).transpose(0, 2, 3, 1, 4).reshape(g, 128, t, 4)), scales


def unpack_table4(words, scales):
    g, _, t, _ = words.shape
    return unpack_weight(words.reshape(g, 128, t, 2, 2).transpose(0, 3, 1, 2, 4).reshape(2 * g, 128, 2 * t), scales, "e2m1")


K, F, N, T, J = 1024, 1024, 256, 4096, 2048


def setup_inputs():
    n = np.random.standard_normal
    s = mx_kscale(K)[:, None]
    u = mx_kscale(F)[:, None]
    p_tab = pack_table4(n((K, T)) * s)
    p_fb = pack_weight(np.abs(n((F, N))) / F / u, "e4m3")
    return {
        "tab_words": p_tab[0],
        "tab_scales": p_tab[1],
        "co": (n((K, F)) / np.sqrt(K) / s).astype(np.float32),
        "si": (n((K, F)) / np.sqrt(K) / s).astype(np.float32),
        "gn": (np.random.uniform(0.5, 2.0, F) * u[:, 0]).astype(np.float32),
        "fb_words": p_fb[0],
        "fb_scales": p_fb[1],
        "offs": striped(np.random.permutation(T)[:J]),
    }


def reference(tab_words, tab_scales, co, si, gn, fb_words, fb_scales, offs):
    idx = unstriped(offs)
    tab_ = unpack_table4(tab_words, tab_scales)[:, idx]
    co_ = mxq(f64(co), 0, "e4m3")
    si_ = mxq(f64(si), 0, "e4m3")
    re = co_.T @ tab_
    im = si_.T @ tab_
    h = f64(gn)[:, None] * ((re) ** 2 + (im) ** 2)
    h_ = mxq(h, 0, "e4m3")
    fb_ = unpack_weight(fb_words, fb_scales, "e4m3")
    y = fb_.T @ h_
    return np.log(y + 1.0)

@@ -1,0 +1,222 @@
+from contextlib import ExitStack
+
+import concourse.mybir as mybir
+
+K, F, N, T, J = 1024, 1024, 256, 4096, 2048
+FLOPS = 2 * (2 * K * F * J + F * N * J)
+
+F32 = mybir.dt.float32
+BF16 = mybir.dt.bfloat16
+I32 = mybir.dt.int32
+U32 = mybir.dt.uint32
+U16 = mybir.dt.uint16
+U8 = mybir.dt.uint8
+FP8X4 = mybir.dt.float8_e4m3fn_x4
+FP4X4 = mybir.dt.float4_e2m1fn_x4
+ALU = mybir.AluOpType
+ACT = mybir.ActivationFunctionType
+
+P = 128
+PACK = 4
+PASS = P * PACK
+JT = 512
+NJ = J // JT
+LIST_COLS = JT // 16
+SMALLEST_GAIN = 2.0 ** -100
+
+
+def tile_list_meltab_log_kernel(
+    tc, tab_words, tab_scales, co, si, gn, fb_words, fb_scales, offs, out
+):
+    nc = tc.nc
+    with ExitStack() as ctx:
+        keep = ctx.enter_context(tc.tile_pool(name="keep", bufs=1))
+        ring = ctx.enter_context(tc.tile_pool(name="ring", bufs=2))
+        psum = ctx.enter_context(tc.psum_pool(name="psum", bufs=1))
+
+        offsets = keep.tile([P, J // 16], U16, name="offsets")
+        nc.sync.dma_start(offsets[:], offs)
+
+        scale_store = keep.tile([P, T], U8, name="scale_store", align_bytes=64)
+        for q in range(4):
+            (nc.vector, nc.gpsimd)[q % 2].memset(scale_store[32 * q : 32 * q + 24, :].bitcast(I32), 0)
+            nc.sync.dma_start(
+                scale_store[32 * q + 24 : 32 * q + 32, :].bitcast(I32),
+                tab_scales[:, 4 * q : 4 * q + 4, :].bitcast(I32),
+            )
+        word_store = keep.tile([P, T], I32, name="word_store", align_bytes=64)
+        nc.sync.dma_start(word_store[:], tab_words[0].rearrange("p t i -> p (t i)").bitcast(I32))
+
+        gain = keep.tile([P, 2, PACK], F32, name="gain")
+        nc.scalar.dma_start(gain[:], gn.rearrange("(b p t) -> p b t", b=2, t=PACK))
+
+        raw = {}
+        def load_weight(w, a, b):
+            raw[w, a, b] = ring.tile([P, PACK, PASS], F32, name="raw", bufs=4)
+            rows = (co, si)[w][a * PASS : (a + 1) * PASS, b * PASS : (b + 1) * PASS]
+            nc.sync.dma_start(raw[w, a, b][:], rows.rearrange("(p i) c -> p i c", i=PACK))
+
+        for b in range(2):
+            for w in range(2):
+                for a in range(2):
+                    load_weight(w, a, b)
+
+        fb_codes = keep.tile([P, 2, N], I32, name="fb_codes", align_bytes=64)
+        nc.sync.dma_start(fb_codes[:], fb_words.rearrange("b p n i -> p b (n i)").bitcast(I32))
+        fb_plane = keep.tile([P, 2, N], U8, name="fb_plane", align_bytes=64)
+        nc.gpsimd.memset(fb_plane[:].bitcast(I32), 0)
+        for q in range(4):
+            nc.sync.dma_start(
+                fb_plane[32 * q : 32 * q + 4, :, :].bitcast(I32),
+                fb_scales[:, 4 * q : 4 * q + 4, :].rearrange("b r n -> r b n").bitcast(I32),
+            )
+
+        g8 = gain[:].rearrange("p b t -> p (b t)")
+        def small(name, dtype=F32):
+            return keep.tile([P, 2 * PACK], dtype, name=name)
+        mag, minus_two, sign = small("mag"), small("minus_two"), small("sign", BF16)
+        inv, guess, step, root = small("inv"), small("guess"), small("step"), small("root")
+        nc.vector.scalar_tensor_tensor(mag[:], g8, -1.0, g8, ALU.mult, ALU.max)
+        nc.scalar.activation(inv[:], mag[:], ACT.Abs_reciprocal_sqrt, bias=SMALLEST_GAIN)
+        nc.vector.tensor_scalar(minus_two[:], g8, 0.0, -2.0, ALU.is_lt, ALU.mult)
+        nc.vector.tensor_scalar(sign[:], minus_two[:], 1.0, None, ALU.add)
+        nc.vector.tensor_tensor(guess[:], mag[:], inv[:], ALU.mult)
+        nc.vector.scalar_tensor_tensor(step[:], guess[:], -0.5, inv[:], ALU.mult, ALU.mult)
+        nc.vector.scalar_tensor_tensor(root[:], step[:], 1.5, guess[:], ALU.add, ALU.mult)
+        warm = keep.tile([P, 1], F32, name="warm")
+        nc.scalar.activation(warm[:], inv[:, 0:1], ACT.Ln, bias=1.0)
+
+        picked_scales = keep.tile([P, J], U8, name="picked_scales", align_bytes=64)
+        nc.vector.tensor_copy(picked_scales[:], scale_store[:].indirect(offsets[:]))
+        tab_planes = []
+        for a in range(2):
+            plane = keep.tile([P, J], U8, name=f"tab_plane{a}", align_bytes=64)
+            nc.gpsimd.memset(plane[:].bitcast(I32), 0)
+            first = 24 + 4 * a
+            nc.gpsimd.dma_start(plane[0:100, :].bitcast(I32), picked_scales[first : first + 100, :].bitcast(I32))
+            tab_planes.append(plane)
+
+        frames = {}
+        def pick_frames(jt):
+            pairs = ring.tile([P, JT], U32, name="pairs")
+            cols = offsets[:, jt * LIST_COLS : (jt + 1) * LIST_COLS]
+            nc.vector.tensor_copy(pairs[:], word_store[:].bitcast(U32).indirect(cols))
+            frames[jt] = keep.tile([P, 2, JT], U16, name=f"frames{jt}", align_bytes=64)
+            nc.vector.tensor_copy(frames[jt][:], pairs[:].bitcast(U16).rearrange("p (j d) -> p d j", d=2))
+
+        rounded, w_codes, w_plane = {}, {}, {}
+        def round_weight(w, a, b, engine):
+            rounded[w, a, b] = ring.tile([P, PACK * PASS], BF16, name="rounded", bufs=3, align_bytes=64)
+            dst = rounded[w, a, b][:].rearrange("p (t m i) -> p m i t", t=PACK, i=PACK)
+            src = raw[w, a, b][:].rearrange("p i (m t) -> p m i t", t=PACK)
+            if engine == "scalar":
+                nc.scalar.copy(dst, src)
+            else:
+                nc.vector.tensor_copy(dst, src)
+
+        def quantise_weight(w, a, b):
+            w_codes[w, a, b] = keep.tile([P, PASS], U32, name=f"w_codes{w}{a}{b}", align_bytes=64)
+            w_plane[w, a, b] = keep.tile([P, PASS], U8, name=f"w_plane{w}{a}{b}", align_bytes=64)
+            nc.vector.quantize_mx(w_codes[w, a, b][:].bitcast(FP8X4), w_plane[w, a, b][:], rounded[w, a, b][:])
+
+        squares = {}
+        def transform(w, b, j0, width):
+            jt, cols = j0 // JT, slice(j0 % JT, j0 % JT + width)
+            squares[w, b, j0] = ring.tile([P, PACK, width], F32, name=f"squares{w}", bufs=4 - w)
+            per_bank = JT // width
+            for t0 in range(0, PACK, per_bank):
+                acc = psum.tile([P, per_bank, width], F32, name="acc", bufs=6)
+                for t in range(t0, t0 + per_bank):
+                    for a in range(2):
+                        nc.tensor.matmul_mx(
+                            acc[:, t - t0, :],
+                            lhsT=w_codes[w, a, b][:, t * P : (t + 1) * P].bitcast(FP8X4),
+                            lhsT_scale=w_plane[w, a, b][:, t * P : (t + 1) * P],
+                            rhs=frames[jt][:, a, cols].bitcast(FP4X4),
+                            rhs_scale=tab_planes[a][:, j0 : j0 + width],
+                            start=(a == 0),
+                            stop=(a == 1),
+                        )
+                for t in range(t0, t0 + per_bank):
+                    nc.scalar.activation(
+                        squares[w, b, j0][:, t, :], acc[:, t - t0, :], ACT.Square,
+                        scale=root[:, PACK * b + t : PACK * b + t + 1],
+                    )
+
+        h_codes = [keep.tile([P, J], U32, name=f"h_codes{b}", align_bytes=64) for b in range(2)]
+        h_plane = [keep.tile([P, J], U8, name=f"h_plane{b}", align_bytes=64) for b in range(2)]
+        def power(b, j0, width):
+            piece = min(width, 256)
+            starts = range(0, width, piece)
+            h = {c: ring.tile([P, piece, PACK], BF16, name="h", bufs=6, align_bytes=64) for c in starts}
+            for c in starts:
+                nc.vector.tensor_tensor(
+                    h[c][:].rearrange("p (c i) t -> p c t i", i=4),
+                    squares[0, b, j0][:, :, c : c + piece].rearrange("p t (c i) -> p c t i", i=4),
+                    squares[1, b, j0][:, :, c : c + piece].rearrange("p t (c i) -> p c t i", i=4),
+                    ALU.add,
+                )
+            signs = sign[:, PACK * b : PACK * (b + 1)].unsqueeze(1).to_broadcast([P, piece, PACK])
+            for c in starts:
+                nc.vector.tensor_tensor(h[c][:], h[c][:], signs, ALU.mult)
+            for c in starts:
+                cols = slice(j0 + c, j0 + c + piece)
+                nc.vector.quantize_mx(
+                    h_codes[b][:, cols].bitcast(FP8X4), h_plane[b][:, cols], h[c][:].rearrange("p j t -> p (j t)")
+                )
+
+        def filters(j0, width):
+            cols = slice(j0, j0 + width)
+            per_bank = min(N // P, JT // width)
+            for n0 in range(0, N // P, per_bank):
+                y = psum.tile([P, per_bank, width], F32, name="y", bufs=2)
+                for nt in range(n0, n0 + per_bank):
+                    for b in range(2):
+                        nc.tensor.matmul_mx(
+                            y[:, nt - n0, :],
+                            lhsT=fb_codes[:, b, nt * P : (nt + 1) * P].bitcast(FP8X4),
+                            lhsT_scale=fb_plane[:, b, nt * P : (nt + 1) * P],
+                            rhs=h_codes[b][:, cols].bitcast(FP8X4),
+                            rhs_scale=h_plane[b][:, cols],
+                            start=(b == 0),
+                            stop=(b == 1),
+                        )
+                result = ring.tile([P, per_bank, width], F32, name="result", bufs=4)
+                nc.scalar.activation(result[:], y[:], ACT.Ln, bias=1.0)
+                rows = out[n0 * P : (n0 + per_bank) * P, cols]
+                nc.sync.dma_start(rows.rearrange("(n p) j -> p n j", p=P), result[:])
+
+        pick_frames(0)
+        round_weight(0, 0, 0, "scalar")
+        round_weight(0, 1, 0, "scalar")
+        quantise_weight(0, 0, 0)
+        quantise_weight(0, 1, 0)
+        pick_frames(1)
+        round_weight(1, 0, 0, "scalar")
+        transform(0, 0, 0, JT)
+        quantise_weight(1, 0, 0)
+        round_weight(1, 1, 0, "vector")
+        pick_frames(2)
+        quantise_weight(1, 1, 0)
+        transform(0, 0, JT, JT)
+        pick_frames(3)
+        transform(1, 0, 0, JT)
+        transform(1, 0, JT, JT)
+        for w in range(2):
+            for a in range(2):
+                round_weight(w, a, 1, "vector")
+                quantise_weight(w, a, 1)
+        power(0, 0, JT)
+        power(0, JT, JT)
+        for j0 in range(2 * JT, J, JT):
+            transform(0, 0, j0, JT)
+            transform(1, 0, j0, JT)
+            power(0, j0, JT)
+        spans = [(j0, JT) for j0 in range(0, J - JT, JT)] + [(j0, P) for j0 in range(J - JT, J, P)]
+        for i, (j0, width) in enumerate(spans):
+            transform(0, 1, j0, width)
+            transform(1, 1, j0, width)
+            power(1, j0, width)
+            if i > 0:
+                filters(*spans[i - 1])
+        filters(*spans[-1])

@@ -83,6 +83,10 @@ def tile_list_meltab_log_kernel(
         nc.vector.tensor_tensor(guess[:], mag[:], inv[:], ALU.mult)
         nc.vector.scalar_tensor_tensor(step[:], guess[:], -0.5, inv[:], ALU.mult, ALU.mult)
         nc.vector.scalar_tensor_tensor(root[:], step[:], 1.5, guess[:], ALU.add, ALU.mult)
+        signs = [keep.tile([P, 256, PACK], BF16, name=f"signs{b}") for b in range(2)]
+        for b in range(2):
+            row = sign[:, PACK * b : PACK * (b + 1)].unsqueeze(1).to_broadcast([P, 256, PACK])
+            nc.scalar.copy(signs[b][:], row)
         warm = keep.tile([P, 1], F32, name="warm")
         nc.scalar.activation(warm[:], inv[:, 0:1], ACT.Ln, bias=1.0)
 
@@ -107,12 +111,15 @@ def tile_list_meltab_log_kernel(
         rounded, w_codes, w_plane = {}, {}, {}
         def round_weight(w, a, b, engine):
             rounded[w, a, b] = ring.tile([P, PACK * PASS], BF16, name="rounded", bufs=3, align_bytes=64)
-            dst = rounded[w, a, b][:].rearrange("p (t m i) -> p m i t", t=PACK, i=PACK)
-            src = raw[w, a, b][:].rearrange("p i (m t) -> p m i t", t=PACK)
+            dst = rounded[w, a, b][:].rearrange("p (u v m i) -> p u m i v", u=2, v=2, i=PACK)
+            src = raw[w, a, b][:].rearrange("p i (m u v) -> p u m i v", u=2, v=2)
             if engine == "scalar":
                 nc.scalar.copy(dst, src)
-            else:
+            elif engine == "vector":
                 nc.vector.tensor_copy(dst, src)
+            else:
+                nc.scalar.copy(dst[:, 0], src[:, 0])
+                nc.vector.tensor_copy(dst[:, 1], src[:, 1])
 
         def quantise_weight(w, a, b):
             w_codes[w, a, b] = keep.tile([P, PASS], U32, name=f"w_codes{w}{a}{b}", align_bytes=64)
@@ -125,7 +132,7 @@ def tile_list_meltab_log_kernel(
             squares[w, b, j0] = ring.tile([P, PACK, width], F32, name=f"squares{w}", bufs=4 - w)
             per_bank = JT // width
             for t0 in range(0, PACK, per_bank):
-                acc = psum.tile([P, per_bank, width], F32, name="acc", bufs=6)
+                acc = psum.tile([P, per_bank, width], F32, name="bank", bufs=8)
                 for t in range(t0, t0 + per_bank):
                     for a in range(2):
                         nc.tensor.matmul_mx(
@@ -151,14 +158,13 @@ def tile_list_meltab_log_kernel(
             h = {c: ring.tile([P, piece, PACK], BF16, name="h", bufs=6, align_bytes=64) for c in starts}
             for c in starts:
                 nc.vector.tensor_tensor(
-                    h[c][:].rearrange("p (c i) t -> p c t i", i=4),
-                    squares[0, b, j0][:, :, c : c + piece].rearrange("p t (c i) -> p c t i", i=4),
-                    squares[1, b, j0][:, :, c : c + piece].rearrange("p t (c i) -> p c t i", i=4),
+                    h[c][:].rearrange("p (c i) t -> p c t i", i=2),
+                    squares[0, b, j0][:, :, c : c + piece].rearrange("p t (c i) -> p c t i", i=2),
+                    squares[1, b, j0][:, :, c : c + piece].rearrange("p t (c i) -> p c t i", i=2),
                     ALU.add,
                 )
-            signs = sign[:, PACK * b : PACK * (b + 1)].unsqueeze(1).to_broadcast([P, piece, PACK])
             for c in starts:
-                nc.vector.tensor_tensor(h[c][:], h[c][:], signs, ALU.mult)
+                nc.vector.tensor_tensor(h[c][:], h[c][:], signs[b][:, 0:piece, :], ALU.mult)
             for c in starts:
                 cols = slice(j0 + c, j0 + c + piece)
                 nc.vector.quantize_mx(
@@ -169,7 +175,7 @@ def tile_list_meltab_log_kernel(
             cols = slice(j0, j0 + width)
             per_bank = min(N // P, JT // width)
             for n0 in range(0, N // P, per_bank):
-                y = psum.tile([P, per_bank, width], F32, name="y", bufs=2)
+                y = psum.tile([P, per_bank, width], F32, name="bank", bufs=8)
                 for nt in range(n0, n0 + per_bank):
                     for b in range(2):
                         nc.tensor.matmul_mx(
@@ -188,7 +194,7 @@ def tile_list_meltab_log_kernel(
 
         pick_frames(0)
         round_weight(0, 0, 0, "scalar")
-        round_weight(0, 1, 0, "scalar")
+        round_weight(0, 1, 0, "both")
         quantise_weight(0, 0, 0)
         quantise_weight(0, 1, 0)
         pick_frames(1)
@@ -217,6 +223,7 @@ def tile_list_meltab_log_kernel(
             transform(0, 1, j0, width)
             transform(1, 1, j0, width)
             power(1, j0, width)
-            if i > 0:
-                filters(*spans[i - 1])
+            if i > 1:
+                filters(*spans[i - 2])
+        filters(*spans[-2])
         filters(*spans[-1])

@@ -52,7 +52,7 @@ def tile_list_meltab_log_kernel(
 
         raw = {}
         def load_weight(w, a, b):
-            raw[w, a, b] = ring.tile([P, PACK, PASS], F32, name="raw", bufs=4)
+            raw[w, a, b] = ring.tile([P, PACK, PASS], F32, name="raw", tag="raw", bufs=4, align_bytes=64)
             rows = (co, si)[w][a * PASS : (a + 1) * PASS, b * PASS : (b + 1) * PASS]
             nc.sync.dma_start(raw[w, a, b][:], rows.rearrange("(p i) c -> p i c", i=PACK))
 
@@ -61,10 +61,10 @@ def tile_list_meltab_log_kernel(
                 for a in range(2):
                     load_weight(w, a, b)
 
-        fb_codes = keep.tile([P, 2, N], I32, name="fb_codes", align_bytes=64)
+        fb_codes = ring.tile([P, 2, N], I32, name="fb_codes", tag="raw", bufs=4, align_bytes=64)
         nc.sync.dma_start(fb_codes[:], fb_words.rearrange("b p n i -> p b (n i)").bitcast(I32))
-        fb_plane = keep.tile([P, 2, N], U8, name="fb_plane", align_bytes=64)
-        nc.gpsimd.memset(fb_plane[:].bitcast(I32), 0)
+        fb_plane = ring.tile([P, 2, N], U8, name="fb_plane", tag="raw", bufs=4, align_bytes=64)
+        nc.vector.memset(fb_plane[:].bitcast(I32), 0)
         for q in range(4):
             nc.sync.dma_start(
                 fb_plane[32 * q : 32 * q + 4, :, :].bitcast(I32),
@@ -97,7 +97,7 @@ def tile_list_meltab_log_kernel(
             plane = keep.tile([P, J], U8, name=f"tab_plane{a}", align_bytes=64)
             nc.gpsimd.memset(plane[:].bitcast(I32), 0)
             first = 24 + 4 * a
-            nc.gpsimd.dma_start(plane[0:100, :].bitcast(I32), picked_scales[first : first + 100, :].bitcast(I32))
+            nc.scalar.dma_start(plane[0:100, :].bitcast(I32), picked_scales[first : first + 100, :].bitcast(I32))
             tab_planes.append(plane)
 
         frames = {}

@@ -38,12 +38,8 @@ def tile_list_meltab_log_kernel(
         nc.sync.dma_start(offsets[:], offs)
 
         scale_store = keep.tile([P, T], U8, name="scale_store", align_bytes=64)
-        for q in range(4):
-            (nc.vector, nc.gpsimd)[q % 2].memset(scale_store[32 * q : 32 * q + 24, :].bitcast(I32), 0)
-            nc.sync.dma_start(
-                scale_store[32 * q + 24 : 32 * q + 32, :].bitcast(I32),
-                tab_scales[:, 4 * q : 4 * q + 4, :].bitcast(I32),
-            )
+        nc.vector.memset(scale_store[0:96, :].bitcast(I32), 0)
+        nc.sync.dma_start(scale_store[96:128, :].bitcast(I32), tab_scales.rearrange("a z t -> z a t").bitcast(I32))
         word_store = keep.tile([P, T], I32, name="word_store", align_bytes=64)
         nc.sync.dma_start(word_store[:], tab_words[0].rearrange("p t i -> p (t i)").bitcast(I32))
 
@@ -52,7 +48,7 @@ def tile_list_meltab_log_kernel(
 
         raw = {}
         def load_weight(w, a, b):
-            raw[w, a, b] = ring.tile([P, PACK, PASS], F32, name="raw", tag="raw", bufs=4, align_bytes=64)
+            raw[w, a, b] = ring.tile([P, PACK, PASS], F32, name="raw", tag="raw", bufs=3, align_bytes=64)
             rows = (co, si)[w][a * PASS : (a + 1) * PASS, b * PASS : (b + 1) * PASS]
             nc.sync.dma_start(raw[w, a, b][:], rows.rearrange("(p i) c -> p i c", i=PACK))
 
@@ -61,10 +57,9 @@ def tile_list_meltab_log_kernel(
                 for a in range(2):
                     load_weight(w, a, b)
 
-        fb_codes = ring.tile([P, 2, N], I32, name="fb_codes", tag="raw", bufs=4, align_bytes=64)
+        fb_codes = ring.tile([P, 2, N], I32, name="fb_codes", tag="raw", bufs=3, align_bytes=64)
         nc.sync.dma_start(fb_codes[:], fb_words.rearrange("b p n i -> p b (n i)").bitcast(I32))
-        fb_plane = ring.tile([P, 2, N], U8, name="fb_plane", tag="raw", bufs=4, align_bytes=64)
-        nc.vector.memset(fb_plane[:].bitcast(I32), 0)
+        fb_plane = ring.tile([P, 2, N], U8, name="fb_plane", tag="raw", bufs=3, align_bytes=64)
         for q in range(4):
             nc.sync.dma_start(
                 fb_plane[32 * q : 32 * q + 4, :, :].bitcast(I32),
@@ -78,31 +73,21 @@ def tile_list_meltab_log_kernel(
         inv, guess, step, root = small("inv"), small("guess"), small("step"), small("root")
         nc.vector.scalar_tensor_tensor(mag[:], g8, -1.0, g8, ALU.mult, ALU.max)
         nc.scalar.activation(inv[:], mag[:], ACT.Abs_reciprocal_sqrt, bias=SMALLEST_GAIN)
-        nc.vector.tensor_scalar(minus_two[:], g8, 0.0, -2.0, ALU.is_lt, ALU.mult)
-        nc.vector.tensor_scalar(sign[:], minus_two[:], 1.0, None, ALU.add)
-        nc.vector.tensor_tensor(guess[:], mag[:], inv[:], ALU.mult)
-        nc.vector.scalar_tensor_tensor(step[:], guess[:], -0.5, inv[:], ALU.mult, ALU.mult)
-        nc.vector.scalar_tensor_tensor(root[:], step[:], 1.5, guess[:], ALU.add, ALU.mult)
-        signs = [keep.tile([P, 256, PACK], BF16, name=f"signs{b}") for b in range(2)]
-        for b in range(2):
-            row = sign[:, PACK * b : PACK * (b + 1)].unsqueeze(1).to_broadcast([P, 256, PACK])
-            nc.scalar.copy(signs[b][:], row)
         warm = keep.tile([P, 1], F32, name="warm")
         nc.scalar.activation(warm[:], inv[:, 0:1], ACT.Ln, bias=1.0)
 
         picked_scales = keep.tile([P, J], U8, name="picked_scales", align_bytes=64)
         nc.vector.tensor_copy(picked_scales[:], scale_store[:].indirect(offsets[:]))
-        tab_planes = []
-        for a in range(2):
-            plane = keep.tile([P, J], U8, name=f"tab_plane{a}", align_bytes=64)
-            nc.gpsimd.memset(plane[:].bitcast(I32), 0)
-            first = 24 + 4 * a
-            nc.scalar.dma_start(plane[0:100, :].bitcast(I32), picked_scales[first : first + 100, :].bitcast(I32))
-            tab_planes.append(plane)
+        tab_planes = keep.tile([P, 2, J], U8, name="tab_planes", align_bytes=64)
+        for q in range(4):
+            nc.scalar.dma_start(
+                tab_planes[32 * q : 32 * q + 4, :, :].bitcast(I32),
+                picked_scales[96 + 8 * q : 96 + 8 * q + 8, :].bitcast(I32),
+            )
 
         frames = {}
         def pick_frames(jt):
-            pairs = ring.tile([P, JT], U32, name="pairs")
+            pairs = ring.tile([P, JT], U32, name="pairs", tag="early" if jt < 2 else "held", bufs=2 if jt < 2 else 1, align_bytes=64)
             cols = offsets[:, jt * LIST_COLS : (jt + 1) * LIST_COLS]
             nc.vector.tensor_copy(pairs[:], word_store[:].bitcast(U32).indirect(cols))
             frames[jt] = keep.tile([P, 2, JT], U16, name=f"frames{jt}", align_bytes=64)
@@ -110,7 +95,10 @@ def tile_list_meltab_log_kernel(
 
         rounded, w_codes, w_plane = {}, {}, {}
         def round_weight(w, a, b, engine):
-            rounded[w, a, b] = ring.tile([P, PACK * PASS], BF16, name="rounded", bufs=3, align_bytes=64)
+            shared = engine == "both"
+            rounded[w, a, b] = ring.tile(
+                [P, PACK * PASS], BF16, name="rounded", tag="held" if shared else "rounded", bufs=1 if shared else 3, align_bytes=64
+            )
             dst = rounded[w, a, b][:].rearrange("p (u v m i) -> p u m i v", u=2, v=2, i=PACK)
             src = raw[w, a, b][:].rearrange("p i (m u v) -> p u m i v", u=2, v=2)
             if engine == "scalar":
@@ -140,7 +128,7 @@ def tile_list_meltab_log_kernel(
                             lhsT=w_codes[w, a, b][:, t * P : (t + 1) * P].bitcast(FP8X4),
                             lhsT_scale=w_plane[w, a, b][:, t * P : (t + 1) * P],
                             rhs=frames[jt][:, a, cols].bitcast(FP4X4),
-                            rhs_scale=tab_planes[a][:, j0 : j0 + width],
+                            rhs_scale=tab_planes[:, a, j0 : j0 + width],
                             start=(a == 0),
                             stop=(a == 1),
                         )
@@ -163,8 +151,9 @@ def tile_list_meltab_log_kernel(
                     squares[1, b, j0][:, :, c : c + piece].rearrange("p t (c i) -> p c t i", i=2),
                     ALU.add,
                 )
+            signs = sign[:, PACK * b : PACK * (b + 1)].unsqueeze(1).to_broadcast([P, piece, PACK])
             for c in starts:
-                nc.vector.tensor_tensor(h[c][:], h[c][:], signs[b][:, 0:piece, :], ALU.mult)
+                nc.vector.tensor_tensor(h[c][:], h[c][:], signs, ALU.mult)
             for c in starts:
                 cols = slice(j0 + c, j0 + c + piece)
                 nc.vector.quantize_mx(
@@ -193,6 +182,11 @@ def tile_list_meltab_log_kernel(
                 nc.sync.dma_start(rows.rearrange("(n p) j -> p n j", p=P), result[:])
 
         pick_frames(0)
+        nc.vector.tensor_scalar(minus_two[:], g8, 0.0, -2.0, ALU.is_lt, ALU.mult)
+        nc.vector.tensor_scalar(sign[:], minus_two[:], 1.0, None, ALU.add)
+        nc.vector.tensor_tensor(guess[:], mag[:], inv[:], ALU.mult)
+        nc.vector.scalar_tensor_tensor(step[:], guess[:], -0.5, inv[:], ALU.mult, ALU.mult)
+        nc.vector.scalar_tensor_tensor(root[:], step[:], 1.5, guess[:], ALU.add, ALU.mult)
         round_weight(0, 0, 0, "scalar")
         round_weight(0, 1, 0, "both")
         quantise_weight(0, 0, 0)
@@ -201,7 +195,7 @@ def tile_list_meltab_log_kernel(
         round_weight(1, 0, 0, "scalar")
         transform(0, 0, 0, JT)
         quantise_weight(1, 0, 0)
-        round_weight(1, 1, 0, "vector")
+        round_weight(1, 1, 0, "scalar")
         pick_frames(2)
         quantise_weight(1, 1, 0)
         transform(0, 0, JT, JT)

@@ -22,7 +22,9 @@ PASS = P * PACK
 JT = 512
 NJ = J // JT
 LIST_COLS = JT // 16
-SMALLEST_GAIN = 2.0 ** -100
+PIECE = 256
+RUN = 4
+HALF_J = J // 2
 
 
 def tile_list_meltab_log_kernel(
@@ -31,7 +33,7 @@ def tile_list_meltab_log_kernel(
     nc = tc.nc
     with ExitStack() as ctx:
         keep = ctx.enter_context(tc.tile_pool(name="keep", bufs=1))
-        ring = ctx.enter_context(tc.tile_pool(name="ring", bufs=2))
+        ring = ctx.enter_context(tc.tile_pool(name="ring", bufs=1))
         psum = ctx.enter_context(tc.psum_pool(name="psum", bufs=1))
 
         offsets = keep.tile([P, J // 16], U16, name="offsets")
@@ -40,125 +42,141 @@ def tile_list_meltab_log_kernel(
         scale_store = keep.tile([P, T], U8, name="scale_store", align_bytes=64)
         nc.vector.memset(scale_store[0:96, :].bitcast(I32), 0)
         nc.sync.dma_start(scale_store[96:128, :].bitcast(I32), tab_scales.rearrange("a z t -> z a t").bitcast(I32))
-        word_store = keep.tile([P, T], I32, name="word_store", align_bytes=64)
-        nc.sync.dma_start(word_store[:], tab_words[0].rearrange("p t i -> p (t i)").bitcast(I32))
-
         gain = keep.tile([P, 2, PACK], F32, name="gain")
         nc.scalar.dma_start(gain[:], gn.rearrange("(b p t) -> p b t", b=2, t=PACK))
 
         raw = {}
-        def load_weight(w, a, b):
-            raw[w, a, b] = ring.tile([P, PACK, PASS], F32, name="raw", tag="raw", bufs=3, align_bytes=64)
+        def load_weight(c, tag):
+            b, w, a = c // 4, c // 2 % 2, c % 2
+            raw[c] = ring.tile([P, PACK, PASS], F32, name="raw", tag=tag, align_bytes=64)
             rows = (co, si)[w][a * PASS : (a + 1) * PASS, b * PASS : (b + 1) * PASS]
-            nc.sync.dma_start(raw[w, a, b][:], rows.rearrange("(p i) c -> p i c", i=PACK))
+            nc.sync.dma_start(raw[c][:], rows.rearrange("(p i) c -> p i c", i=PACK))
 
-        for b in range(2):
-            for w in range(2):
-                for a in range(2):
-                    load_weight(w, a, b)
-
-        fb_codes = ring.tile([P, 2, N], I32, name="fb_codes", tag="raw", bufs=3, align_bytes=64)
-        nc.sync.dma_start(fb_codes[:], fb_words.rearrange("b p n i -> p b (n i)").bitcast(I32))
-        fb_plane = ring.tile([P, 2, N], U8, name="fb_plane", tag="raw", bufs=3, align_bytes=64)
-        for q in range(4):
-            nc.sync.dma_start(
-                fb_plane[32 * q : 32 * q + 4, :, :].bitcast(I32),
-                fb_scales[:, 4 * q : 4 * q + 4, :].rearrange("b r n -> r b n").bitcast(I32),
-            )
+        load_weight(0, "first")
+        word_store = keep.tile([P, T], I32, name="word_store", align_bytes=64)
+        nc.sync.dma_start(word_store[:], tab_words[0].rearrange("p t i -> p (t i)").bitcast(I32))
+        load_weight(1, "raw1")
 
         g8 = gain[:].rearrange("p b t -> p (b t)")
         def small(name, dtype=F32):
             return keep.tile([P, 2 * PACK], dtype, name=name)
-        mag, minus_two, sign = small("mag"), small("minus_two"), small("sign", BF16)
-        inv, guess, step, root = small("inv"), small("guess"), small("step"), small("root")
-        nc.vector.scalar_tensor_tensor(mag[:], g8, -1.0, g8, ALU.mult, ALU.max)
-        nc.scalar.activation(inv[:], mag[:], ACT.Abs_reciprocal_sqrt, bias=SMALLEST_GAIN)
+        half, minus_two, sign, mag, root = small("half"), small("minus_two"), small("sign", BF16), small("mag"), small("root")
+        nc.gpsimd.memset(half[:], 0.5)
         warm = keep.tile([P, 1], F32, name="warm")
-        nc.scalar.activation(warm[:], inv[:, 0:1], ACT.Ln, bias=1.0)
+        nc.scalar.activation(warm[:], half[:, 0:1], ACT.Ln, bias=1.0)
+        nc.gpsimd.tensor_scalar(minus_two[:], g8, 0.0, -2.0, ALU.is_lt, ALU.mult)
+        nc.gpsimd.tensor_scalar(sign[:], minus_two[:], 1.0, 1.0, ALU.mult, ALU.add)
+        nc.gpsimd.tensor_tensor(mag[:], g8, sign[:], ALU.mult)
+        nc.gpsimd.tensor_tensor(root[:], mag[:], half[:], ALU.pow)
 
         picked_scales = keep.tile([P, J], U8, name="picked_scales", align_bytes=64)
         nc.vector.tensor_copy(picked_scales[:], scale_store[:].indirect(offsets[:]))
-        tab_planes = keep.tile([P, 2, J], U8, name="tab_planes", align_bytes=64)
-        for q in range(4):
-            nc.scalar.dma_start(
-                tab_planes[32 * q : 32 * q + 4, :, :].bitcast(I32),
-                picked_scales[96 + 8 * q : 96 + 8 * q + 8, :].bitcast(I32),
-            )
+        tab_planes = {}
+        def move_planes(hj, queue, tag):
+            tab_planes[hj] = ring.tile([P, 2, HALF_J], U8, name="tab_planes", tag=tag, align_bytes=64)
+            for q in range(4):
+                queue.dma_start(
+                    tab_planes[hj][32 * q : 32 * q + 4, :, :].bitcast(I32),
+                    picked_scales[96 + 8 * q : 96 + 8 * q + 8, hj * HALF_J : (hj + 1) * HALF_J].bitcast(I32),
+                )
 
         frames = {}
-        def pick_frames(jt):
-            pairs = ring.tile([P, JT], U32, name="pairs", tag="early" if jt < 2 else "held", bufs=2 if jt < 2 else 1, align_bytes=64)
+        def pick_frames(jt, tag):
+            pairs = ring.tile([P, JT], U32, name="pairs", tag=tag, align_bytes=64)
             cols = offsets[:, jt * LIST_COLS : (jt + 1) * LIST_COLS]
             nc.vector.tensor_copy(pairs[:], word_store[:].bitcast(U32).indirect(cols))
             frames[jt] = keep.tile([P, 2, JT], U16, name=f"frames{jt}", align_bytes=64)
             nc.vector.tensor_copy(frames[jt][:], pairs[:].bitcast(U16).rearrange("p (j d) -> p d j", d=2))
 
         rounded, w_codes, w_plane = {}, {}, {}
-        def round_weight(w, a, b, engine):
-            shared = engine == "both"
-            rounded[w, a, b] = ring.tile(
-                [P, PACK * PASS], BF16, name="rounded", tag="held" if shared else "rounded", bufs=1 if shared else 3, align_bytes=64
-            )
-            dst = rounded[w, a, b][:].rearrange("p (u v m i) -> p u m i v", u=2, v=2, i=PACK)
-            src = raw[w, a, b][:].rearrange("p i (m u v) -> p u m i v", u=2, v=2)
+        def round_weight(c, u, engine, tag=None):
+            if u == 0:
+                rounded[c] = ring.tile([P, PACK * PASS], BF16, name="rounded", tag=tag, align_bytes=64)
+            dst = rounded[c][:].rearrange("p (u v m i) -> p u m i v", u=2, v=2, i=PACK)[:, u]
+            src = raw[c][:].rearrange("p i (m u v) -> p u m i v", u=2, v=2)[:, u]
             if engine == "scalar":
                 nc.scalar.copy(dst, src)
-            elif engine == "vector":
-                nc.vector.tensor_copy(dst, src)
             else:
-                nc.scalar.copy(dst[:, 0], src[:, 0])
-                nc.vector.tensor_copy(dst[:, 1], src[:, 1])
+                nc.vector.tensor_copy(dst, src)
 
-        def quantise_weight(w, a, b):
-            w_codes[w, a, b] = keep.tile([P, PASS], U32, name=f"w_codes{w}{a}{b}", align_bytes=64)
-            w_plane[w, a, b] = keep.tile([P, PASS], U8, name=f"w_plane{w}{a}{b}", align_bytes=64)
-            nc.vector.quantize_mx(w_codes[w, a, b][:].bitcast(FP8X4), w_plane[w, a, b][:], rounded[w, a, b][:])
+        def quantise_weight(c, u):
+            if c not in w_codes:
+                w_codes[c] = keep.tile([P, PASS], U32, name=f"w_codes{c}", align_bytes=64)
+                w_plane[c] = keep.tile([P, PASS], U8, name=f"w_plane{c}", align_bytes=64)
+            cols = slice(u * 2 * P, (u + 1) * 2 * P)
+            nc.vector.quantize_mx(
+                w_codes[c][:, cols].bitcast(FP8X4), w_plane[c][:, cols], rounded[c][:, u * 2 * PASS : (u + 1) * 2 * PASS]
+            )
 
-        squares = {}
-        def transform(w, b, j0, width):
-            jt, cols = j0 // JT, slice(j0 % JT, j0 % JT + width)
-            squares[w, b, j0] = ring.tile([P, PACK, width], F32, name=f"squares{w}", bufs=4 - w)
-            per_bank = JT // width
-            for t0 in range(0, PACK, per_bank):
-                acc = psum.tile([P, per_bank, width], F32, name="bank", bufs=8)
-                for t in range(t0, t0 + per_bank):
-                    for a in range(2):
-                        nc.tensor.matmul_mx(
-                            acc[:, t - t0, :],
-                            lhsT=w_codes[w, a, b][:, t * P : (t + 1) * P].bitcast(FP8X4),
-                            lhsT_scale=w_plane[w, a, b][:, t * P : (t + 1) * P],
-                            rhs=frames[jt][:, a, cols].bitcast(FP4X4),
-                            rhs_scale=tab_planes[:, a, j0 : j0 + width],
-                            start=(a == 0),
-                            stop=(a == 1),
-                        )
-                for t in range(t0, t0 + per_bank):
-                    nc.scalar.activation(
-                        squares[w, b, j0][:, t, :], acc[:, t - t0, :], ACT.Square,
-                        scale=root[:, PACK * b + t : PACK * b + t + 1],
-                    )
+        def prepare_weight(c, tag):
+            for u in range(2):
+                round_weight(c, u, "vector", tag)
+            for u in range(2):
+                quantise_weight(c, u)
+
+        squares, banks = {}, {}
+        def product(w, b, jt, t, a):
+            if a == 0:
+                banks[w, b, jt, t] = psum.tile([P, JT], F32, name="bank", bufs=8)
+            c = 4 * b + 2 * w + a
+            j0 = jt * JT % HALF_J
+            nc.tensor.matmul_mx(
+                banks[w, b, jt, t][:],
+                lhsT=w_codes[c][:, t * P : (t + 1) * P].bitcast(FP8X4),
+                lhsT_scale=w_plane[c][:, t * P : (t + 1) * P],
+                rhs=frames[jt][:, a, :].bitcast(FP4X4),
+                rhs_scale=tab_planes[jt * JT // HALF_J][:, a, j0 : j0 + JT],
+                start=(a == 0),
+                stop=(a == 1),
+            )
+
+        def square(w, b, jt, t, c0=0, n=JT):
+            if t == 0:
+                tile = ring.tile([P, PACK, n], F32, name=f"squares{w}", bufs=5)
+                for c in range(0, n, P):
+                    squares[w, b, jt * JT + c0 + c] = tile, c
+            nc.scalar.activation(
+                squares[w, b, jt * JT + c0][0][:, t, :], banks[w, b, jt, t][:, c0 : c0 + n], ACT.Square,
+                scale=root[:, PACK * b + t : PACK * b + t + 1],
+            )
+
+        def transform(w, b, jt):
+            for t in range(PACK):
+                product(w, b, jt, t, 0)
+                product(w, b, jt, t, 1)
+                square(w, b, jt, t)
 
         h_codes = [keep.tile([P, J], U32, name=f"h_codes{b}", align_bytes=64) for b in range(2)]
         h_plane = [keep.tile([P, J], U8, name=f"h_plane{b}", align_bytes=64) for b in range(2)]
-        def power(b, j0, width):
-            piece = min(width, 256)
-            starts = range(0, width, piece)
-            h = {c: ring.tile([P, piece, PACK], BF16, name="h", bufs=6, align_bytes=64) for c in starts}
-            for c in starts:
-                nc.vector.tensor_tensor(
-                    h[c][:].rearrange("p (c i) t -> p c t i", i=2),
-                    squares[0, b, j0][:, :, c : c + piece].rearrange("p t (c i) -> p c t i", i=2),
-                    squares[1, b, j0][:, :, c : c + piece].rearrange("p t (c i) -> p c t i", i=2),
-                    ALU.add,
-                )
-            signs = sign[:, PACK * b : PACK * (b + 1)].unsqueeze(1).to_broadcast([P, piece, PACK])
-            for c in starts:
-                nc.vector.tensor_tensor(h[c][:], h[c][:], signs, ALU.mult)
-            for c in starts:
-                cols = slice(j0 + c, j0 + c + piece)
-                nc.vector.quantize_mx(
-                    h_codes[b][:, cols].bitcast(FP8X4), h_plane[b][:, cols], h[c][:].rearrange("p j t -> p (j t)")
-                )
+        h, todo = {}, []
+        def add_squares(b, j0, n):
+            (re2, c), (im2, c) = squares[0, b, j0], squares[1, b, j0]
+            h[b, j0] = ring.tile([P, n, PACK], BF16, name="h", bufs=3, align_bytes=64)
+            nc.vector.tensor_tensor(
+                h[b, j0][:].rearrange("p (c i) t -> p c t i", i=RUN),
+                re2[:, :, c : c + n].rearrange("p t (c i) -> p c t i", i=RUN),
+                im2[:, :, c : c + n].rearrange("p t (c i) -> p c t i", i=RUN),
+                ALU.add,
+            )
+
+        def apply_sign(b, j0, n):
+            signs = sign[:, PACK * b : PACK * (b + 1)].unsqueeze(1).to_broadcast([P, n, PACK])
+            nc.vector.tensor_tensor(h[b, j0][:], h[b, j0][:], signs, ALU.mult)
+
+        def quantise_power(b, j0, n):
+            cols = slice(j0, j0 + n)
+            nc.vector.quantize_mx(
+                h_codes[b][:, cols].bitcast(FP8X4), h_plane[b][:, cols], h[b, j0][:].rearrange("p j t -> p (j t)")
+            )
+
+        def power(piece):
+            if todo:
+                apply_sign(*todo[-1])
+            if piece:
+                add_squares(*piece)
+            if todo:
+                quantise_power(*todo[-1])
+            todo.append(piece)
 
         def filters(j0, width):
             cols = slice(j0, j0 + width)
@@ -181,43 +199,79 @@ def tile_list_meltab_log_kernel(
                 rows = out[n0 * P : (n0 + per_bank) * P, cols]
                 nc.sync.dma_start(rows.rearrange("(n p) j -> p n j", p=P), result[:])
 
-        pick_frames(0)
-        nc.vector.tensor_scalar(minus_two[:], g8, 0.0, -2.0, ALU.is_lt, ALU.mult)
-        nc.vector.tensor_scalar(sign[:], minus_two[:], 1.0, None, ALU.add)
-        nc.vector.tensor_tensor(guess[:], mag[:], inv[:], ALU.mult)
-        nc.vector.scalar_tensor_tensor(step[:], guess[:], -0.5, inv[:], ALU.mult, ALU.mult)
-        nc.vector.scalar_tensor_tensor(root[:], step[:], 1.5, guess[:], ALU.add, ALU.mult)
-        round_weight(0, 0, 0, "scalar")
-        round_weight(0, 1, 0, "both")
-        quantise_weight(0, 0, 0)
-        quantise_weight(0, 1, 0)
-        pick_frames(1)
-        round_weight(1, 0, 0, "scalar")
-        transform(0, 0, 0, JT)
-        quantise_weight(1, 0, 0)
-        round_weight(1, 1, 0, "scalar")
-        pick_frames(2)
-        quantise_weight(1, 1, 0)
-        transform(0, 0, JT, JT)
-        pick_frames(3)
-        transform(1, 0, 0, JT)
-        transform(1, 0, JT, JT)
+        round_weight(0, 0, "scalar", "raw2")
+        round_weight(0, 1, "scalar")
+        move_planes(0, nc.scalar, "first")
+        quantise_weight(0, 0)
+        quantise_weight(0, 1)
+        load_weight(2, "raw2")
+        pick_frames(0, "raw0")
+        load_weight(3, "raw0")
+        pick_frames(1, "rounded3")
+        round_weight(1, 0, "vector", "rounded1")
+        round_weight(1, 1, "scalar")
+        load_weight(4, "raw1")
+        quantise_weight(1, 0)
+        quantise_weight(1, 1)
+        for jt in range(2):
+            for t in range(PACK):
+                product(0, 0, jt, t, 0)
+        for jt in range(2):
+            for t in range(PACK):
+                product(0, 0, jt, t, 1)
+                square(0, 0, jt, t)
+        pick_frames(2, "rounded1")
+        prepare_weight(2, "rounded2")
+        load_weight(5, "raw2")
+        move_planes(1, nc.sync, "rounded2")
+        prepare_weight(3, "rounded3")
+        load_weight(6, "raw0")
+        pick_frames(3, "rounded3")
+        transform(1, 0, 0)
+        round_weight(4, 0, "scalar", "rounded1")
+        transform(1, 0, 1)
+        round_weight(4, 1, "scalar")
+        load_weight(7, "raw1")
+        quantise_weight(4, 0)
+        quantise_weight(4, 1)
+        power((0, 0, JT))
+        transform(0, 0, 2)
+        round_weight(5, 0, "scalar", "rounded0")
+        transform(1, 0, 2)
+        round_weight(5, 1, "scalar")
+        quantise_weight(5, 0)
+        quantise_weight(5, 1)
+        prepare_weight(6, "rounded3")
+        prepare_weight(7, "rounded1")
+        fb_codes = ring.tile([P, 2, N], I32, name="fb_codes", tag="raw0", align_bytes=64)
+        nc.sync.dma_start(fb_codes[:], fb_words.rearrange("b p n i -> p b (n i)").bitcast(I32))
+        fb_plane = ring.tile([P, 2, N], U8, name="fb_plane", tag="raw2", align_bytes=64)
+        for q in range(4):
+            nc.sync.dma_start(
+                fb_plane[32 * q : 32 * q + 4, :, :].bitcast(I32),
+                fb_scales[:, 4 * q : 4 * q + 4, :].rearrange("b r n -> r b n").bitcast(I32),
+            )
+        power((0, JT, JT))
+        power((0, 2 * JT, JT))
+        transform(0, 0, 3)
+        transform(1, 0, 3)
+        power((0, 3 * JT, JT))
+        for jt in range(NJ - 1):
+            transform(0, 1, jt)
+            transform(1, 1, jt)
+            for j0 in range(jt * JT, (jt + 1) * JT, JT if jt < NJ - 2 else JT // 2):
+                power((1, j0, JT if jt < NJ - 2 else JT // 2))
         for w in range(2):
-            for a in range(2):
-                round_weight(w, a, 1, "vector")
-                quantise_weight(w, a, 1)
-        power(0, 0, JT)
-        power(0, JT, JT)
-        for j0 in range(2 * JT, J, JT):
-            transform(0, 0, j0, JT)
-            transform(1, 0, j0, JT)
-            power(0, j0, JT)
-        spans = [(j0, JT) for j0 in range(0, J - JT, JT)] + [(j0, P) for j0 in range(J - JT, J, P)]
-        for i, (j0, width) in enumerate(spans):
-            transform(0, 1, j0, width)
-            transform(1, 1, j0, width)
-            power(1, j0, width)
-            if i > 1:
-                filters(*spans[i - 2])
-        filters(*spans[-2])
-        filters(*spans[-1])
+            for t in range(PACK):
+                product(w, 1, NJ - 1, t, 0)
+                product(w, 1, NJ - 1, t, 1)
+                square(w, 1, NJ - 1, t, 0, JT // 2)
+        for w in range(2):
+            for t in range(PACK):
+                square(w, 1, NJ - 1, t, JT // 2, JT // 2)
+        last = [(J - JT, 2 * P), (J - 2 * P, P), (J - P, P)]
+        for j0, n in last:
+            power((1, j0, n))
+        power(None)
+        for j0, n in [(0, JT), (JT, JT), (2 * JT, JT // 2), (2 * JT + JT // 2, JT // 2)] + last:
+            filters(j0, n)

@@ -131,7 +131,7 @@ def tile_list_meltab_log_kernel(
             )
 
         def square(w, b, jt, t, c0=0, n=JT):
-            if t == 0:
+            if (w, b, jt * JT + c0) not in squares:
                 tile = ring.tile([P, PACK, n], F32, name=f"squares{w}", bufs=5)
                 for c in range(0, n, P):
                     squares[w, b, jt * JT + c0 + c] = tile, c
@@ -144,6 +144,7 @@ def tile_list_meltab_log_kernel(
             for t in range(PACK):
                 product(w, b, jt, t, 0)
                 product(w, b, jt, t, 1)
+            for t in reversed(range(PACK)):
                 square(w, b, jt, t)
 
         h_codes = [keep.tile([P, J], U32, name=f"h_codes{b}", align_bytes=64) for b in range(2)]
@@ -219,6 +220,7 @@ def tile_list_meltab_log_kernel(
         for jt in range(2):
             for t in range(PACK):
                 product(0, 0, jt, t, 1)
+            for t in reversed(range(PACK)):
                 square(0, 0, jt, t)
         pick_frames(2, "rounded1")
         prepare_weight(2, "rounded2")
@@ -265,6 +267,7 @@ def tile_list_meltab_log_kernel(
             for t in range(PACK):
                 product(w, 1, NJ - 1, t, 0)
                 product(w, 1, NJ - 1, t, 1)
+            for t in reversed(range(PACK)):
                 square(w, 1, NJ - 1, t, 0, JT // 2)
         for w in range(2):
             for t in range(PACK):

@@ -230,19 +230,13 @@ def tile_list_meltab_log_kernel(
         load_weight(6, "raw0")
         pick_frames(3, "rounded3")
         transform(1, 0, 0)
-        round_weight(4, 0, "scalar", "rounded1")
         transform(1, 0, 1)
-        round_weight(4, 1, "scalar")
+        prepare_weight(4, "rounded1")
         load_weight(7, "raw1")
-        quantise_weight(4, 0)
-        quantise_weight(4, 1)
         power((0, 0, JT))
         transform(0, 0, 2)
-        round_weight(5, 0, "scalar", "rounded0")
         transform(1, 0, 2)
-        round_weight(5, 1, "scalar")
-        quantise_weight(5, 0)
-        quantise_weight(5, 1)
+        prepare_weight(5, "rounded0")
         prepare_weight(6, "rounded3")
         prepare_weight(7, "rounded1")
         fb_codes = ring.tile([P, 2, N], I32, name="fb_codes", tag="raw0", align_bytes=64)

@@ -52,21 +52,20 @@ def tile_list_meltab_log_kernel(
             rows = (co, si)[w][a * PASS : (a + 1) * PASS, b * PASS : (b + 1) * PASS]
             nc.sync.dma_start(raw[c][:], rows.rearrange("(p i) c -> p i c", i=PACK))
 
-        load_weight(0, "first")
         word_store = keep.tile([P, T], I32, name="word_store", align_bytes=64)
         nc.sync.dma_start(word_store[:], tab_words[0].rearrange("p t i -> p (t i)").bitcast(I32))
+        load_weight(0, "raw0")
         load_weight(1, "raw1")
 
         g8 = gain[:].rearrange("p b t -> p (b t)")
         def small(name, dtype=F32):
             return keep.tile([P, 2 * PACK], dtype, name=name)
-        half, minus_two, sign, mag, root = small("half"), small("minus_two"), small("sign", BF16), small("mag"), small("root")
+        half, sign, mag, root = small("half"), small("sign", BF16), small("mag"), small("root")
         nc.gpsimd.memset(half[:], 0.5)
         warm = keep.tile([P, 1], F32, name="warm")
         nc.scalar.activation(warm[:], half[:, 0:1], ACT.Ln, bias=1.0)
-        nc.gpsimd.tensor_scalar(minus_two[:], g8, 0.0, -2.0, ALU.is_lt, ALU.mult)
-        nc.gpsimd.tensor_scalar(sign[:], minus_two[:], 1.0, 1.0, ALU.mult, ALU.add)
-        nc.gpsimd.tensor_tensor(mag[:], g8, sign[:], ALU.mult)
+        nc.scalar.activation(mag[:], g8, ACT.Abs)
+        nc.scalar.activation(sign[:], g8, ACT.Sign)
         nc.gpsimd.tensor_tensor(root[:], mag[:], half[:], ALU.pow)
 
         picked_scales = keep.tile([P, J], U8, name="picked_scales", align_bytes=64)
@@ -80,17 +79,23 @@ def tile_list_meltab_log_kernel(
                     picked_scales[96 + 8 * q : 96 + 8 * q + 8, hj * HALF_J : (hj + 1) * HALF_J].bitcast(I32),
                 )
 
-        frames = {}
-        def pick_frames(jt, tag):
-            pairs = ring.tile([P, JT], U32, name="pairs", tag=tag, align_bytes=64)
+        pairs, frames = {}, {}
+        def pick_pairs(jt, tag):
+            pairs[jt] = ring.tile([P, JT], U32, name="pairs", tag=tag, align_bytes=64)
             cols = offsets[:, jt * LIST_COLS : (jt + 1) * LIST_COLS]
-            nc.vector.tensor_copy(pairs[:], word_store[:].bitcast(U32).indirect(cols))
-            frames[jt] = keep.tile([P, 2, JT], U16, name=f"frames{jt}", align_bytes=64)
-            nc.vector.tensor_copy(frames[jt][:], pairs[:].bitcast(U16).rearrange("p (j d) -> p d j", d=2))
+            nc.vector.tensor_copy(pairs[jt][:], word_store[:].bitcast(U32).indirect(cols))
+
+        def part_pairs(jt, tag):
+            frames[jt] = ring.tile([P, 2, JT], U16, name="frames", tag=tag, align_bytes=64)
+            nc.vector.tensor_copy(frames[jt][:], pairs[jt][:].bitcast(U16).rearrange("p (j d) -> p d j", d=2))
+
+        def pick_frames(jt, tag):
+            pick_pairs(jt, tag)
+            part_pairs(jt, f"frames{jt}")
 
         rounded, w_codes, w_plane = {}, {}, {}
         def round_weight(c, u, engine, tag=None):
-            if u == 0:
+            if c not in rounded:
                 rounded[c] = ring.tile([P, PACK * PASS], BF16, name="rounded", tag=tag, align_bytes=64)
             dst = rounded[c][:].rearrange("p (u v m i) -> p u m i v", u=2, v=2, i=PACK)[:, u]
             src = raw[c][:].rearrange("p i (m u v) -> p u m i v", u=2, v=2)[:, u]
@@ -103,16 +108,12 @@ def tile_list_meltab_log_kernel(
             if c not in w_codes:
                 w_codes[c] = keep.tile([P, PASS], U32, name=f"w_codes{c}", align_bytes=64)
                 w_plane[c] = keep.tile([P, PASS], U8, name=f"w_plane{c}", align_bytes=64)
-            cols = slice(u * 2 * P, (u + 1) * 2 * P)
+            cols = slice(u.start * 2 * P, u.stop * 2 * P)
             nc.vector.quantize_mx(
-                w_codes[c][:, cols].bitcast(FP8X4), w_plane[c][:, cols], rounded[c][:, u * 2 * PASS : (u + 1) * 2 * PASS]
+                w_codes[c][:, cols].bitcast(FP8X4), w_plane[c][:, cols], rounded[c][:, PACK * cols.start : PACK * cols.stop]
             )
 
-        def prepare_weight(c, tag):
-            for u in range(2):
-                round_weight(c, u, "vector", tag)
-            for u in range(2):
-                quantise_weight(c, u)
+        LO, HI, ALL = slice(0, 1), slice(1, 2), slice(0, 2)
 
         squares, banks = {}, {}
         def product(w, b, jt, t, a):
@@ -144,17 +145,15 @@ def tile_list_meltab_log_kernel(
             for t in range(PACK):
                 product(w, b, jt, t, 0)
                 product(w, b, jt, t, 1)
-            for t in reversed(range(PACK)):
                 square(w, b, jt, t)
 
         h_codes = [keep.tile([P, J], U32, name=f"h_codes{b}", align_bytes=64) for b in range(2)]
         h_plane = [keep.tile([P, J], U8, name=f"h_plane{b}", align_bytes=64) for b in range(2)]
         h, todo = {}, []
-        def add_squares(b, j0, n):
+        def add_squares(dst, b, j0, n):
             (re2, c), (im2, c) = squares[0, b, j0], squares[1, b, j0]
-            h[b, j0] = ring.tile([P, n, PACK], BF16, name="h", bufs=3, align_bytes=64)
             nc.vector.tensor_tensor(
-                h[b, j0][:].rearrange("p (c i) t -> p c t i", i=RUN),
+                dst.rearrange("p (c i) t -> p c t i", i=RUN),
                 re2[:, :, c : c + n].rearrange("p t (c i) -> p c t i", i=RUN),
                 im2[:, :, c : c + n].rearrange("p t (c i) -> p c t i", i=RUN),
                 ALU.add,
@@ -170,14 +169,19 @@ def tile_list_meltab_log_kernel(
                 h_codes[b][:, cols].bitcast(FP8X4), h_plane[b][:, cols], h[b, j0][:].rearrange("p j t -> p (j t)")
             )
 
-        def power(piece):
-            if todo:
+        def power(b, j0, n, part):
+            if part == 1:
+                j0, n = j0 - n, 2 * n
+            else:
+                h[b, j0] = ring.tile([P, n if part is None else 2 * n, PACK], BF16, name="h", bufs=2, align_bytes=64)
+            if part != 0 and todo:
                 apply_sign(*todo[-1])
-            if piece:
-                add_squares(*piece)
-            if todo:
-                quantise_power(*todo[-1])
-            todo.append(piece)
+            lo = n // 2 if part == 1 else 0
+            add_squares(h[b, j0][:, lo:n, :], b, j0 + lo, n - lo)
+            if part != 0:
+                if todo:
+                    quantise_power(*todo[-1])
+                todo.append((b, j0, n))
 
         def filters(j0, width):
             cols = slice(j0, j0 + width)
@@ -200,45 +204,52 @@ def tile_list_meltab_log_kernel(
                 rows = out[n0 * P : (n0 + per_bank) * P, cols]
                 nc.sync.dma_start(rows.rearrange("(n p) j -> p n j", p=P), result[:])
 
-        round_weight(0, 0, "scalar", "raw2")
-        round_weight(0, 1, "scalar")
-        move_planes(0, nc.scalar, "first")
-        quantise_weight(0, 0)
-        quantise_weight(0, 1)
+        move_planes(0, nc.scalar, "planes0")
+        pick_frames(0, "raw2")
         load_weight(2, "raw2")
-        pick_frames(0, "raw0")
-        load_weight(3, "raw0")
         pick_frames(1, "rounded3")
+        pick_pairs(2, "pairs")
+        round_weight(0, ALL, "scalar", "rounded0")
+        load_weight(3, "raw0")
+        quantise_weight(0, ALL)
         round_weight(1, 0, "vector", "rounded1")
         round_weight(1, 1, "scalar")
         load_weight(4, "raw1")
-        quantise_weight(1, 0)
-        quantise_weight(1, 1)
-        for jt in range(2):
-            for t in range(PACK):
-                product(0, 0, jt, t, 0)
-        for jt in range(2):
-            for t in range(PACK):
-                product(0, 0, jt, t, 1)
-            for t in reversed(range(PACK)):
-                square(0, 0, jt, t)
-        pick_frames(2, "rounded1")
-        prepare_weight(2, "rounded2")
+        quantise_weight(1, LO)
+        quantise_weight(1, HI)
+        transform(0, 0, 0)
+        transform(0, 0, 1)
+        round_weight(2, ALL, "vector", "rounded2")
         load_weight(5, "raw2")
-        move_planes(1, nc.sync, "rounded2")
-        prepare_weight(3, "rounded3")
+        quantise_weight(2, ALL)
+        part_pairs(2, "rounded2")
+        move_planes(1, nc.sync, "rounded1")
+        round_weight(3, 0, "vector", "rounded3")
+        round_weight(3, 1, "vector")
         load_weight(6, "raw0")
+        quantise_weight(3, LO)
+        quantise_weight(3, HI)
         pick_frames(3, "rounded3")
         transform(1, 0, 0)
         transform(1, 0, 1)
-        prepare_weight(4, "rounded1")
+        round_weight(4, ALL, "vector", "rounded0")
         load_weight(7, "raw1")
-        power((0, 0, JT))
+        quantise_weight(4, ALL)
+        power(0, 0, JT, 0)
+        round_weight(5, ALL, "vector", "rounded4")
+        quantise_weight(5, ALL)
+        round_weight(6, 0, "scalar", "rounded3")
         transform(0, 0, 2)
+        round_weight(6, 1, "scalar")
+        power(0, JT, JT, 1)
         transform(1, 0, 2)
-        prepare_weight(5, "rounded0")
-        prepare_weight(6, "rounded3")
-        prepare_weight(7, "rounded1")
+        round_weight(7, 0, "scalar", "rounded0")
+        quantise_weight(6, ALL)
+        round_weight(7, 1, "vector")
+        quantise_weight(7, ALL)
+        transform(0, 0, 3)
+        transform(1, 0, 3)
+        power(0, 2 * JT, JT, 0)
         fb_codes = ring.tile([P, 2, N], I32, name="fb_codes", tag="raw0", align_bytes=64)
         nc.sync.dma_start(fb_codes[:], fb_words.rearrange("b p n i -> p b (n i)").bitcast(I32))
         fb_plane = ring.tile([P, 2, N], U8, name="fb_plane", tag="raw2", align_bytes=64)
@@ -247,28 +258,27 @@ def tile_list_meltab_log_kernel(
                 fb_plane[32 * q : 32 * q + 4, :, :].bitcast(I32),
                 fb_scales[:, 4 * q : 4 * q + 4, :].rearrange("b r n -> r b n").bitcast(I32),
             )
-        power((0, JT, JT))
-        power((0, 2 * JT, JT))
-        transform(0, 0, 3)
-        transform(1, 0, 3)
-        power((0, 3 * JT, JT))
+        power(0, 3 * JT, JT, 1)
         for jt in range(NJ - 1):
             transform(0, 1, jt)
             transform(1, 1, jt)
-            for j0 in range(jt * JT, (jt + 1) * JT, JT if jt < NJ - 2 else JT // 2):
-                power((1, j0, JT if jt < NJ - 2 else JT // 2))
+            if jt < NJ - 2:
+                power(1, jt * JT, JT, jt)
+            else:
+                power(1, jt * JT, JT // 2, None)
+                power(1, jt * JT + JT // 2, JT // 2, None)
         for w in range(2):
             for t in range(PACK):
                 product(w, 1, NJ - 1, t, 0)
                 product(w, 1, NJ - 1, t, 1)
-            for t in reversed(range(PACK)):
                 square(w, 1, NJ - 1, t, 0, JT // 2)
         for w in range(2):
             for t in range(PACK):
                 square(w, 1, NJ - 1, t, JT // 2, JT // 2)
         last = [(J - JT, 2 * P), (J - 2 * P, P), (J - P, P)]
         for j0, n in last:
-            power((1, j0, n))
-        power(None)
+            power(1, j0, n, None)
+        apply_sign(*todo[-1])
+        quantise_power(*todo[-1])
         for j0, n in [(0, JT), (JT, JT), (2 * JT, JT // 2), (2 * JT + JT // 2, JT // 2)] + last:
             filters(j0, n)

@@ -25,6 +25,7 @@ LIST_COLS = JT // 16
 PIECE = 256
 RUN = 4
 HALF_J = J // 2
+SMALLEST_GAIN = 2.0 ** -100
 
 
 def tile_list_meltab_log_kernel(
@@ -60,13 +61,13 @@ def tile_list_meltab_log_kernel(
         g8 = gain[:].rearrange("p b t -> p (b t)")
         def small(name, dtype=F32):
             return keep.tile([P, 2 * PACK], dtype, name=name)
-        half, sign, mag, root = small("half"), small("sign", BF16), small("mag"), small("root")
-        nc.gpsimd.memset(half[:], 0.5)
+        sign, mag, inv = small("sign", BF16), small("mag"), small("inv")
+        guess, step, root = small("guess"), small("step"), small("root")
+        nc.vector.scalar_tensor_tensor(mag[:], g8, -1.0, g8, ALU.mult, ALU.max)
+        nc.scalar.activation(inv[:], mag[:], ACT.Abs_reciprocal_sqrt, bias=SMALLEST_GAIN, scale=2.0)
+        nc.vector.tensor_scalar(sign[:], g8, 0.0, 0.5, ALU.is_ge, ALU.subtract)
         warm = keep.tile([P, 1], F32, name="warm")
-        nc.scalar.activation(warm[:], half[:, 0:1], ACT.Ln, bias=1.0)
-        nc.scalar.activation(mag[:], g8, ACT.Abs)
-        nc.scalar.activation(sign[:], g8, ACT.Sign)
-        nc.gpsimd.tensor_tensor(root[:], mag[:], half[:], ALU.pow)
+        nc.scalar.activation(warm[:], inv[:, 0:1], ACT.Ln, bias=1.0)
 
         picked_scales = keep.tile([P, J], U8, name="picked_scales", align_bytes=64)
         nc.vector.tensor_copy(picked_scales[:], scale_store[:].indirect(offsets[:]))
@@ -205,7 +206,11 @@ def tile_list_meltab_log_kernel(
                 nc.sync.dma_start(rows.rearrange("(n p) j -> p n j", p=P), result[:])
 
         move_planes(0, nc.scalar, "planes0")
-        pick_frames(0, "raw2")
+        nc.vector.scalar_tensor_tensor(guess[:], mag[:], 2.0, inv[:], ALU.mult, ALU.mult)
+        pick_pairs(0, "raw2")
+        nc.vector.scalar_tensor_tensor(step[:], guess[:], -0.5, inv[:], ALU.mult, ALU.mult)
+        part_pairs(0, "frames0")
+        nc.vector.scalar_tensor_tensor(root[:], step[:], 1.5, guess[:], ALU.add, ALU.mult)
         load_weight(2, "raw2")
         pick_frames(1, "rounded3")
         pick_pairs(2, "pairs")
@@ -243,9 +248,8 @@ def tile_list_meltab_log_kernel(
         round_weight(6, 1, "scalar")
         power(0, JT, JT, 1)
         transform(1, 0, 2)
-        round_weight(7, 0, "scalar", "rounded0")
+        round_weight(7, ALL, "vector", "rounded0")
         quantise_weight(6, ALL)
-        round_weight(7, 1, "vector")
         quantise_weight(7, ALL)
         transform(0, 0, 3)
         transform(1, 0, 3)

@@ -116,14 +116,22 @@ def tile_list_meltab_log_kernel(
 
         LO, HI, ALL = slice(0, 1), slice(1, 2), slice(0, 2)
 
-        squares, banks = {}, {}
+        squares, banks, taken = {}, {}, []
+        def next_bank():
+            if len(taken) % 2 == 0:
+                pair = psum.tile([P, 2, JT], F32, name="pair", bufs=4)
+            else:
+                pair = taken[-1]
+            taken.append(pair)
+            return pair[:, (len(taken) - 1) % 2, :]
+
         def product(w, b, jt, t, a):
             if a == 0:
-                banks[w, b, jt, t] = psum.tile([P, JT], F32, name="bank", bufs=8)
+                banks[w, b, jt, t] = next_bank()
             c = 4 * b + 2 * w + a
             j0 = jt * JT % HALF_J
             nc.tensor.matmul_mx(
-                banks[w, b, jt, t][:],
+                banks[w, b, jt, t],
                 lhsT=w_codes[c][:, t * P : (t + 1) * P].bitcast(FP8X4),
                 lhsT_scale=w_plane[c][:, t * P : (t + 1) * P],
                 rhs=frames[jt][:, a, :].bitcast(FP4X4),
@@ -143,10 +151,12 @@ def tile_list_meltab_log_kernel(
             )
 
         def transform(w, b, jt):
-            for t in range(PACK):
-                product(w, b, jt, t, 0)
-                product(w, b, jt, t, 1)
-                square(w, b, jt, t)
+            for t0 in range(0, PACK, 2):
+                for t in (t0, t0 + 1):
+                    product(w, b, jt, t, 0)
+                    product(w, b, jt, t, 1)
+                for t in (t0, t0 + 1):
+                    square(w, b, jt, t)
 
         h_codes = [keep.tile([P, J], U32, name=f"h_codes{b}", align_bytes=64) for b in range(2)]
         h_plane = [keep.tile([P, J], U8, name=f"h_plane{b}", align_bytes=64) for b in range(2)]
@@ -186,22 +196,23 @@ def tile_list_meltab_log_kernel(
 
         def filters(j0, width):
             cols = slice(j0, j0 + width)
+            pair = psum.tile([P, 2, JT], F32, name="pair", bufs=4)
+            y = pair[:].rearrange("p k j -> p (k j)")[:, 0 : 2 * width].rearrange("p (n j) -> p n j", n=2)
+            for nt in range(N // P):
+                for b in range(2):
+                    nc.tensor.matmul_mx(
+                        y[:, nt, :],
+                        lhsT=fb_codes[:, b, nt * P : (nt + 1) * P].bitcast(FP8X4),
+                        lhsT_scale=fb_plane[:, b, nt * P : (nt + 1) * P],
+                        rhs=h_codes[b][:, cols].bitcast(FP8X4),
+                        rhs_scale=h_plane[b][:, cols],
+                        start=(b == 0),
+                        stop=(b == 1),
+                    )
             per_bank = min(N // P, JT // width)
             for n0 in range(0, N // P, per_bank):
-                y = psum.tile([P, per_bank, width], F32, name="bank", bufs=8)
-                for nt in range(n0, n0 + per_bank):
-                    for b in range(2):
-                        nc.tensor.matmul_mx(
-                            y[:, nt - n0, :],
-                            lhsT=fb_codes[:, b, nt * P : (nt + 1) * P].bitcast(FP8X4),
-                            lhsT_scale=fb_plane[:, b, nt * P : (nt + 1) * P],
-                            rhs=h_codes[b][:, cols].bitcast(FP8X4),
-                            rhs_scale=h_plane[b][:, cols],
-                            start=(b == 0),
-                            stop=(b == 1),
-                        )
                 result = ring.tile([P, per_bank, width], F32, name="result", bufs=4)
-                nc.scalar.activation(result[:], y[:], ACT.Ln, bias=1.0)
+                nc.scalar.activation(result[:], y[:, n0 : n0 + per_bank, :], ACT.Ln, bias=1.0)
                 rows = out[n0 * P : (n0 + per_bank) * P, cols]
                 nc.sync.dma_start(rows.rearrange("(n p) j -> p n j", p=P), result[:])
 
@@ -275,6 +286,7 @@ def tile_list_meltab_log_kernel(
             for t in range(PACK):
                 product(w, 1, NJ - 1, t, 0)
                 product(w, 1, NJ - 1, t, 1)
+            for t in range(PACK):
                 square(w, 1, NJ - 1, t, 0, JT // 2)
         for w in range(2):
             for t in range(PACK):

@@ -23,8 +23,8 @@ JT = 512
 NJ = J // JT
 LIST_COLS = JT // 16
 PIECE = 256
-RUN = 4
-HALF_J = J // 2
+RUN = 2
+SIGN_ROW = 64
 SMALLEST_GAIN = 2.0 ** -100
 
 
@@ -53,9 +53,9 @@ def tile_list_meltab_log_kernel(
             rows = (co, si)[w][a * PASS : (a + 1) * PASS, b * PASS : (b + 1) * PASS]
             nc.sync.dma_start(raw[c][:], rows.rearrange("(p i) c -> p i c", i=PACK))
 
+        load_weight(0, "first")
         word_store = keep.tile([P, T], I32, name="word_store", align_bytes=64)
         nc.sync.dma_start(word_store[:], tab_words[0].rearrange("p t i -> p (t i)").bitcast(I32))
-        load_weight(0, "raw0")
         load_weight(1, "raw1")
 
         g8 = gain[:].rearrange("p b t -> p (b t)")
@@ -66,19 +66,23 @@ def tile_list_meltab_log_kernel(
         nc.vector.scalar_tensor_tensor(mag[:], g8, -1.0, g8, ALU.mult, ALU.max)
         nc.scalar.activation(inv[:], mag[:], ACT.Abs_reciprocal_sqrt, bias=SMALLEST_GAIN, scale=2.0)
         nc.vector.tensor_scalar(sign[:], g8, 0.0, 0.5, ALU.is_ge, ALU.subtract)
+        sign_rows = keep.tile([P, 2, SIGN_ROW, PACK], BF16, name="sign_rows")
+        nc.scalar.copy(
+            sign_rows[:], sign[:].rearrange("p (b t) -> p b t", b=2).unsqueeze(2).to_broadcast([P, 2, SIGN_ROW, PACK])
+        )
         warm = keep.tile([P, 1], F32, name="warm")
         nc.scalar.activation(warm[:], inv[:, 0:1], ACT.Ln, bias=1.0)
 
         picked_scales = keep.tile([P, J], U8, name="picked_scales", align_bytes=64)
         nc.vector.tensor_copy(picked_scales[:], scale_store[:].indirect(offsets[:]))
-        tab_planes = {}
-        def move_planes(hj, queue, tag):
-            tab_planes[hj] = ring.tile([P, 2, HALF_J], U8, name="tab_planes", tag=tag, align_bytes=64)
+        def move_planes(tag):
+            planes = ring.tile([P, 2, J], U8, name="tab_planes", tag=tag, align_bytes=64)
             for q in range(4):
-                queue.dma_start(
-                    tab_planes[hj][32 * q : 32 * q + 4, :, :].bitcast(I32),
-                    picked_scales[96 + 8 * q : 96 + 8 * q + 8, hj * HALF_J : (hj + 1) * HALF_J].bitcast(I32),
+                nc.scalar.dma_start(
+                    planes[32 * q : 32 * q + 4, :, :].bitcast(I32),
+                    picked_scales[96 + 8 * q : 96 + 8 * q + 8, :].bitcast(I32),
                 )
+            return planes
 
         pairs, frames = {}, {}
         def pick_pairs(jt, tag):
@@ -114,8 +118,6 @@ def tile_list_meltab_log_kernel(
                 w_codes[c][:, cols].bitcast(FP8X4), w_plane[c][:, cols], rounded[c][:, PACK * cols.start : PACK * cols.stop]
             )
 
-        LO, HI, ALL = slice(0, 1), slice(1, 2), slice(0, 2)
-
         squares, banks, taken = {}, {}, []
         def next_bank():
             if len(taken) % 2 == 0:
@@ -129,13 +131,12 @@ def tile_list_meltab_log_kernel(
             if a == 0:
                 banks[w, b, jt, t] = next_bank()
             c = 4 * b + 2 * w + a
-            j0 = jt * JT % HALF_J
             nc.tensor.matmul_mx(
                 banks[w, b, jt, t],
                 lhsT=w_codes[c][:, t * P : (t + 1) * P].bitcast(FP8X4),
                 lhsT_scale=w_plane[c][:, t * P : (t + 1) * P],
                 rhs=frames[jt][:, a, :].bitcast(FP4X4),
-                rhs_scale=tab_planes[jt * JT // HALF_J][:, a, j0 : j0 + JT],
+                rhs_scale=tab_planes[:, a, jt * JT : (jt + 1) * JT],
                 start=(a == 0),
                 stop=(a == 1),
             )
@@ -171,8 +172,10 @@ def tile_list_meltab_log_kernel(
             )
 
         def apply_sign(b, j0, n):
-            signs = sign[:, PACK * b : PACK * (b + 1)].unsqueeze(1).to_broadcast([P, n, PACK])
-            nc.vector.tensor_tensor(h[b, j0][:], h[b, j0][:], signs, ALU.mult)
+            row = sign_rows[:, b].rearrange("p j t -> p (j t)")
+            signs = row.unsqueeze(1).to_broadcast([P, n // SIGN_ROW, SIGN_ROW * PACK])
+            values = h[b, j0][:].rearrange("p (r j) t -> p r (j t)", j=SIGN_ROW)
+            nc.vector.tensor_tensor(values, values, signs, ALU.mult)
 
         def quantise_power(b, j0, n):
             cols = slice(j0, j0 + n)
@@ -216,30 +219,37 @@ def tile_list_meltab_log_kernel(
                 rows = out[n0 * P : (n0 + per_bank) * P, cols]
                 nc.sync.dma_start(rows.rearrange("(n p) j -> p n j", p=P), result[:])
 
-        move_planes(0, nc.scalar, "planes0")
+        LO, HI, ALL = slice(0, 1), slice(1, 2), slice(0, 2)
+        round_weight(0, ALL, "scalar", "raw2")
+        tab_planes = move_planes("first")
         nc.vector.scalar_tensor_tensor(guess[:], mag[:], 2.0, inv[:], ALU.mult, ALU.mult)
-        pick_pairs(0, "raw2")
-        nc.vector.scalar_tensor_tensor(step[:], guess[:], -0.5, inv[:], ALU.mult, ALU.mult)
-        part_pairs(0, "frames0")
-        nc.vector.scalar_tensor_tensor(root[:], step[:], 1.5, guess[:], ALU.add, ALU.mult)
-        load_weight(2, "raw2")
-        pick_frames(1, "rounded3")
-        pick_pairs(2, "pairs")
-        round_weight(0, ALL, "scalar", "rounded0")
-        load_weight(3, "raw0")
         quantise_weight(0, ALL)
+        nc.vector.scalar_tensor_tensor(step[:], guess[:], -0.5, inv[:], ALU.mult, ALU.mult)
+        load_weight(2, "raw2")
+        pick_pairs(0, "raw0")
+        nc.vector.scalar_tensor_tensor(root[:], step[:], 1.5, guess[:], ALU.add, ALU.mult)
+        part_pairs(0, "frames0")
+        load_weight(3, "raw0")
+        pick_frames(1, "rounded3")
         round_weight(1, 0, "vector", "rounded1")
         round_weight(1, 1, "scalar")
         load_weight(4, "raw1")
         quantise_weight(1, LO)
         quantise_weight(1, HI)
-        transform(0, 0, 0)
-        transform(0, 0, 1)
+        for jt in range(2):
+            for t in range(PACK):
+                product(0, 0, jt, t, 0)
+        for jt in range(2):
+            for t0 in range(0, PACK, 2):
+                for t in (t0, t0 + 1):
+                    product(0, 0, jt, t, 1)
+                for t in (t0, t0 + 1):
+                    square(0, 0, jt, t)
+        pick_frames(2, "rounded1")
+        transform(0, 0, 2)
         round_weight(2, ALL, "vector", "rounded2")
         load_weight(5, "raw2")
         quantise_weight(2, ALL)
-        part_pairs(2, "rounded2")
-        move_planes(1, nc.sync, "rounded1")
         round_weight(3, 0, "vector", "rounded3")
         round_weight(3, 1, "vector")
         load_weight(6, "raw0")
@@ -248,21 +258,20 @@ def tile_list_meltab_log_kernel(
         pick_frames(3, "rounded3")
         transform(1, 0, 0)
         transform(1, 0, 1)
-        round_weight(4, ALL, "vector", "rounded0")
+        round_weight(4, ALL, "vector", "rounded1")
         load_weight(7, "raw1")
         quantise_weight(4, ALL)
-        power(0, 0, JT, 0)
-        round_weight(5, ALL, "vector", "rounded4")
+        round_weight(5, ALL, "vector", "rounded2")
         quantise_weight(5, ALL)
+        power(0, 0, JT, 0)
         round_weight(6, 0, "scalar", "rounded3")
-        transform(0, 0, 2)
+        transform(1, 0, 2)
         round_weight(6, 1, "scalar")
         power(0, JT, JT, 1)
-        transform(1, 0, 2)
-        round_weight(7, ALL, "vector", "rounded0")
+        transform(0, 0, 3)
+        round_weight(7, ALL, "vector", "rounded1")
         quantise_weight(6, ALL)
         quantise_weight(7, ALL)
-        transform(0, 0, 3)
         transform(1, 0, 3)
         power(0, 2 * JT, JT, 0)
         fb_codes = ring.tile([P, 2, N], I32, name="fb_codes", tag="raw0", align_bytes=64)

@@ -23,8 +23,7 @@ JT = 512
 NJ = J // JT
 LIST_COLS = JT // 16
 PIECE = 256
-RUN = 2
-SIGN_ROW = 64
+RUN = 4
 SMALLEST_GAIN = 2.0 ** -100
 
 
@@ -53,9 +52,16 @@ def tile_list_meltab_log_kernel(
             rows = (co, si)[w][a * PASS : (a + 1) * PASS, b * PASS : (b + 1) * PASS]
             nc.sync.dma_start(raw[c][:], rows.rearrange("(p i) c -> p i c", i=PACK))
 
-        load_weight(0, "first")
+        def load_first(side, tag):
+            part = ring.tile([P, PACK, PASS // 2], F32, name="raw_half", tag=tag, align_bytes=64)
+            rows = co[0:PASS, side * PASS // 2 : (side + 1) * PASS // 2]
+            nc.sync.dma_start(part[:], rows.rearrange("(p i) c -> p i c", i=PACK))
+            return part
+
+        first = [load_first(0, "first")]
         word_store = keep.tile([P, T], I32, name="word_store", align_bytes=64)
         nc.sync.dma_start(word_store[:], tab_words[0].rearrange("p t i -> p (t i)").bitcast(I32))
+        first.append(load_first(1, "raw0"))
         load_weight(1, "raw1")
 
         g8 = gain[:].rearrange("p b t -> p (b t)")
@@ -66,10 +72,6 @@ def tile_list_meltab_log_kernel(
         nc.vector.scalar_tensor_tensor(mag[:], g8, -1.0, g8, ALU.mult, ALU.max)
         nc.scalar.activation(inv[:], mag[:], ACT.Abs_reciprocal_sqrt, bias=SMALLEST_GAIN, scale=2.0)
         nc.vector.tensor_scalar(sign[:], g8, 0.0, 0.5, ALU.is_ge, ALU.subtract)
-        sign_rows = keep.tile([P, 2, SIGN_ROW, PACK], BF16, name="sign_rows")
-        nc.scalar.copy(
-            sign_rows[:], sign[:].rearrange("p (b t) -> p b t", b=2).unsqueeze(2).to_broadcast([P, 2, SIGN_ROW, PACK])
-        )
         warm = keep.tile([P, 1], F32, name="warm")
         nc.scalar.activation(warm[:], inv[:, 0:1], ACT.Ln, bias=1.0)
 
@@ -102,7 +104,7 @@ def tile_list_meltab_log_kernel(
         def round_weight(c, u, engine, tag=None):
             if c not in rounded:
                 rounded[c] = ring.tile([P, PACK * PASS], BF16, name="rounded", tag=tag, align_bytes=64)
-            dst = rounded[c][:].rearrange("p (u v m i) -> p u m i v", u=2, v=2, i=PACK)[:, u]
+            dst = rounded[c][:, :].rearrange("p (u v m i) -> p u m i v", u=2, v=2, i=PACK)[:, u]
             src = raw[c][:].rearrange("p i (m u v) -> p u m i v", u=2, v=2)[:, u]
             if engine == "scalar":
                 nc.scalar.copy(dst, src)
@@ -116,6 +118,20 @@ def tile_list_meltab_log_kernel(
             cols = slice(u.start * 2 * P, u.stop * 2 * P)
             nc.vector.quantize_mx(
                 w_codes[c][:, cols].bitcast(FP8X4), w_plane[c][:, cols], rounded[c][:, PACK * cols.start : PACK * cols.stop]
+            )
+
+        def late_pair(c):
+            both = ring.tile([P, 2, PACK * PASS], BF16, name="rounded_pair", tag="rounded_pair", bufs=2, align_bytes=64)
+            rounded[c], rounded[c + 1] = both[:, 0], both[:, 1]
+            return both
+
+        def quantise_pair(c, both):
+            codes = keep.tile([P, 2, PASS], U32, name=f"w_codes{c}", align_bytes=64)
+            plane = keep.tile([P, 2, PASS], U8, name=f"w_plane{c}", align_bytes=64)
+            w_codes[c], w_codes[c + 1], w_plane[c], w_plane[c + 1] = codes[:, 0], codes[:, 1], plane[:, 0], plane[:, 1]
+            nc.vector.quantize_mx(
+                codes[:].rearrange("p a c -> p (a c)").bitcast(FP8X4), plane[:].rearrange("p a c -> p (a c)"),
+                both[:].rearrange("p a c -> p (a c)"),
             )
 
         squares, banks, taken = {}, {}, []
@@ -143,7 +159,7 @@ def tile_list_meltab_log_kernel(
 
         def square(w, b, jt, t, c0=0, n=JT):
             if (w, b, jt * JT + c0) not in squares:
-                tile = ring.tile([P, PACK, n], F32, name=f"squares{w}", bufs=5)
+                tile = ring.tile([P, PACK, n], F32, name=f"squares{w}", bufs=5 - w)
                 for c in range(0, n, P):
                     squares[w, b, jt * JT + c0 + c] = tile, c
             nc.scalar.activation(
@@ -151,13 +167,16 @@ def tile_list_meltab_log_kernel(
                 scale=root[:, PACK * b + t : PACK * b + t + 1],
             )
 
+        def transform_half(w, b, jt, t0):
+            for a in range(2):
+                for t in (t0, t0 + 1):
+                    product(w, b, jt, t, a)
+            for t in (t0, t0 + 1):
+                square(w, b, jt, t)
+
         def transform(w, b, jt):
-            for t0 in range(0, PACK, 2):
-                for t in (t0, t0 + 1):
-                    product(w, b, jt, t, 0)
-                    product(w, b, jt, t, 1)
-                for t in (t0, t0 + 1):
-                    square(w, b, jt, t)
+            transform_half(w, b, jt, 0)
+            transform_half(w, b, jt, 2)
 
         h_codes = [keep.tile([P, J], U32, name=f"h_codes{b}", align_bytes=64) for b in range(2)]
         h_plane = [keep.tile([P, J], U8, name=f"h_plane{b}", align_bytes=64) for b in range(2)]
@@ -172,10 +191,8 @@ def tile_list_meltab_log_kernel(
             )
 
         def apply_sign(b, j0, n):
-            row = sign_rows[:, b].rearrange("p j t -> p (j t)")
-            signs = row.unsqueeze(1).to_broadcast([P, n // SIGN_ROW, SIGN_ROW * PACK])
-            values = h[b, j0][:].rearrange("p (r j) t -> p r (j t)", j=SIGN_ROW)
-            nc.vector.tensor_tensor(values, values, signs, ALU.mult)
+            signs = sign[:, PACK * b : PACK * (b + 1)].unsqueeze(1).to_broadcast([P, n, PACK])
+            nc.vector.tensor_tensor(h[b, j0][:], h[b, j0][:], signs, ALU.mult)
 
         def quantise_power(b, j0, n):
             cols = slice(j0, j0 + n)
@@ -220,31 +237,33 @@ def tile_list_meltab_log_kernel(
                 nc.sync.dma_start(rows.rearrange("(n p) j -> p n j", p=P), result[:])
 
         LO, HI, ALL = slice(0, 1), slice(1, 2), slice(0, 2)
-        round_weight(0, ALL, "scalar", "raw2")
+        rounded[0] = ring.tile([P, PACK * PASS], BF16, name="rounded", tag="rounded2", align_bytes=64)
+        by_side = rounded[0][:].rearrange("p (u v s m i) -> p s u m i v", u=2, v=2, s=2, i=PACK)
+        nc.scalar.copy(by_side[:, 0], first[0][:].rearrange("p i (m u v) -> p u m i v", u=2, v=2))
         tab_planes = move_planes("first")
+        nc.scalar.copy(by_side[:, 1], first[1][:].rearrange("p i (m u v) -> p u m i v", u=2, v=2))
         nc.vector.scalar_tensor_tensor(guess[:], mag[:], 2.0, inv[:], ALU.mult, ALU.mult)
-        quantise_weight(0, ALL)
         nc.vector.scalar_tensor_tensor(step[:], guess[:], -0.5, inv[:], ALU.mult, ALU.mult)
-        load_weight(2, "raw2")
-        pick_pairs(0, "raw0")
         nc.vector.scalar_tensor_tensor(root[:], step[:], 1.5, guess[:], ALU.add, ALU.mult)
+        pick_pairs(0, "raw2")
         part_pairs(0, "frames0")
+        load_weight(2, "raw2")
         load_weight(3, "raw0")
-        pick_frames(1, "rounded3")
-        round_weight(1, 0, "vector", "rounded1")
-        round_weight(1, 1, "scalar")
+        quantise_weight(0, ALL)
+        pick_pairs(1, "rounded3")
+        w_codes[1] = keep.tile([P, PASS], U32, name="w_codes1", align_bytes=64)
+        w_plane[1] = keep.tile([P, PASS], U8, name="w_plane1", align_bytes=64)
+        halves = [ring.tile([P, 2 * PASS], BF16, name="half", tag=tag, align_bytes=64) for tag in ("half0", "rounded1")]
+        src = raw[1][:].rearrange("p i (m u v) -> p u m i v", u=2, v=2)
+        nc.vector.tensor_copy(halves[0][:].rearrange("p (v m i) -> p m i v", v=2, i=PACK), src[:, 0])
+        nc.scalar.copy(halves[1][:].rearrange("p (v m i) -> p m i v", v=2, i=PACK), src[:, 1])
         load_weight(4, "raw1")
-        quantise_weight(1, LO)
-        quantise_weight(1, HI)
-        for jt in range(2):
-            for t in range(PACK):
-                product(0, 0, jt, t, 0)
-        for jt in range(2):
-            for t0 in range(0, PACK, 2):
-                for t in (t0, t0 + 1):
-                    product(0, 0, jt, t, 1)
-                for t in (t0, t0 + 1):
-                    square(0, 0, jt, t)
+        for u in range(2):
+            cols = slice(u * 2 * P, (u + 1) * 2 * P)
+            nc.vector.quantize_mx(w_codes[1][:, cols].bitcast(FP8X4), w_plane[1][:, cols], halves[u][:])
+        part_pairs(1, "half0")
+        transform(0, 0, 0)
+        transform(0, 0, 1)
         pick_frames(2, "rounded1")
         transform(0, 0, 2)
         round_weight(2, ALL, "vector", "rounded2")
@@ -258,20 +277,21 @@ def tile_list_meltab_log_kernel(
         pick_frames(3, "rounded3")
         transform(1, 0, 0)
         transform(1, 0, 1)
-        round_weight(4, ALL, "vector", "rounded1")
+        co_late = late_pair(4)
+        round_weight(4, ALL, "vector")
         load_weight(7, "raw1")
-        quantise_weight(4, ALL)
-        round_weight(5, ALL, "vector", "rounded2")
-        quantise_weight(5, ALL)
+        round_weight(5, ALL, "vector")
         power(0, 0, JT, 0)
-        round_weight(6, 0, "scalar", "rounded3")
-        transform(1, 0, 2)
+        quantise_pair(4, co_late)
+        si_late = late_pair(6)
+        round_weight(6, 0, "scalar")
+        transform_half(1, 0, 2, 0)
         round_weight(6, 1, "scalar")
+        transform_half(1, 0, 2, 2)
+        round_weight(7, ALL, "vector")
         power(0, JT, JT, 1)
+        quantise_pair(6, si_late)
         transform(0, 0, 3)
-        round_weight(7, ALL, "vector", "rounded1")
-        quantise_weight(6, ALL)
-        quantise_weight(7, ALL)
         transform(1, 0, 3)
         power(0, 2 * JT, JT, 0)
         fb_codes = ring.tile([P, 2, N], I32, name="fb_codes", tag="raw0", align_bytes=64)

@@ -1,6 +1,7 @@
 from contextlib import ExitStack
 
 import concourse.mybir as mybir
+from concourse.masks import make_identity
 
 K, F, N, T, J = 1024, 1024, 256, 4096, 2048
 FLOPS = 2 * (2 * K * F * J + F * N * J)
@@ -22,7 +23,7 @@ PASS = P * PACK
 JT = 512
 NJ = J // JT
 LIST_COLS = JT // 16
-PIECE = 256
+BESIDE = 160
 RUN = 4
 SMALLEST_GAIN = 2.0 ** -100
 
@@ -67,13 +68,23 @@ def tile_list_meltab_log_kernel(
         g8 = gain[:].rearrange("p b t -> p (b t)")
         def small(name, dtype=F32):
             return keep.tile([P, 2 * PACK], dtype, name=name)
-        sign, mag, inv = small("sign", BF16), small("mag"), small("inv")
+        mag, inv = small("mag"), small("inv")
+        identity = keep.tile([P, P], BF16, name="identity")
+        make_identity(nc, identity[:])
+        padded = keep.tile([P, P], BF16, name="padded")
+        nc.gpsimd.memset(padded[:], 0.0)
+        turned = keep.tile([P, P], BF16, name="turned")
+        sign_bank = psum.tile([P, 2, P], BF16, name="sign_bank")
+        sign = sign_bank[:, 0, :]
         guess, step, root = small("guess"), small("step"), small("root")
         nc.vector.scalar_tensor_tensor(mag[:], g8, -1.0, g8, ALU.mult, ALU.max)
         nc.scalar.activation(inv[:], mag[:], ACT.Abs_reciprocal_sqrt, bias=SMALLEST_GAIN, scale=2.0)
-        nc.vector.tensor_scalar(sign[:], g8, 0.0, 0.5, ALU.is_ge, ALU.subtract)
+        nc.vector.tensor_scalar(padded[:, 0 : 2 * PACK], g8, 0.0, 0.5, ALU.is_ge, ALU.subtract)
+        nc.tensor.transpose(sign_bank[:, 1, :], padded[:], identity[:])
         warm = keep.tile([P, 1], F32, name="warm")
         nc.scalar.activation(warm[:], inv[:, 0:1], ACT.Ln, bias=1.0)
+        nc.scalar.copy(turned[:], sign_bank[:, 1, :])
+        nc.tensor.transpose(sign, turned[:], identity[:])
 
         picked_scales = keep.tile([P, J], U8, name="picked_scales", align_bytes=64)
         nc.vector.tensor_copy(picked_scales[:], scale_store[:].indirect(offsets[:]))
@@ -134,14 +145,10 @@ def tile_list_meltab_log_kernel(
                 both[:].rearrange("p a c -> p (a c)"),
             )
 
-        squares, banks, taken = {}, {}, []
+        squares, banks = {}, {}
         def next_bank():
-            if len(taken) % 2 == 0:
-                pair = psum.tile([P, 2, JT], F32, name="pair", bufs=4)
-            else:
-                pair = taken[-1]
-            taken.append(pair)
-            return pair[:, (len(taken) - 1) % 2, :]
+            bank = psum.tile([P, JT], F32, name="bank", bufs=7)
+            return bank[:]
 
         def product(w, b, jt, t, a):
             if a == 0:
@@ -159,7 +166,10 @@ def tile_list_meltab_log_kernel(
 
         def square(w, b, jt, t, c0=0, n=JT):
             if (w, b, jt * JT + c0) not in squares:
-                tile = ring.tile([P, PACK, n], F32, name=f"squares{w}", bufs=5 - w)
+                if (w, b, jt) == (0, 0, 1):
+                    tile = ring.tile([P, PACK, n], F32, name="squares", tag="h1", align_bytes=64)
+                else:
+                    tile = ring.tile([P, PACK, n], F32, name=f"squares{w}", bufs=4)
                 for c in range(0, n, P):
                     squares[w, b, jt * JT + c0 + c] = tile, c
             nc.scalar.activation(
@@ -181,12 +191,12 @@ def tile_list_meltab_log_kernel(
         h_codes = [keep.tile([P, J], U32, name=f"h_codes{b}", align_bytes=64) for b in range(2)]
         h_plane = [keep.tile([P, J], U8, name=f"h_plane{b}", align_bytes=64) for b in range(2)]
         h, todo = {}, []
-        def add_squares(dst, b, j0, n):
-            (re2, c), (im2, c) = squares[0, b, j0], squares[1, b, j0]
-            nc.vector.tensor_tensor(
+        def add_squares(engine, dst, b, j0, skip, n):
+            (re2, cr), (im2, ci) = squares[0, b, j0], squares[1, b, j0]
+            engine.tensor_tensor(
                 dst.rearrange("p (c i) t -> p c t i", i=RUN),
-                re2[:, :, c : c + n].rearrange("p t (c i) -> p c t i", i=RUN),
-                im2[:, :, c : c + n].rearrange("p t (c i) -> p c t i", i=RUN),
+                re2[:, :, cr + skip : cr + skip + n].rearrange("p t (c i) -> p c t i", i=RUN),
+                im2[:, :, ci + skip : ci + skip + n].rearrange("p t (c i) -> p c t i", i=RUN),
                 ALU.add,
             )
 
@@ -200,39 +210,40 @@ def tile_list_meltab_log_kernel(
                 h_codes[b][:, cols].bitcast(FP8X4), h_plane[b][:, cols], h[b, j0][:].rearrange("p j t -> p (j t)")
             )
 
-        def power(b, j0, n, part):
-            if part == 1:
-                j0, n = j0 - n, 2 * n
-            else:
-                h[b, j0] = ring.tile([P, n if part is None else 2 * n, PACK], BF16, name="h", bufs=2, align_bytes=64)
-            if part != 0 and todo:
+        def open_span(b, j0, n, beside):
+            h[b, j0] = ring.tile([P, n, PACK], BF16, name="h", tag=f"h{len(todo) % 2}", align_bytes=64)
+            if todo:
                 apply_sign(*todo[-1])
-            lo = n // 2 if part == 1 else 0
-            add_squares(h[b, j0][:, lo:n, :], b, j0 + lo, n - lo)
-            if part != 0:
-                if todo:
-                    quantise_power(*todo[-1])
-                todo.append((b, j0, n))
+            if beside:
+                add_squares(nc.gpsimd, h[b, j0][:, 0:beside, :], b, j0, 0, beside)
+            first_n = min(n, JT)
+            add_squares(nc.vector, h[b, j0][:, beside:first_n, :], b, j0, beside, first_n - beside)
+
+        def close_span(b, j0, n):
+            if n > JT:
+                add_squares(nc.vector, h[b, j0][:, JT:n, :], b, j0 + JT, 0, n - JT)
+            if todo:
+                quantise_power(*todo[-1])
+            todo.append((b, j0, n))
 
         def filters(j0, width):
             cols = slice(j0, j0 + width)
-            pair = psum.tile([P, 2, JT], F32, name="pair", bufs=4)
-            y = pair[:].rearrange("p k j -> p (k j)")[:, 0 : 2 * width].rearrange("p (n j) -> p n j", n=2)
-            for nt in range(N // P):
-                for b in range(2):
-                    nc.tensor.matmul_mx(
-                        y[:, nt, :],
-                        lhsT=fb_codes[:, b, nt * P : (nt + 1) * P].bitcast(FP8X4),
-                        lhsT_scale=fb_plane[:, b, nt * P : (nt + 1) * P],
-                        rhs=h_codes[b][:, cols].bitcast(FP8X4),
-                        rhs_scale=h_plane[b][:, cols],
-                        start=(b == 0),
-                        stop=(b == 1),
-                    )
             per_bank = min(N // P, JT // width)
             for n0 in range(0, N // P, per_bank):
+                y = next_bank()[:, 0 : per_bank * width].rearrange("p (n j) -> p n j", n=per_bank)
+                for nt in range(n0, n0 + per_bank):
+                    for b in range(2):
+                        nc.tensor.matmul_mx(
+                            y[:, nt - n0, :],
+                            lhsT=fb_codes[:, b, nt * P : (nt + 1) * P].bitcast(FP8X4),
+                            lhsT_scale=fb_plane[:, b, nt * P : (nt + 1) * P],
+                            rhs=h_codes[b][:, cols].bitcast(FP8X4),
+                            rhs_scale=h_plane[b][:, cols],
+                            start=(b == 0),
+                            stop=(b == 1),
+                        )
                 result = ring.tile([P, per_bank, width], F32, name="result", bufs=4)
-                nc.scalar.activation(result[:], y[:, n0 : n0 + per_bank, :], ACT.Ln, bias=1.0)
+                nc.scalar.activation(result[:], y, ACT.Ln, bias=1.0)
                 rows = out[n0 * P : (n0 + per_bank) * P, cols]
                 nc.sync.dma_start(rows.rearrange("(n p) j -> p n j", p=P), result[:])
 
@@ -281,19 +292,17 @@ def tile_list_meltab_log_kernel(
         round_weight(4, ALL, "vector")
         load_weight(7, "raw1")
         round_weight(5, ALL, "vector")
-        power(0, 0, JT, 0)
+        open_span(0, 0, 2 * JT, 0)
         quantise_pair(4, co_late)
         si_late = late_pair(6)
-        round_weight(6, 0, "scalar")
-        transform_half(1, 0, 2, 0)
-        round_weight(6, 1, "scalar")
-        transform_half(1, 0, 2, 2)
+        transform(1, 0, 2)
+        round_weight(6, ALL, "vector")
         round_weight(7, ALL, "vector")
-        power(0, JT, JT, 1)
         quantise_pair(6, si_late)
+        close_span(0, 0, 2 * JT)
+        open_span(0, 2 * JT, 2 * JT, BESIDE)
         transform(0, 0, 3)
         transform(1, 0, 3)
-        power(0, 2 * JT, JT, 0)
         fb_codes = ring.tile([P, 2, N], I32, name="fb_codes", tag="raw0", align_bytes=64)
         nc.sync.dma_start(fb_codes[:], fb_words.rearrange("b p n i -> p b (n i)").bitcast(I32))
         fb_plane = ring.tile([P, 2, N], U8, name="fb_plane", tag="raw2", align_bytes=64)
@@ -302,27 +311,30 @@ def tile_list_meltab_log_kernel(
                 fb_plane[32 * q : 32 * q + 4, :, :].bitcast(I32),
                 fb_scales[:, 4 * q : 4 * q + 4, :].rearrange("b r n -> r b n").bitcast(I32),
             )
-        power(0, 3 * JT, JT, 1)
-        for jt in range(NJ - 1):
-            transform(0, 1, jt)
-            transform(1, 1, jt)
-            if jt < NJ - 2:
-                power(1, jt * JT, JT, jt)
-            else:
-                power(1, jt * JT, JT // 2, None)
-                power(1, jt * JT + JT // 2, JT // 2, None)
-        for w in range(2):
-            for t in range(PACK):
-                product(w, 1, NJ - 1, t, 0)
-                product(w, 1, NJ - 1, t, 1)
-            for t in range(PACK):
-                square(w, 1, NJ - 1, t, 0, JT // 2)
-        for w in range(2):
-            for t in range(PACK):
-                square(w, 1, NJ - 1, t, JT // 2, JT // 2)
+        close_span(0, 2 * JT, 2 * JT)
+        transform(0, 1, 0)
+        transform(1, 1, 0)
+        open_span(1, 0, 2 * JT, BESIDE)
+        transform(0, 1, 1)
+        transform(1, 1, 1)
+        close_span(1, 0, 2 * JT)
+        transform(0, 1, 2)
+        transform(1, 1, 2)
+        open_span(1, 2 * JT, JT // 2, BESIDE)
+        close_span(1, 2 * JT, JT // 2)
+        open_span(1, 2 * JT + JT // 2, JT // 2, 0)
+        close_span(1, 2 * JT + JT // 2, JT // 2)
+        transform(0, 1, 3)
+        for t in range(PACK):
+            product(1, 1, 3, t, 0)
+            product(1, 1, 3, t, 1)
+            square(1, 1, 3, t, 0, JT // 2)
+        for t in range(PACK):
+            square(1, 1, 3, t, JT // 2, JT // 2)
         last = [(J - JT, 2 * P), (J - 2 * P, P), (J - P, P)]
         for j0, n in last:
-            power(1, j0, n, None)
+            open_span(1, j0, n, 0)
+            close_span(1, j0, n)
         apply_sign(*todo[-1])
         quantise_power(*todo[-1])
         for j0, n in [(0, JT), (JT, JT), (2 * JT, JT // 2), (2 * JT + JT // 2, JT // 2)] + last:

@@ -107,10 +107,6 @@ def tile_list_meltab_log_kernel(
             frames[jt] = ring.tile([P, 2, JT], U16, name="frames", tag=tag, align_bytes=64)
             nc.vector.tensor_copy(frames[jt][:], pairs[jt][:].bitcast(U16).rearrange("p (j d) -> p d j", d=2))
 
-        def pick_frames(jt, tag):
-            pick_pairs(jt, tag)
-            part_pairs(jt, f"frames{jt}")
-
         rounded, w_codes, w_plane = {}, {}, {}
         def round_weight(c, u, engine, tag=None):
             if c not in rounded:
@@ -231,16 +227,16 @@ def tile_list_meltab_log_kernel(
             per_bank = min(N // P, JT // width)
             for n0 in range(0, N // P, per_bank):
                 y = next_bank()[:, 0 : per_bank * width].rearrange("p (n j) -> p n j", n=per_bank)
-                for nt in range(n0, n0 + per_bank):
-                    for b in range(2):
+                for b in range(2):
+                    for nt in range(n0, n0 + per_bank):
                         nc.tensor.matmul_mx(
                             y[:, nt - n0, :],
                             lhsT=fb_codes[:, b, nt * P : (nt + 1) * P].bitcast(FP8X4),
                             lhsT_scale=fb_plane[:, b, nt * P : (nt + 1) * P],
                             rhs=h_codes[b][:, cols].bitcast(FP8X4),
                             rhs_scale=h_plane[b][:, cols],
-                            start=(b == 0),
-                            stop=(b == 1),
+                            start=(b == 0 and nt == n0),
+                            stop=(b == 1 and nt == n0 + per_bank - 1),
                         )
                 result = ring.tile([P, per_bank, width], F32, name="result", bufs=4)
                 nc.scalar.activation(result[:], y, ACT.Ln, bias=1.0)
@@ -275,28 +271,32 @@ def tile_list_meltab_log_kernel(
         part_pairs(1, "half0")
         transform(0, 0, 0)
         transform(0, 0, 1)
-        pick_frames(2, "rounded1")
-        transform(0, 0, 2)
+        pick_pairs(2, "rounded1")
         round_weight(2, ALL, "vector", "rounded2")
-        load_weight(5, "raw2")
+        part_pairs(2, "raw2")
+        load_weight(5, "rounded1")
         quantise_weight(2, ALL)
         round_weight(3, 0, "vector", "rounded3")
         round_weight(3, 1, "vector")
         load_weight(6, "raw0")
         quantise_weight(3, LO)
         quantise_weight(3, HI)
-        pick_frames(3, "rounded3")
+        pick_pairs(3, "rounded3")
+        transform_half(0, 0, 2, 0)
         transform(1, 0, 0)
         transform(1, 0, 1)
+        transform_half(0, 0, 2, 2)
         co_late = late_pair(4)
         round_weight(4, ALL, "vector")
-        load_weight(7, "raw1")
+        part_pairs(3, "raw1")
+        load_weight(7, "rounded3")
         round_weight(5, ALL, "vector")
         open_span(0, 0, 2 * JT, 0)
         quantise_pair(4, co_late)
         si_late = late_pair(6)
+        round_weight(6, 0, "scalar")
         transform(1, 0, 2)
-        round_weight(6, ALL, "vector")
+        round_weight(6, 1, "vector")
         round_weight(7, ALL, "vector")
         quantise_pair(6, si_late)
         close_span(0, 0, 2 * JT)
@@ -305,7 +305,7 @@ def tile_list_meltab_log_kernel(
         transform(1, 0, 3)
         fb_codes = ring.tile([P, 2, N], I32, name="fb_codes", tag="raw0", align_bytes=64)
         nc.sync.dma_start(fb_codes[:], fb_words.rearrange("b p n i -> p b (n i)").bitcast(I32))
-        fb_plane = ring.tile([P, 2, N], U8, name="fb_plane", tag="raw2", align_bytes=64)
+        fb_plane = ring.tile([P, 2, N], U8, name="fb_plane", tag="rounded1", align_bytes=64)
         for q in range(4):
             nc.sync.dma_start(
                 fb_plane[32 * q : 32 * q + 4, :, :].bitcast(I32),

@@ -141,10 +141,14 @@ def tile_list_meltab_log_kernel(
                 both[:].rearrange("p a c -> p (a c)"),
             )
 
-        squares, banks = {}, {}
+        squares, banks, taken = {}, {}, []
         def next_bank():
-            bank = psum.tile([P, JT], F32, name="bank", bufs=7)
-            return bank[:]
+            if len(taken) % 2 == 0:
+                pair = psum.tile([P, 2, JT], F32, name="pair", bufs=3)
+            else:
+                pair = taken[-1]
+            taken.append(pair)
+            return pair[:, (len(taken) - 1) % 2, :]
 
         def product(w, b, jt, t, a):
             if a == 0:
@@ -184,6 +188,16 @@ def tile_list_meltab_log_kernel(
             transform_half(w, b, jt, 0)
             transform_half(w, b, jt, 2)
 
+        def transform_in_halves(jt):
+            for t0 in range(0, PACK, 2):
+                for a in range(2):
+                    for t in (t0, t0 + 1):
+                        product(1, 1, jt, t, a)
+                for t in (t0, t0 + 1):
+                    square(1, 1, jt, t, 0, JT // 2)
+            for t in range(PACK):
+                square(1, 1, jt, t, JT // 2, JT // 2)
+
         h_codes = [keep.tile([P, J], U32, name=f"h_codes{b}", align_bytes=64) for b in range(2)]
         h_plane = [keep.tile([P, J], U8, name=f"h_plane{b}", align_bytes=64) for b in range(2)]
         h, todo = {}, []
@@ -222,24 +236,29 @@ def tile_list_meltab_log_kernel(
                 quantise_power(*todo[-1])
             todo.append((b, j0, n))
 
-        def filters(j0, width):
+        def filters(j0, width, in_single):
             cols = slice(j0, j0 + width)
             per_bank = min(N // P, JT // width)
+            if in_single:
+                single = psum.tile([P, 2, width], F32, name="single")
+                y = single[:]
+            else:
+                pair = psum.tile([P, 2, JT], F32, name="pair", bufs=3)
+                y = pair[:].rearrange("p k j -> p (k j)")[:, 0 : 2 * width].rearrange("p (n j) -> p n j", n=2)
+            for b in range(2):
+                for nt in range(N // P):
+                    nc.tensor.matmul_mx(
+                        y[:, nt, :],
+                        lhsT=fb_codes[:, b, nt * P : (nt + 1) * P].bitcast(FP8X4),
+                        lhsT_scale=fb_plane[:, b, nt * P : (nt + 1) * P],
+                        rhs=h_codes[b][:, cols].bitcast(FP8X4),
+                        rhs_scale=h_plane[b][:, cols],
+                        start=(b == 0 and nt % per_bank == 0),
+                        stop=(b == 1 and nt % per_bank == per_bank - 1),
+                    )
             for n0 in range(0, N // P, per_bank):
-                y = next_bank()[:, 0 : per_bank * width].rearrange("p (n j) -> p n j", n=per_bank)
-                for b in range(2):
-                    for nt in range(n0, n0 + per_bank):
-                        nc.tensor.matmul_mx(
-                            y[:, nt - n0, :],
-                            lhsT=fb_codes[:, b, nt * P : (nt + 1) * P].bitcast(FP8X4),
-                            lhsT_scale=fb_plane[:, b, nt * P : (nt + 1) * P],
-                            rhs=h_codes[b][:, cols].bitcast(FP8X4),
-                            rhs_scale=h_plane[b][:, cols],
-                            start=(b == 0 and nt == n0),
-                            stop=(b == 1 and nt == n0 + per_bank - 1),
-                        )
                 result = ring.tile([P, per_bank, width], F32, name="result", bufs=4)
-                nc.scalar.activation(result[:], y, ACT.Ln, bias=1.0)
+                nc.scalar.activation(result[:], y[:, n0 : n0 + per_bank, :], ACT.Ln, bias=1.0)
                 rows = out[n0 * P : (n0 + per_bank) * P, cols]
                 nc.sync.dma_start(rows.rearrange("(n p) j -> p n j", p=P), result[:])
 
@@ -319,23 +338,18 @@ def tile_list_meltab_log_kernel(
         transform(1, 1, 1)
         close_span(1, 0, 2 * JT)
         transform(0, 1, 2)
-        transform(1, 1, 2)
+        transform_in_halves(2)
         open_span(1, 2 * JT, JT // 2, BESIDE)
         close_span(1, 2 * JT, JT // 2)
         open_span(1, 2 * JT + JT // 2, JT // 2, 0)
         close_span(1, 2 * JT + JT // 2, JT // 2)
         transform(0, 1, 3)
-        for t in range(PACK):
-            product(1, 1, 3, t, 0)
-            product(1, 1, 3, t, 1)
-            square(1, 1, 3, t, 0, JT // 2)
-        for t in range(PACK):
-            square(1, 1, 3, t, JT // 2, JT // 2)
+        transform_in_halves(3)
         last = [(J - JT, 2 * P), (J - 2 * P, P), (J - P, P)]
         for j0, n in last:
             open_span(1, j0, n, 0)
             close_span(1, j0, n)
         apply_sign(*todo[-1])
         quantise_power(*todo[-1])
-        for j0, n in [(0, JT), (JT, JT), (2 * JT, JT // 2), (2 * JT + JT // 2, JT // 2)] + last:
-            filters(j0, n)
+        for k, (j0, n) in enumerate([(0, JT), (JT, JT), (2 * JT, JT // 2), (2 * JT + JT // 2, JT // 2)] + last):
+            filters(j0, n, k % 3 == 2)

@@ -20,12 +20,11 @@ ACT = mybir.ActivationFunctionType
 P = 128
 PACK = 4
 PASS = P * PACK
+HALF = PASS // 2
 JT = 512
-NJ = J // JT
 LIST_COLS = JT // 16
-BESIDE = 160
+BESIDE = 192
 RUN = 4
-SMALLEST_GAIN = 2.0 ** -100
 
 
 def tile_list_meltab_log_kernel(
@@ -34,6 +33,7 @@ def tile_list_meltab_log_kernel(
     nc = tc.nc
     with ExitStack() as ctx:
         keep = ctx.enter_context(tc.tile_pool(name="keep", bufs=1))
+        placed = ctx.enter_context(tc.tile_pool(name="placed", bufs=1))
         ring = ctx.enter_context(tc.tile_pool(name="ring", bufs=1))
         psum = ctx.enter_context(tc.psum_pool(name="psum", bufs=1))
 
@@ -46,100 +46,96 @@ def tile_list_meltab_log_kernel(
         gain = keep.tile([P, 2, PACK], F32, name="gain")
         nc.scalar.dma_start(gain[:], gn.rearrange("(b p t) -> p b t", b=2, t=PACK))
 
-        raw = {}
-        def load_weight(c, tag):
+        def weight_rows(c, c0, n):
             b, w, a = c // 4, c // 2 % 2, c % 2
-            raw[c] = ring.tile([P, PACK, PASS], F32, name="raw", tag=tag, align_bytes=64)
-            rows = (co, si)[w][a * PASS : (a + 1) * PASS, b * PASS : (b + 1) * PASS]
-            nc.sync.dma_start(raw[c][:], rows.rearrange("(p i) c -> p i c", i=PACK))
+            rows = (co, si)[w][a * PASS : (a + 1) * PASS, b * PASS + c0 : b * PASS + c0 + n]
+            return rows.rearrange("(p i) c -> p i c", i=PACK)
 
-        def load_first(side, tag):
-            part = ring.tile([P, PACK, PASS // 2], F32, name="raw_half", tag=tag, align_bytes=64)
-            rows = co[0:PASS, side * PASS // 2 : (side + 1) * PASS // 2]
-            nc.sync.dma_start(part[:], rows.rearrange("(p i) c -> p i c", i=PACK))
-            return part
+        raw = {}
+        def buffer(shape, dtype, name, where):
+            if isinstance(where, int):
+                return placed.tile(shape, dtype, name=name, offset=where, align_bytes=64)
+            return ring.tile(shape, dtype, name=name, tag=where, align_bytes=64)
 
-        first = [load_first(0, "first")]
+        def load_weight(c, where):
+            raw[c] = buffer([P, PACK, PASS], F32, f"raw{c}", where)
+            nc.sync.dma_start(raw[c][:], weight_rows(c, 0, PASS))
+
+        def load_half(c, side, where):
+            raw[c, side] = buffer([P, PACK, HALF], F32, f"raw{c}_{side}", where)
+            nc.sync.dma_start(raw[c, side][:], weight_rows(c, side * HALF, HALF))
+
+        load_half(0, 0, 8192)
         word_store = keep.tile([P, T], I32, name="word_store", align_bytes=64)
         nc.sync.dma_start(word_store[:], tab_words[0].rearrange("p t i -> p (t i)").bitcast(I32))
-        first.append(load_first(1, "raw0"))
-        load_weight(1, "raw1")
 
         g8 = gain[:].rearrange("p b t -> p (b t)")
-        def small(name, dtype=F32):
-            return keep.tile([P, 2 * PACK], dtype, name=name)
-        mag, inv = small("mag"), small("inv")
+        mag = keep.tile([P, 2 * PACK], F32, name="mag")
+        root = keep.tile([P, 2 * PACK], F32, name="root")
         identity = keep.tile([P, P], BF16, name="identity")
         make_identity(nc, identity[:])
-        padded = keep.tile([P, P], BF16, name="padded")
-        nc.gpsimd.memset(padded[:], 0.0)
-        turned = keep.tile([P, P], BF16, name="turned")
-        sign_bank = psum.tile([P, 2, P], BF16, name="sign_bank")
-        sign = sign_bank[:, 0, :]
-        guess, step, root = small("guess"), small("step"), small("root")
         nc.vector.scalar_tensor_tensor(mag[:], g8, -1.0, g8, ALU.mult, ALU.max)
-        nc.scalar.activation(inv[:], mag[:], ACT.Abs_reciprocal_sqrt, bias=SMALLEST_GAIN, scale=2.0)
-        nc.vector.tensor_scalar(padded[:, 0 : 2 * PACK], g8, 0.0, 0.5, ALU.is_ge, ALU.subtract)
-        nc.tensor.transpose(sign_bank[:, 1, :], padded[:], identity[:])
-        warm = keep.tile([P, 1], F32, name="warm")
-        nc.scalar.activation(warm[:], inv[:, 0:1], ACT.Ln, bias=1.0)
-        nc.scalar.copy(turned[:], sign_bank[:, 1, :])
-        nc.tensor.transpose(sign, turned[:], identity[:])
+        nc.scalar.activation(root[:], mag[:], ACT.Sqrt)
 
-        picked_scales = keep.tile([P, J], U8, name="picked_scales", align_bytes=64)
-        nc.vector.tensor_copy(picked_scales[:], scale_store[:].indirect(offsets[:]))
-        def move_planes(tag):
-            planes = ring.tile([P, 2, J], U8, name="tab_planes", tag=tag, align_bytes=64)
+        picked, tab_planes = {}, {}
+        def pick_scales(k, tag):
+            picked[k] = ring.tile([P, 2 * JT], U8, name="picked", tag=tag, align_bytes=64)
+            cols = offsets[:, 2 * k * LIST_COLS : 2 * (k + 1) * LIST_COLS]
+            nc.vector.tensor_copy(picked[k][:], scale_store[:].indirect(cols))
+
+        def move_planes(k, queue, where):
+            tab_planes[k] = buffer([P, 2, 2 * JT], U8, f"tab_planes{k}", where)
             for q in range(4):
-                nc.scalar.dma_start(
-                    planes[32 * q : 32 * q + 4, :, :].bitcast(I32),
-                    picked_scales[96 + 8 * q : 96 + 8 * q + 8, :].bitcast(I32),
+                queue.dma_start(
+                    tab_planes[k][32 * q : 32 * q + 4, :, :].bitcast(I32),
+                    picked[k][96 + 8 * q : 96 + 8 * q + 8, :].bitcast(I32),
                 )
-            return planes
 
         pairs, frames = {}, {}
-        def pick_pairs(jt, tag):
-            pairs[jt] = ring.tile([P, JT], U32, name="pairs", tag=tag, align_bytes=64)
-            cols = offsets[:, jt * LIST_COLS : (jt + 1) * LIST_COLS]
-            nc.vector.tensor_copy(pairs[jt][:], word_store[:].bitcast(U32).indirect(cols))
+        def pick_pairs(jt, n, where):
+            tile = buffer([P, n * JT], U32, f"pairs{jt}", where)
+            for k in range(n):
+                pairs[jt + k] = tile[:, k * JT : (k + 1) * JT]
+            cols = offsets[:, jt * LIST_COLS : (jt + n) * LIST_COLS]
+            nc.vector.tensor_copy(tile[:], word_store[:].bitcast(U32).indirect(cols))
 
-        def part_pairs(jt, tag):
-            frames[jt] = ring.tile([P, 2, JT], U16, name="frames", tag=tag, align_bytes=64)
-            nc.vector.tensor_copy(frames[jt][:], pairs[jt][:].bitcast(U16).rearrange("p (j d) -> p d j", d=2))
+        def part_pairs(jt, where):
+            frames[jt] = buffer([P, 2, JT], U16, f"frames{jt}", where)
+            nc.vector.tensor_copy(frames[jt][:], pairs[jt].bitcast(U16).rearrange("p (j d) -> p d j", d=2))
 
         rounded, w_codes, w_plane = {}, {}, {}
-        def round_weight(c, u, engine, tag=None):
-            if c not in rounded:
-                rounded[c] = ring.tile([P, PACK * PASS], BF16, name="rounded", tag=tag, align_bytes=64)
-            dst = rounded[c][:, :].rearrange("p (u v m i) -> p u m i v", u=2, v=2, i=PACK)[:, u]
-            src = raw[c][:].rearrange("p i (m u v) -> p u m i v", u=2, v=2)[:, u]
-            if engine == "scalar":
-                nc.scalar.copy(dst, src)
-            else:
-                nc.vector.tensor_copy(dst, src)
+        def in_pairs(src):
+            return src.rearrange("p i (m u v) -> p u m i v", u=2, v=2)
 
-        def quantise_weight(c, u):
-            if c not in w_codes:
-                w_codes[c] = keep.tile([P, PASS], U32, name=f"w_codes{c}", align_bytes=64)
-                w_plane[c] = keep.tile([P, PASS], U8, name=f"w_plane{c}", align_bytes=64)
-            cols = slice(u.start * 2 * P, u.stop * 2 * P)
-            nc.vector.quantize_mx(
-                w_codes[c][:, cols].bitcast(FP8X4), w_plane[c][:, cols], rounded[c][:, PACK * cols.start : PACK * cols.stop]
-            )
+        def whole(c):
+            return rounded[c].rearrange("p (u v m i) -> p u m i v", u=2, v=2, i=PACK)
 
-        def late_pair(c):
-            both = ring.tile([P, 2, PACK * PASS], BF16, name="rounded_pair", tag="rounded_pair", bufs=2, align_bytes=64)
-            rounded[c], rounded[c + 1] = both[:, 0], both[:, 1]
-            return both
+        def round_weight(c):
+            nc.vector.tensor_copy(whole(c), in_pairs(raw[c][:]))
 
-        def quantise_pair(c, both):
-            codes = keep.tile([P, 2, PASS], U32, name=f"w_codes{c}", align_bytes=64)
-            plane = keep.tile([P, 2, PASS], U8, name=f"w_plane{c}", align_bytes=64)
-            w_codes[c], w_codes[c + 1], w_plane[c], w_plane[c + 1] = codes[:, 0], codes[:, 1], plane[:, 0], plane[:, 1]
-            nc.vector.quantize_mx(
-                codes[:].rearrange("p a c -> p (a c)").bitcast(FP8X4), plane[:].rearrange("p a c -> p (a c)"),
-                both[:].rearrange("p a c -> p (a c)"),
-            )
+        def side_of(c, side):
+            return rounded[c].rearrange("p (u v s m i) -> p s u m i v", u=2, v=2, s=2, i=PACK)[:, side]
+
+        def code_tiles(c, n):
+            codes = keep.tile([P, n * PASS], U32, name=f"w_codes{c}", align_bytes=64)
+            plane = keep.tile([P, n * PASS], U8, name=f"w_plane{c}", align_bytes=64)
+            for k in range(n):
+                w_codes[c + k], w_plane[c + k] = codes[:, k * PASS : (k + 1) * PASS], plane[:, k * PASS : (k + 1) * PASS]
+            return codes, plane
+
+        def quantise_half(c, u, values):
+            cols = slice(u * HALF, (u + 1) * HALF)
+            nc.vector.quantize_mx(w_codes[c][:, cols].bitcast(FP8X4), w_plane[c][:, cols], values)
+
+        def quantise_weights(c, n, values):
+            codes, plane = code_tiles(c, n)
+            nc.vector.quantize_mx(codes[:].bitcast(FP8X4), plane[:], values)
+
+        def rounded_tile(c, n, tag):
+            tile = ring.tile([P, n * PACK * PASS], BF16, name="rounded", tag=tag, align_bytes=64)
+            for k in range(n):
+                rounded[c + k] = tile[:, k * PACK * PASS : (k + 1) * PACK * PASS]
+            return tile
 
         squares, banks, taken = {}, {}, []
         def next_bank():
@@ -159,55 +155,42 @@ def tile_list_meltab_log_kernel(
                 lhsT=w_codes[c][:, t * P : (t + 1) * P].bitcast(FP8X4),
                 lhsT_scale=w_plane[c][:, t * P : (t + 1) * P],
                 rhs=frames[jt][:, a, :].bitcast(FP4X4),
-                rhs_scale=tab_planes[:, a, jt * JT : (jt + 1) * JT],
+                rhs_scale=tab_planes[jt // 2][:, a, jt % 2 * JT : (jt % 2 + 1) * JT],
                 start=(a == 0),
                 stop=(a == 1),
             )
 
-        def square(w, b, jt, t, c0=0, n=JT):
+        def square(w, b, jt, t, c0, n):
             if (w, b, jt * JT + c0) not in squares:
-                if (w, b, jt) == (0, 0, 1):
-                    tile = ring.tile([P, PACK, n], F32, name="squares", tag="h1", align_bytes=64)
-                else:
-                    tile = ring.tile([P, PACK, n], F32, name=f"squares{w}", bufs=4)
-                for c in range(0, n, P):
-                    squares[w, b, jt * JT + c0 + c] = tile, c
+                squares[w, b, jt * JT + c0] = ring.tile([P, PACK, n], F32, name=f"squares{w}", bufs=4)
             nc.scalar.activation(
-                squares[w, b, jt * JT + c0][0][:, t, :], banks[w, b, jt, t][:, c0 : c0 + n], ACT.Square,
+                squares[w, b, jt * JT + c0][:, t, :], banks[w, b, jt, t][:, c0 : c0 + n], ACT.Square,
                 scale=root[:, PACK * b + t : PACK * b + t + 1],
             )
 
-        def transform_half(w, b, jt, t0):
-            for a in range(2):
-                for t in (t0, t0 + 1):
-                    product(w, b, jt, t, a)
-            for t in (t0, t0 + 1):
-                square(w, b, jt, t)
-
-        def transform(w, b, jt):
-            transform_half(w, b, jt, 0)
-            transform_half(w, b, jt, 2)
-
-        def transform_in_halves(jt):
+        def transform(w, b, jt, cut=JT):
             for t0 in range(0, PACK, 2):
                 for a in range(2):
                     for t in (t0, t0 + 1):
-                        product(1, 1, jt, t, a)
+                        product(w, b, jt, t, a)
                 for t in (t0, t0 + 1):
-                    square(1, 1, jt, t, 0, JT // 2)
-            for t in range(PACK):
-                square(1, 1, jt, t, JT // 2, JT // 2)
+                    square(w, b, jt, t, 0, cut)
+            if cut < JT:
+                for t in range(PACK):
+                    square(w, b, jt, t, cut, JT - cut)
+
+        def squared(w, b, j0, n):
+            start = max(j for (ww, bb, j) in squares if (ww, bb) == (w, b) and j <= j0)
+            return squares[w, b, start][:, :, j0 - start : j0 - start + n].rearrange("p t (c i) -> p c t i", i=RUN)
 
         h_codes = [keep.tile([P, J], U32, name=f"h_codes{b}", align_bytes=64) for b in range(2)]
         h_plane = [keep.tile([P, J], U8, name=f"h_plane{b}", align_bytes=64) for b in range(2)]
-        h, todo = {}, []
-        def add_squares(engine, dst, b, j0, skip, n):
-            (re2, cr), (im2, ci) = squares[0, b, j0], squares[1, b, j0]
+        h, spans = {}, []
+        def add_squares(engine, j0, n):
+            b, span0, width = spans[-1]
+            dst = h[b, span0][:, j0 - span0 : j0 - span0 + n, :]
             engine.tensor_tensor(
-                dst.rearrange("p (c i) t -> p c t i", i=RUN),
-                re2[:, :, cr + skip : cr + skip + n].rearrange("p t (c i) -> p c t i", i=RUN),
-                im2[:, :, ci + skip : ci + skip + n].rearrange("p t (c i) -> p c t i", i=RUN),
-                ALU.add,
+                dst.rearrange("p (c i) t -> p c t i", i=RUN), squared(0, b, j0, n), squared(1, b, j0, n), ALU.add
             )
 
         def apply_sign(b, j0, n):
@@ -221,20 +204,20 @@ def tile_list_meltab_log_kernel(
             )
 
         def open_span(b, j0, n, beside):
-            h[b, j0] = ring.tile([P, n, PACK], BF16, name="h", tag=f"h{len(todo) % 2}", align_bytes=64)
-            if todo:
-                apply_sign(*todo[-1])
+            h[b, j0] = ring.tile([P, n, PACK], BF16, name="h", tag=f"h{len(spans) % 2}", align_bytes=64)
+            spans.append((b, j0, n))
+            if len(spans) > 1:
+                apply_sign(*spans[-2])
             if beside:
-                add_squares(nc.gpsimd, h[b, j0][:, 0:beside, :], b, j0, 0, beside)
-            first_n = min(n, JT)
-            add_squares(nc.vector, h[b, j0][:, beside:first_n, :], b, j0, beside, first_n - beside)
+                add_squares(nc.gpsimd, j0, beside)
+            add_squares(nc.vector, j0 + beside, min(n, JT) - beside)
 
-        def close_span(b, j0, n):
+        def close_span():
+            b, j0, n = spans[-1]
             if n > JT:
-                add_squares(nc.vector, h[b, j0][:, JT:n, :], b, j0 + JT, 0, n - JT)
-            if todo:
-                quantise_power(*todo[-1])
-            todo.append((b, j0, n))
+                add_squares(nc.vector, j0 + JT, n - JT)
+            if len(spans) > 1:
+                quantise_power(*spans[-2])
 
         def filters(j0, width, in_single):
             cols = slice(j0, j0 + width)
@@ -257,99 +240,114 @@ def tile_list_meltab_log_kernel(
                         stop=(b == 1 and nt % per_bank == per_bank - 1),
                     )
             for n0 in range(0, N // P, per_bank):
-                result = ring.tile([P, per_bank, width], F32, name="result", bufs=4)
+                result = ring.tile([P, per_bank, width], F32, name="result", bufs=9)
                 nc.scalar.activation(result[:], y[:, n0 : n0 + per_bank, :], ACT.Ln, bias=1.0)
                 rows = out[n0 * P : (n0 + per_bank) * P, cols]
                 nc.sync.dma_start(rows.rearrange("(n p) j -> p n j", p=P), result[:])
 
-        LO, HI, ALL = slice(0, 1), slice(1, 2), slice(0, 2)
-        rounded[0] = ring.tile([P, PACK * PASS], BF16, name="rounded", tag="rounded2", align_bytes=64)
-        by_side = rounded[0][:].rearrange("p (u v s m i) -> p s u m i v", u=2, v=2, s=2, i=PACK)
-        nc.scalar.copy(by_side[:, 0], first[0][:].rearrange("p i (m u v) -> p u m i v", u=2, v=2))
-        tab_planes = move_planes("first")
-        nc.scalar.copy(by_side[:, 1], first[1][:].rearrange("p i (m u v) -> p u m i v", u=2, v=2))
-        nc.vector.scalar_tensor_tensor(guess[:], mag[:], 2.0, inv[:], ALU.mult, ALU.mult)
-        nc.vector.scalar_tensor_tensor(step[:], guess[:], -0.5, inv[:], ALU.mult, ALU.mult)
-        nc.vector.scalar_tensor_tensor(root[:], step[:], 1.5, guess[:], ALU.add, ALU.mult)
-        pick_pairs(0, "raw2")
+        load_half(0, 1, 22528)
+        load_half(1, 0, "rawC")
+        pick_scales(0, "picked0")
+        move_planes(0, nc.sync, "planes0")
+        pick_scales(1, "picked1")
+        rounded_tile(0, 1, "rounded0")
+        nc.scalar.copy(side_of(0, 0), in_pairs(raw[0, 0][:]))
+        load_half(1, 1, 4608)
+        warm = buffer([P, 1], F32, "warm", 8704)
+        nc.scalar.activation(warm[:], root[:, 0:1], ACT.Ln, bias=1.0)
+        repeated = buffer([P, P // 8, 8], BF16, "repeated", 11776)
+        nc.scalar.activation(repeated[:], g8.unsqueeze(1).to_broadcast([P, P // 8, 8]), ACT.Sign)
+        turned = keep.tile([P, P], BF16, name="turned")
+        sign_bank = psum.tile([P, 2, P], BF16, name="sign_bank")
+        sign = sign_bank[:, 0, :]
+        nc.tensor.transpose(sign_bank[:, 1, :], repeated[:].rearrange("p r e -> p (r e)"), identity[:])
+        nc.scalar.copy(turned[:], sign_bank[:, 1, :])
+        nc.tensor.transpose(sign, turned[:], identity[:])
+        load_half(2, 0, 11776)
+        pick_pairs(0, 1, "pairs0")
         part_pairs(0, "frames0")
-        load_weight(2, "raw2")
-        load_weight(3, "raw0")
-        quantise_weight(0, ALL)
-        pick_pairs(1, "rounded3")
-        w_codes[1] = keep.tile([P, PASS], U32, name="w_codes1", align_bytes=64)
-        w_plane[1] = keep.tile([P, PASS], U8, name="w_plane1", align_bytes=64)
-        halves = [ring.tile([P, 2 * PASS], BF16, name="half", tag=tag, align_bytes=64) for tag in ("half0", "rounded1")]
-        src = raw[1][:].rearrange("p i (m u v) -> p u m i v", u=2, v=2)
-        nc.vector.tensor_copy(halves[0][:].rearrange("p (v m i) -> p m i v", v=2, i=PACK), src[:, 0])
-        nc.scalar.copy(halves[1][:].rearrange("p (v m i) -> p m i v", v=2, i=PACK), src[:, 1])
-        load_weight(4, "raw1")
+        load_half(2, 1, "pairs0")
+        code_tiles(0, 1)
         for u in range(2):
-            cols = slice(u * 2 * P, (u + 1) * 2 * P)
-            nc.vector.quantize_mx(w_codes[1][:, cols].bitcast(FP8X4), w_plane[1][:, cols], halves[u][:])
-        part_pairs(1, "half0")
+            nc.scalar.copy(side_of(0, 1)[:, u], in_pairs(raw[0, 1][:])[:, u])
+            quantise_half(0, u, rounded[0][:, u * 2 * PASS : (u + 1) * 2 * PASS])
+        pick_pairs(1, 1, 24576)
+        load_weight(3, 16384)
+        move_planes(1, nc.sync, "rounded0")
+
+        halves = [ring.tile([P, 2 * PASS], BF16, name="half", tag=tag, align_bytes=64) for tag in ("low", "high")]
+        by_side = [half[:].rearrange("p (v s m i) -> p s m i v", v=2, s=2, i=PACK) for half in halves]
+        for u in range(2):
+            nc.scalar.copy(by_side[u][:, 0], in_pairs(raw[1, 0][:])[:, u])
+        load_weight(4, "rawC")
+        nc.scalar.copy(by_side[0][:, 1], in_pairs(raw[1, 1][:])[:, 0])
+        nc.vector.tensor_copy(by_side[1][:, 1], in_pairs(raw[1, 1][:])[:, 1])
+        code_tiles(1, 1)
+        quantise_half(1, 0, halves[0][:])
+        part_pairs(1, 4608)
+        load_weight(5, 24576)
+        quantise_half(1, 1, halves[1][:])
         transform(0, 0, 0)
         transform(0, 0, 1)
-        pick_pairs(2, "rounded1")
-        round_weight(2, ALL, "vector", "rounded2")
-        part_pairs(2, "raw2")
-        load_weight(5, "rounded1")
-        quantise_weight(2, ALL)
-        round_weight(3, 0, "vector", "rounded3")
-        round_weight(3, 1, "vector")
-        load_weight(6, "raw0")
-        quantise_weight(3, LO)
-        quantise_weight(3, HI)
-        pick_pairs(3, "rounded3")
-        transform_half(0, 0, 2, 0)
-        transform(1, 0, 0)
-        transform(1, 0, 1)
-        transform_half(0, 0, 2, 2)
-        co_late = late_pair(4)
-        round_weight(4, ALL, "vector")
-        part_pairs(3, "raw1")
-        load_weight(7, "rounded3")
-        round_weight(5, ALL, "vector")
-        open_span(0, 0, 2 * JT, 0)
-        quantise_pair(4, co_late)
-        si_late = late_pair(6)
-        round_weight(6, 0, "scalar")
-        transform(1, 0, 2)
-        round_weight(6, 1, "vector")
-        round_weight(7, ALL, "vector")
-        quantise_pair(6, si_late)
-        close_span(0, 0, 2 * JT)
-        open_span(0, 2 * JT, 2 * JT, BESIDE)
+
+        pick_pairs(2, 2, "low")
+        rounded_tile(2, 1, "high")
+        nc.gpsimd.tensor_scalar(
+            rounded[2].rearrange("p (t s m i) -> p s m t i", t=PACK, s=2, i=PACK)[:, 0],
+            raw[2, 0][:].rearrange("p i (m t) -> p m t i", t=PACK), 1.0, 0.0, ALU.mult, ALU.add,
+        )
+        nc.vector.tensor_copy(side_of(2, 1), in_pairs(raw[2, 1][:]))
+        load_weight(6, "pairs0")
+        part_pairs(2, 11776)
+        quantise_weights(2, 1, rounded[2])
+        rounded_tile(3, 1, "rounded3")
+        round_weight(3)
+        load_weight(7, 16384)
+        part_pairs(3, "high")
+        quantise_weights(3, 1, rounded[3])
+        transform(0, 0, 2)
         transform(0, 0, 3)
+        transform(1, 0, 0)
+        co_late = rounded_tile(4, 2, "h0")
+        round_weight(4)
+        round_weight(5)
+        quantise_weights(4, 2, co_late[:])
+        si_late = rounded_tile(6, 2, "h1")
+        transform(1, 0, 1)
+        round_weight(6)
+        open_span(0, 0, 2 * JT, 0)
+        nc.scalar.copy(whole(7)[:, 0], in_pairs(raw[7][:])[:, 0])
+        nc.vector.tensor_copy(whole(7)[:, 1], in_pairs(raw[7][:])[:, 1])
+        close_span()
+        quantise_weights(6, 2, si_late[:])
+        transform(1, 0, 2)
         transform(1, 0, 3)
-        fb_codes = ring.tile([P, 2, N], I32, name="fb_codes", tag="raw0", align_bytes=64)
+        open_span(0, 2 * JT, 2 * JT, BESIDE)
+        fb_codes = buffer([P, 2, N], I32, "fb_codes", "rawC")
         nc.sync.dma_start(fb_codes[:], fb_words.rearrange("b p n i -> p b (n i)").bitcast(I32))
-        fb_plane = ring.tile([P, 2, N], U8, name="fb_plane", tag="rounded1", align_bytes=64)
+        fb_plane = buffer([P, 2, N], U8, "fb_plane", 24576)
         for q in range(4):
             nc.sync.dma_start(
                 fb_plane[32 * q : 32 * q + 4, :, :].bitcast(I32),
                 fb_scales[:, 4 * q : 4 * q + 4, :].rearrange("b r n -> r b n").bitcast(I32),
             )
-        close_span(0, 2 * JT, 2 * JT)
-        transform(0, 1, 0)
-        transform(1, 1, 0)
+        close_span()
+        for w in range(2):
+            transform(w, 1, 0)
+            transform(w, 1, 1)
         open_span(1, 0, 2 * JT, BESIDE)
-        transform(0, 1, 1)
-        transform(1, 1, 1)
-        close_span(1, 0, 2 * JT)
+        close_span()
         transform(0, 1, 2)
-        transform_in_halves(2)
-        open_span(1, 2 * JT, JT // 2, BESIDE)
-        close_span(1, 2 * JT, JT // 2)
-        open_span(1, 2 * JT + JT // 2, JT // 2, 0)
-        close_span(1, 2 * JT + JT // 2, JT // 2)
+        transform(1, 1, 2, BESIDE)
+        open_span(1, 2 * JT, JT, BESIDE)
+        close_span()
         transform(0, 1, 3)
-        transform_in_halves(3)
+        transform(1, 1, 3, JT // 2)
         last = [(J - JT, 2 * P), (J - 2 * P, P), (J - P, P)]
         for j0, n in last:
             open_span(1, j0, n, 0)
-            close_span(1, j0, n)
-        apply_sign(*todo[-1])
-        quantise_power(*todo[-1])
-        for k, (j0, n) in enumerate([(0, JT), (JT, JT), (2 * JT, JT // 2), (2 * JT + JT // 2, JT // 2)] + last):
-            filters(j0, n, k % 3 == 2)
+            close_span()
+        apply_sign(*spans[-1])
+        quantise_power(*spans[-1])
+        for k, (j0, n) in enumerate([(0, JT), (JT, JT), (2 * JT, JT)] + last):
+            filters(j0, n, k == 3)

@@ -292,10 +292,7 @@ def tile_list_meltab_log_kernel(
 
         pick_pairs(2, 2, "low")
         rounded_tile(2, 1, "high")
-        nc.gpsimd.tensor_scalar(
-            rounded[2].rearrange("p (t s m i) -> p s m t i", t=PACK, s=2, i=PACK)[:, 0],
-            raw[2, 0][:].rearrange("p i (m t) -> p m t i", t=PACK), 1.0, 0.0, ALU.mult, ALU.add,
-        )
+        nc.vector.tensor_copy(side_of(2, 0), in_pairs(raw[2, 0][:]))
         nc.vector.tensor_copy(side_of(2, 1), in_pairs(raw[2, 1][:]))
         load_weight(6, "pairs0")
         part_pairs(2, 11776)

@@ -290,7 +290,7 @@ def tile_list_meltab_log_kernel(
         transform(0, 0, 0)
         transform(0, 0, 1)
 
-        pick_pairs(2, 2, "low")
+        pick_pairs(2, 1, "low")
         rounded_tile(2, 1, "high")
         nc.vector.tensor_copy(side_of(2, 0), in_pairs(raw[2, 0][:]))
         nc.vector.tensor_copy(side_of(2, 1), in_pairs(raw[2, 1][:]))
@@ -300,13 +300,13 @@ def tile_list_meltab_log_kernel(
         rounded_tile(3, 1, "rounded3")
         round_weight(3)
         load_weight(7, 16384)
-        part_pairs(3, "high")
+        pick_pairs(3, 1, "high")
         quantise_weights(3, 1, rounded[3])
         transform(0, 0, 2)
-        transform(0, 0, 3)
         transform(1, 0, 0)
         co_late = rounded_tile(4, 2, "h0")
         round_weight(4)
+        part_pairs(3, "frames3")
         round_weight(5)
         quantise_weights(4, 2, co_late[:])
         si_late = rounded_tile(6, 2, "h1")
@@ -318,6 +318,7 @@ def tile_list_meltab_log_kernel(
         close_span()
         quantise_weights(6, 2, si_late[:])
         transform(1, 0, 2)
+        transform(0, 0, 3)
         transform(1, 0, 3)
         open_span(0, 2 * JT, 2 * JT, BESIDE)
         fb_codes = buffer([P, 2, N], I32, "fb_codes", "rawC")

@@ -33,7 +33,6 @@ def tile_list_meltab_log_kernel(
     nc = tc.nc
     with ExitStack() as ctx:
         keep = ctx.enter_context(tc.tile_pool(name="keep", bufs=1))
-        placed = ctx.enter_context(tc.tile_pool(name="placed", bufs=1))
         ring = ctx.enter_context(tc.tile_pool(name="ring", bufs=1))
         psum = ctx.enter_context(tc.psum_pool(name="psum", bufs=1))
 
@@ -53,43 +52,30 @@ def tile_list_meltab_log_kernel(
 
         raw = {}
         def buffer(shape, dtype, name, where):
-            if isinstance(where, int):
-                return placed.tile(shape, dtype, name=name, offset=where, align_bytes=64)
             return ring.tile(shape, dtype, name=name, tag=where, align_bytes=64)
 
         def load_weight(c, where):
             raw[c] = buffer([P, PACK, PASS], F32, f"raw{c}", where)
             nc.sync.dma_start(raw[c][:], weight_rows(c, 0, PASS))
 
-        def load_half(c, side, where):
-            raw[c, side] = buffer([P, PACK, HALF], F32, f"raw{c}_{side}", where)
-            nc.sync.dma_start(raw[c, side][:], weight_rows(c, side * HALF, HALF))
-
-        load_half(0, 0, 8192)
         word_store = keep.tile([P, T], I32, name="word_store", align_bytes=64)
         nc.sync.dma_start(word_store[:], tab_words[0].rearrange("p t i -> p (t i)").bitcast(I32))
 
+        load_weight(0, "raw0")
+        load_weight(1, "raw1")
+
         g8 = gain[:].rearrange("p b t -> p (b t)")
-        mag = keep.tile([P, 2 * PACK], F32, name="mag")
+        mag = buffer([P, 2 * PACK], F32, "mag", "mag")
         root = keep.tile([P, 2 * PACK], F32, name="root")
         identity = keep.tile([P, P], BF16, name="identity")
         make_identity(nc, identity[:])
         nc.vector.scalar_tensor_tensor(mag[:], g8, -1.0, g8, ALU.mult, ALU.max)
         nc.scalar.activation(root[:], mag[:], ACT.Sqrt)
 
-        picked, tab_planes = {}, {}
-        def pick_scales(k, tag):
-            picked[k] = ring.tile([P, 2 * JT], U8, name="picked", tag=tag, align_bytes=64)
-            cols = offsets[:, 2 * k * LIST_COLS : 2 * (k + 1) * LIST_COLS]
-            nc.vector.tensor_copy(picked[k][:], scale_store[:].indirect(cols))
-
-        def move_planes(k, queue, where):
-            tab_planes[k] = buffer([P, 2, 2 * JT], U8, f"tab_planes{k}", where)
-            for q in range(4):
-                queue.dma_start(
-                    tab_planes[k][32 * q : 32 * q + 4, :, :].bitcast(I32),
-                    picked[k][96 + 8 * q : 96 + 8 * q + 8, :].bitcast(I32),
-                )
+        warm = keep.tile([P, 1], F32, name="warm")
+        nc.scalar.activation(warm[:], root[:, 0:1], ACT.Ln, bias=1.0)
+        repeated = buffer([P, P // 8, 8], BF16, "repeated", "mag")
+        nc.scalar.activation(repeated[:], g8.unsqueeze(1).to_broadcast([P, P // 8, 8]), ACT.Sign)
 
         pairs, frames = {}, {}
         def pick_pairs(jt, n, where):
@@ -112,9 +98,6 @@ def tile_list_meltab_log_kernel(
 
         def round_weight(c):
             nc.vector.tensor_copy(whole(c), in_pairs(raw[c][:]))
-
-        def side_of(c, side):
-            return rounded[c].rearrange("p (u v s m i) -> p s u m i v", u=2, v=2, s=2, i=PACK)[:, side]
 
         def code_tiles(c, n):
             codes = keep.tile([P, n * PASS], U32, name=f"w_codes{c}", align_bytes=64)
@@ -155,7 +138,7 @@ def tile_list_meltab_log_kernel(
                 lhsT=w_codes[c][:, t * P : (t + 1) * P].bitcast(FP8X4),
                 lhsT_scale=w_plane[c][:, t * P : (t + 1) * P],
                 rhs=frames[jt][:, a, :].bitcast(FP4X4),
-                rhs_scale=tab_planes[jt // 2][:, a, jt % 2 * JT : (jt % 2 + 1) * JT],
+                rhs_scale=tab_planes[:, a, jt * JT : (jt + 1) * JT],
                 start=(a == 0),
                 stop=(a == 1),
             )
@@ -245,61 +228,56 @@ def tile_list_meltab_log_kernel(
                 rows = out[n0 * P : (n0 + per_bank) * P, cols]
                 nc.sync.dma_start(rows.rearrange("(n p) j -> p n j", p=P), result[:])
 
-        load_half(0, 1, 22528)
-        load_half(1, 0, "rawC")
-        pick_scales(0, "picked0")
-        move_planes(0, nc.sync, "planes0")
-        pick_scales(1, "picked1")
-        rounded_tile(0, 1, "rounded0")
-        nc.scalar.copy(side_of(0, 0), in_pairs(raw[0, 0][:]))
-        load_half(1, 1, 4608)
-        warm = buffer([P, 1], F32, "warm", 8704)
-        nc.scalar.activation(warm[:], root[:, 0:1], ACT.Ln, bias=1.0)
-        repeated = buffer([P, P // 8, 8], BF16, "repeated", 11776)
-        nc.scalar.activation(repeated[:], g8.unsqueeze(1).to_broadcast([P, P // 8, 8]), ACT.Sign)
-        turned = keep.tile([P, P], BF16, name="turned")
+        picked = keep.tile([P, J], U8, name="picked", align_bytes=64)
+        nc.vector.tensor_copy(picked[:], scale_store[:].indirect(offsets[:]))
+        tab_planes = keep.tile([P, 2, J], U8, name="tab_planes", align_bytes=64)
+        for q in range(4):
+            nc.scalar.dma_start(
+                tab_planes[32 * q : 32 * q + 4, :, :].bitcast(I32), picked[96 + 8 * q : 96 + 8 * q + 8, :].bitcast(I32)
+            )
+        turned = ring.tile([P, P], BF16, name="turned", tag="raw2", align_bytes=64)
         sign_bank = psum.tile([P, 2, P], BF16, name="sign_bank")
         sign = sign_bank[:, 0, :]
         nc.tensor.transpose(sign_bank[:, 1, :], repeated[:].rearrange("p r e -> p (r e)"), identity[:])
         nc.scalar.copy(turned[:], sign_bank[:, 1, :])
         nc.tensor.transpose(sign, turned[:], identity[:])
-        load_half(2, 0, 11776)
-        pick_pairs(0, 1, "pairs0")
+        load_weight(2, "raw2")
+        pick_pairs(0, 1, "raw3")
+        pick_pairs(1, 1, "pairs1")
         part_pairs(0, "frames0")
-        load_half(2, 1, "pairs0")
-        code_tiles(0, 1)
-        for u in range(2):
-            nc.scalar.copy(side_of(0, 1)[:, u], in_pairs(raw[0, 1][:])[:, u])
-            quantise_half(0, u, rounded[0][:, u * 2 * PASS : (u + 1) * 2 * PASS])
-        pick_pairs(1, 1, 24576)
-        load_weight(3, 16384)
-        move_planes(1, nc.sync, "rounded0")
+        load_weight(3, "raw3")
+        part_pairs(1, "frames1")
 
-        halves = [ring.tile([P, 2 * PASS], BF16, name="half", tag=tag, align_bytes=64) for tag in ("low", "high")]
-        by_side = [half[:].rearrange("p (v s m i) -> p s m i v", v=2, s=2, i=PACK) for half in halves]
-        for u in range(2):
-            nc.scalar.copy(by_side[u][:, 0], in_pairs(raw[1, 0][:])[:, u])
-        load_weight(4, "rawC")
-        nc.scalar.copy(by_side[0][:, 1], in_pairs(raw[1, 1][:])[:, 0])
-        nc.vector.tensor_copy(by_side[1][:, 1], in_pairs(raw[1, 1][:])[:, 1])
+        def half_tile(tag):
+            return ring.tile([P, 2 * PASS], BF16, name="half", tag=tag, align_bytes=64)
+
+        def by_pairs(half):
+            return half[:].rearrange("p (v m i) -> p m i v", v=2, i=PACK)
+
+        halves = {(0, 0): half_tile("low0"), (0, 1): half_tile("high0"), (1, 0): half_tile("low1"), (1, 1): half_tile("high1")}
+        code_tiles(0, 1)
         code_tiles(1, 1)
-        quantise_half(1, 0, halves[0][:])
-        part_pairs(1, 4608)
-        load_weight(5, 24576)
-        quantise_half(1, 1, halves[1][:])
+        nc.scalar.copy(by_pairs(halves[0, 0]), in_pairs(raw[0][:])[:, 0])
+        nc.scalar.copy(by_pairs(halves[0, 1]), in_pairs(raw[0][:])[:, 1])
+        load_weight(4, "raw0")
+        quantise_half(0, 0, halves[0, 0][:])
+        pick_pairs(2, 1, "low0")
+        nc.vector.tensor_copy(by_pairs(halves[1, 0]), in_pairs(raw[1][:])[:, 0])
+        nc.scalar.copy(by_pairs(halves[1, 1]), in_pairs(raw[1][:])[:, 1])
+        quantise_half(0, 1, halves[0, 1][:])
+        quantise_half(1, 0, halves[1, 0][:])
+        load_weight(5, "low1")
+        quantise_half(1, 1, halves[1, 1][:])
+        part_pairs(2, "raw1")
         transform(0, 0, 0)
         transform(0, 0, 1)
-
-        pick_pairs(2, 1, "low")
         rounded_tile(2, 1, "high")
-        nc.vector.tensor_copy(side_of(2, 0), in_pairs(raw[2, 0][:]))
-        nc.vector.tensor_copy(side_of(2, 1), in_pairs(raw[2, 1][:]))
-        load_weight(6, "pairs0")
-        part_pairs(2, 11776)
+        round_weight(2)
+        load_weight(6, "raw2")
         quantise_weights(2, 1, rounded[2])
         rounded_tile(3, 1, "rounded3")
         round_weight(3)
-        load_weight(7, 16384)
+        load_weight(7, "raw3")
         pick_pairs(3, 1, "high")
         quantise_weights(3, 1, rounded[3])
         transform(0, 0, 2)
@@ -321,9 +299,9 @@ def tile_list_meltab_log_kernel(
         transform(0, 0, 3)
         transform(1, 0, 3)
         open_span(0, 2 * JT, 2 * JT, BESIDE)
-        fb_codes = buffer([P, 2, N], I32, "fb_codes", "rawC")
+        fb_codes = buffer([P, 2, N], I32, "fb_codes", "raw0")
         nc.sync.dma_start(fb_codes[:], fb_words.rearrange("b p n i -> p b (n i)").bitcast(I32))
-        fb_plane = buffer([P, 2, N], U8, "fb_plane", 24576)
+        fb_plane = buffer([P, 2, N], U8, "fb_plane", "low1")
         for q in range(4):
             nc.sync.dma_start(
                 fb_plane[32 * q : 32 * q + 4, :, :].bitcast(I32),

@@ -308,9 +308,9 @@ def tile_list_meltab_log_kernel(
                 fb_scales[:, 4 * q : 4 * q + 4, :].rearrange("b r n -> r b n").bitcast(I32),
             )
         close_span()
-        for w in range(2):
-            transform(w, 1, 0)
-            transform(w, 1, 1)
+        for jt in range(2):
+            transform(0, 1, jt)
+            transform(1, 1, jt)
         open_span(1, 0, 2 * JT, BESIDE)
         close_span()
         transform(0, 1, 2)

@@ -62,7 +62,6 @@ def tile_list_meltab_log_kernel(
         nc.sync.dma_start(word_store[:], tab_words[0].rearrange("p t i -> p (t i)").bitcast(I32))
 
         load_weight(0, "raw0")
-        load_weight(1, "raw1")
 
         g8 = gain[:].rearrange("p b t -> p (b t)")
         mag = buffer([P, 2 * PACK], F32, "mag", "mag")
@@ -138,7 +137,7 @@ def tile_list_meltab_log_kernel(
                 lhsT=w_codes[c][:, t * P : (t + 1) * P].bitcast(FP8X4),
                 lhsT_scale=w_plane[c][:, t * P : (t + 1) * P],
                 rhs=frames[jt][:, a, :].bitcast(FP4X4),
-                rhs_scale=tab_planes[:, a, jt * JT : (jt + 1) * JT],
+                rhs_scale=tab_planes[jt // 2][:, a, jt % 2 * JT : (jt % 2 + 1) * JT],
                 start=(a == 0),
                 stop=(a == 1),
             )
@@ -228,17 +227,28 @@ def tile_list_meltab_log_kernel(
                 rows = out[n0 * P : (n0 + per_bank) * P, cols]
                 nc.sync.dma_start(rows.rearrange("(n p) j -> p n j", p=P), result[:])
 
-        picked = keep.tile([P, J], U8, name="picked", align_bytes=64)
-        nc.vector.tensor_copy(picked[:], scale_store[:].indirect(offsets[:]))
-        tab_planes = keep.tile([P, 2, J], U8, name="tab_planes", align_bytes=64)
-        for q in range(4):
-            nc.scalar.dma_start(
-                tab_planes[32 * q : 32 * q + 4, :, :].bitcast(I32), picked[96 + 8 * q : 96 + 8 * q + 8, :].bitcast(I32)
-            )
+        picked, tab_planes = {}, {}
+        def pick_scales(k):
+            picked[k] = keep.tile([P, 2 * JT], U8, name=f"picked{k}", align_bytes=64)
+            cols = offsets[:, 2 * k * LIST_COLS : 2 * (k + 1) * LIST_COLS]
+            nc.vector.tensor_copy(picked[k][:], scale_store[:].indirect(cols))
+
+        def move_planes(k, where):
+            tab_planes[k] = buffer([P, 2, 2 * JT], U8, f"tab_planes{k}", where)
+            for q in range(4):
+                nc.sync.dma_start(
+                    tab_planes[k][32 * q : 32 * q + 4, :, :].bitcast(I32),
+                    picked[k][96 + 8 * q : 96 + 8 * q + 8, :].bitcast(I32),
+                )
+
+        pick_scales(0)
+        move_planes(0, "planes0")
+        pick_scales(1)
         turned = ring.tile([P, P], BF16, name="turned", tag="raw2", align_bytes=64)
         sign_bank = psum.tile([P, 2, P], BF16, name="sign_bank")
         sign = sign_bank[:, 0, :]
         nc.tensor.transpose(sign_bank[:, 1, :], repeated[:].rearrange("p r e -> p (r e)"), identity[:])
+        load_weight(1, "mag")
         nc.scalar.copy(turned[:], sign_bank[:, 1, :])
         nc.tensor.transpose(sign, turned[:], identity[:])
         load_weight(2, "raw2")
@@ -247,6 +257,7 @@ def tile_list_meltab_log_kernel(
         part_pairs(0, "frames0")
         load_weight(3, "raw3")
         part_pairs(1, "frames1")
+        move_planes(1, "pairs1")
 
         def half_tile(tag):
             return ring.tile([P, 2 * PASS], BF16, name="half", tag=tag, align_bytes=64)
@@ -261,14 +272,14 @@ def tile_list_meltab_log_kernel(
         nc.scalar.copy(by_pairs(halves[0, 1]), in_pairs(raw[0][:])[:, 1])
         load_weight(4, "raw0")
         quantise_half(0, 0, halves[0, 0][:])
-        pick_pairs(2, 1, "low0")
-        nc.vector.tensor_copy(by_pairs(halves[1, 0]), in_pairs(raw[1][:])[:, 0])
+        nc.scalar.copy(by_pairs(halves[1, 0]), in_pairs(raw[1][:])[:, 0])
         nc.scalar.copy(by_pairs(halves[1, 1]), in_pairs(raw[1][:])[:, 1])
+        pick_pairs(2, 1, "low0")
         quantise_half(0, 1, halves[0, 1][:])
+        part_pairs(2, "high0")
         quantise_half(1, 0, halves[1, 0][:])
-        load_weight(5, "low1")
         quantise_half(1, 1, halves[1, 1][:])
-        part_pairs(2, "raw1")
+        load_weight(5, "mag")
         transform(0, 0, 0)
         transform(0, 0, 1)
         rounded_tile(2, 1, "high")
@@ -291,8 +302,7 @@ def tile_list_meltab_log_kernel(
         transform(1, 0, 1)
         round_weight(6)
         open_span(0, 0, 2 * JT, 0)
-        nc.scalar.copy(whole(7)[:, 0], in_pairs(raw[7][:])[:, 0])
-        nc.vector.tensor_copy(whole(7)[:, 1], in_pairs(raw[7][:])[:, 1])
+        round_weight(7)
         close_span()
         quantise_weights(6, 2, si_late[:])
         transform(1, 0, 2)
@@ -301,7 +311,7 @@ def tile_list_meltab_log_kernel(
         open_span(0, 2 * JT, 2 * JT, BESIDE)
         fb_codes = buffer([P, 2, N], I32, "fb_codes", "raw0")
         nc.sync.dma_start(fb_codes[:], fb_words.rearrange("b p n i -> p b (n i)").bitcast(I32))
-        fb_plane = buffer([P, 2, N], U8, "fb_plane", "low1")
+        fb_plane = buffer([P, 2, N], U8, "fb_plane", "mag")
         for q in range(4):
             nc.sync.dma_start(
                 fb_plane[32 * q : 32 * q + 4, :, :].bitcast(I32),

@@ -23,7 +23,9 @@ PASS = P * PACK
 HALF = PASS // 2
 JT = 512
 LIST_COLS = JT // 16
-BESIDE = 192
+BESIDE = 208
+BESIDE_SHORT = 64
+SPACER = 96
 RUN = 4
 
 
@@ -179,20 +181,20 @@ def tile_list_meltab_log_kernel(
             signs = sign[:, PACK * b : PACK * (b + 1)].unsqueeze(1).to_broadcast([P, n, PACK])
             nc.vector.tensor_tensor(h[b, j0][:], h[b, j0][:], signs, ALU.mult)
 
-        def quantise_power(b, j0, n):
-            cols = slice(j0, j0 + n)
+        def quantise_power(b, j0, n, skip=0):
+            cols = slice(j0 + skip, j0 + n)
             nc.vector.quantize_mx(
-                h_codes[b][:, cols].bitcast(FP8X4), h_plane[b][:, cols], h[b, j0][:].rearrange("p j t -> p (j t)")
+                h_codes[b][:, cols].bitcast(FP8X4), h_plane[b][:, cols], h[b, j0][:, skip:n, :].rearrange("p j t -> p (j t)")
             )
 
-        def open_span(b, j0, n, beside):
+        def open_span(b, j0, n, beside, first=JT):
             h[b, j0] = ring.tile([P, n, PACK], BF16, name="h", tag=f"h{len(spans) % 2}", align_bytes=64)
             spans.append((b, j0, n))
             if len(spans) > 1:
                 apply_sign(*spans[-2])
             if beside:
                 add_squares(nc.gpsimd, j0, beside)
-            add_squares(nc.vector, j0 + beside, min(n, JT) - beside)
+            add_squares(nc.vector, j0 + beside, min(n, first) - beside)
 
         def close_span():
             b, j0, n = spans[-1]
@@ -201,7 +203,7 @@ def tile_list_meltab_log_kernel(
             if len(spans) > 1:
                 quantise_power(*spans[-2])
 
-        def filters(j0, width, in_single):
+        def filters(j0, width, in_single, queue):
             cols = slice(j0, j0 + width)
             per_bank = min(N // P, JT // width)
             if in_single:
@@ -225,7 +227,7 @@ def tile_list_meltab_log_kernel(
                 result = ring.tile([P, per_bank, width], F32, name="result", bufs=9)
                 nc.scalar.activation(result[:], y[:, n0 : n0 + per_bank, :], ACT.Ln, bias=1.0)
                 rows = out[n0 * P : (n0 + per_bank) * P, cols]
-                nc.sync.dma_start(rows.rearrange("(n p) j -> p n j", p=P), result[:])
+                queue.dma_start(rows.rearrange("(n p) j -> p n j", p=P), result[:])
 
         picked, tab_planes = {}, {}
         def pick_scales(k):
@@ -270,14 +272,14 @@ def tile_list_meltab_log_kernel(
         code_tiles(1, 1)
         nc.scalar.copy(by_pairs(halves[0, 0]), in_pairs(raw[0][:])[:, 0])
         nc.scalar.copy(by_pairs(halves[0, 1]), in_pairs(raw[0][:])[:, 1])
-        load_weight(4, "raw0")
         quantise_half(0, 0, halves[0, 0][:])
+        load_weight(4, "low0")
         nc.scalar.copy(by_pairs(halves[1, 0]), in_pairs(raw[1][:])[:, 0])
         nc.scalar.copy(by_pairs(halves[1, 1]), in_pairs(raw[1][:])[:, 1])
-        pick_pairs(2, 1, "low0")
         quantise_half(0, 1, halves[0, 1][:])
-        part_pairs(2, "high0")
+        pick_pairs(2, 1, "raw0")
         quantise_half(1, 0, halves[1, 0][:])
+        part_pairs(2, "low1")
         quantise_half(1, 1, halves[1, 1][:])
         load_weight(5, "mag")
         transform(0, 0, 0)
@@ -285,17 +287,17 @@ def tile_list_meltab_log_kernel(
         rounded_tile(2, 1, "high")
         round_weight(2)
         load_weight(6, "raw2")
-        quantise_weights(2, 1, rounded[2])
+        pick_pairs(3, 1, "high1")
         rounded_tile(3, 1, "rounded3")
         round_weight(3)
         load_weight(7, "raw3")
-        pick_pairs(3, 1, "high")
+        quantise_weights(2, 1, rounded[2])
         quantise_weights(3, 1, rounded[3])
+        part_pairs(3, "frames3")
         transform(0, 0, 2)
         transform(1, 0, 0)
         co_late = rounded_tile(4, 2, "h0")
         round_weight(4)
-        part_pairs(3, "frames3")
         round_weight(5)
         quantise_weights(4, 2, co_late[:])
         si_late = rounded_tile(6, 2, "h1")
@@ -309,7 +311,7 @@ def tile_list_meltab_log_kernel(
         transform(0, 0, 3)
         transform(1, 0, 3)
         open_span(0, 2 * JT, 2 * JT, BESIDE)
-        fb_codes = buffer([P, 2, N], I32, "fb_codes", "raw0")
+        fb_codes = buffer([P, 2, N], I32, "fb_codes", "low0")
         nc.sync.dma_start(fb_codes[:], fb_words.rearrange("b p n i -> p b (n i)").bitcast(I32))
         fb_plane = buffer([P, 2, N], U8, "fb_plane", "mag")
         for q in range(4):
@@ -325,15 +327,17 @@ def tile_list_meltab_log_kernel(
         close_span()
         transform(0, 1, 2)
         transform(1, 1, 2, BESIDE)
-        open_span(1, 2 * JT, JT, BESIDE)
-        close_span()
+        open_span(1, 2 * JT, JT, BESIDE, BESIDE + SPACER)
+        quantise_power(1, 0, JT)
+        add_squares(nc.vector, 2 * JT + BESIDE + SPACER, JT - BESIDE - SPACER)
+        quantise_power(1, 0, 2 * JT, JT)
         transform(0, 1, 3)
         transform(1, 1, 3, JT // 2)
         last = [(J - JT, 2 * P), (J - 2 * P, P), (J - P, P)]
         for j0, n in last:
-            open_span(1, j0, n, 0)
+            open_span(1, j0, n, BESIDE_SHORT if n > P else 0)
             close_span()
         apply_sign(*spans[-1])
         quantise_power(*spans[-1])
         for k, (j0, n) in enumerate([(0, JT), (JT, JT), (2 * JT, JT)] + last):
-            filters(j0, n, k == 3)
+            filters(j0, n, k == 3, nc.sync)

@@ -26,6 +26,7 @@ LIST_COLS = JT // 16
 BESIDE = 208
 BESIDE_SHORT = 64
 SPACER = 96
+ON_SCALAR = 32
 RUN = 4
 
 
@@ -90,7 +91,7 @@ def tile_list_meltab_log_kernel(
             frames[jt] = buffer([P, 2, JT], U16, f"frames{jt}", where)
             nc.vector.tensor_copy(frames[jt][:], pairs[jt].bitcast(U16).rearrange("p (j d) -> p d j", d=2))
 
-        rounded, w_codes, w_plane = {}, {}, {}
+        rounded, w_codes, w_plane, stationary = {}, {}, {}, {}
         def in_pairs(src):
             return src.rearrange("p i (m u v) -> p u m i v", u=2, v=2)
 
@@ -105,6 +106,8 @@ def tile_list_meltab_log_kernel(
             plane = keep.tile([P, n * PASS], U8, name=f"w_plane{c}", align_bytes=64)
             for k in range(n):
                 w_codes[c + k], w_plane[c + k] = codes[:, k * PASS : (k + 1) * PASS], plane[:, k * PASS : (k + 1) * PASS]
+                for t in range(PACK):
+                    stationary[c + k, t] = w_codes[c + k][:, t * P : (t + 1) * P], w_plane[c + k][:, t * P : (t + 1) * P]
             return codes, plane
 
         def quantise_half(c, u, values):
@@ -121,6 +124,24 @@ def tile_list_meltab_log_kernel(
                 rounded[c + k] = tile[:, k * PACK * PASS : (k + 1) * PACK * PASS]
             return tile
 
+        def late_pair(c, tags, between):
+            values = [buffer([P, 2, 2 * PASS], BF16, "rounded", tag) for tag in tags]
+            codes = keep.tile([P, 2, 2, HALF], U32, name=f"w_codes{c}", align_bytes=64)
+            plane = keep.tile([P, 2, 2, HALF], U8, name=f"w_plane{c}", align_bytes=64)
+            for a in range(2):
+                for u in range(2):
+                    dst = values[u][:, a, :].rearrange("p (v m i) -> p m i v", v=2, i=PACK)
+                    nc.vector.tensor_copy(dst, in_pairs(raw[c + a][:])[:, u])
+                    for v in range(2):
+                        stationary[c + a, 2 * u + v] = codes[:, u, a, v * P : (v + 1) * P], plane[:, u, a, v * P : (v + 1) * P]
+                if a == 0:
+                    between()
+            for u in range(2):
+                nc.vector.quantize_mx(
+                    codes[:, u].rearrange("p a c -> p (a c)").bitcast(FP8X4), plane[:, u].rearrange("p a c -> p (a c)"),
+                    values[u][:].rearrange("p a c -> p (a c)"),
+                )
+
         squares, banks, taken = {}, {}, []
         def next_bank():
             if len(taken) % 2 == 0:
@@ -136,8 +157,8 @@ def tile_list_meltab_log_kernel(
             c = 4 * b + 2 * w + a
             nc.tensor.matmul_mx(
                 banks[w, b, jt, t],
-                lhsT=w_codes[c][:, t * P : (t + 1) * P].bitcast(FP8X4),
-                lhsT_scale=w_plane[c][:, t * P : (t + 1) * P],
+                lhsT=stationary[c, t][0].bitcast(FP8X4),
+                lhsT_scale=stationary[c, t][1],
                 rhs=frames[jt][:, a, :].bitcast(FP4X4),
                 rhs_scale=tab_planes[jt // 2][:, a, jt % 2 * JT : (jt % 2 + 1) * JT],
                 start=(a == 0),
@@ -177,9 +198,9 @@ def tile_list_meltab_log_kernel(
                 dst.rearrange("p (c i) t -> p c t i", i=RUN), squared(0, b, j0, n), squared(1, b, j0, n), ALU.add
             )
 
-        def apply_sign(b, j0, n):
-            signs = sign[:, PACK * b : PACK * (b + 1)].unsqueeze(1).to_broadcast([P, n, PACK])
-            nc.vector.tensor_tensor(h[b, j0][:], h[b, j0][:], signs, ALU.mult)
+        def apply_sign(b, j0, n, skip=0):
+            signs = sign[:, PACK * b : PACK * (b + 1)].unsqueeze(1).to_broadcast([P, n - skip, PACK])
+            nc.vector.tensor_tensor(h[b, j0][:, skip:n, :], h[b, j0][:, skip:n, :], signs, ALU.mult)
 
         def quantise_power(b, j0, n, skip=0):
             cols = slice(j0 + skip, j0 + n)
@@ -258,8 +279,6 @@ def tile_list_meltab_log_kernel(
         pick_pairs(1, 1, "pairs1")
         part_pairs(0, "frames0")
         load_weight(3, "raw3")
-        part_pairs(1, "frames1")
-        move_planes(1, "pairs1")
 
         def half_tile(tag):
             return ring.tile([P, 2 * PASS], BF16, name="half", tag=tag, align_bytes=64)
@@ -272,14 +291,15 @@ def tile_list_meltab_log_kernel(
         code_tiles(1, 1)
         nc.scalar.copy(by_pairs(halves[0, 0]), in_pairs(raw[0][:])[:, 0])
         nc.scalar.copy(by_pairs(halves[0, 1]), in_pairs(raw[0][:])[:, 1])
+        move_planes(1, "raw0")
         quantise_half(0, 0, halves[0, 0][:])
-        load_weight(4, "low0")
         nc.scalar.copy(by_pairs(halves[1, 0]), in_pairs(raw[1][:])[:, 0])
         nc.scalar.copy(by_pairs(halves[1, 1]), in_pairs(raw[1][:])[:, 1])
+        pick_pairs(2, 1, "low0")
         quantise_half(0, 1, halves[0, 1][:])
-        pick_pairs(2, 1, "raw0")
+        load_weight(4, "high0")
         quantise_half(1, 0, halves[1, 0][:])
-        part_pairs(2, "low1")
+        part_pairs(1, "low1")
         quantise_half(1, 1, halves[1, 1][:])
         load_weight(5, "mag")
         transform(0, 0, 0)
@@ -287,31 +307,29 @@ def tile_list_meltab_log_kernel(
         rounded_tile(2, 1, "high")
         round_weight(2)
         load_weight(6, "raw2")
-        pick_pairs(3, 1, "high1")
+        part_pairs(2, "high1")
+        quantise_weights(2, 1, rounded[2])
         rounded_tile(3, 1, "rounded3")
         round_weight(3)
         load_weight(7, "raw3")
-        quantise_weights(2, 1, rounded[2])
+        pick_pairs(3, 1, "high")
         quantise_weights(3, 1, rounded[3])
-        part_pairs(3, "frames3")
         transform(0, 0, 2)
         transform(1, 0, 0)
-        co_late = rounded_tile(4, 2, "h0")
-        round_weight(4)
-        round_weight(5)
-        quantise_weights(4, 2, co_late[:])
+        late_pair(4, ("h0", "rounded3"), lambda: part_pairs(3, "frames3"))
         si_late = rounded_tile(6, 2, "h1")
         transform(1, 0, 1)
         round_weight(6)
         open_span(0, 0, 2 * JT, 0)
-        round_weight(7)
+        nc.scalar.copy(whole(7)[:, :, 0:ON_SCALAR], in_pairs(raw[7][:])[:, :, 0:ON_SCALAR])
+        nc.vector.tensor_copy(whole(7)[:, :, ON_SCALAR:P], in_pairs(raw[7][:])[:, :, ON_SCALAR:P])
         close_span()
         quantise_weights(6, 2, si_late[:])
         transform(1, 0, 2)
         transform(0, 0, 3)
         transform(1, 0, 3)
         open_span(0, 2 * JT, 2 * JT, BESIDE)
-        fb_codes = buffer([P, 2, N], I32, "fb_codes", "low0")
+        fb_codes = buffer([P, 2, N], I32, "fb_codes", "high0")
         nc.sync.dma_start(fb_codes[:], fb_words.rearrange("b p n i -> p b (n i)").bitcast(I32))
         fb_plane = buffer([P, 2, N], U8, "fb_plane", "mag")
         for q in range(4):
@@ -334,10 +352,13 @@ def tile_list_meltab_log_kernel(
         transform(0, 1, 3)
         transform(1, 1, 3, JT // 2)
         last = [(J - JT, 2 * P), (J - 2 * P, P), (J - P, P)]
-        for j0, n in last:
-            open_span(1, j0, n, BESIDE_SHORT if n > P else 0)
-            close_span()
-        apply_sign(*spans[-1])
-        quantise_power(*spans[-1])
+        open_span(1, J - JT, 2 * P, BESIDE_SHORT)
+        close_span()
+        open_span(1, J - 2 * P, 2 * P, 0)
+        close_span()
+        apply_sign(1, J - 2 * P, P)
+        apply_sign(1, J - 2 * P, 2 * P, P)
+        quantise_power(1, J - 2 * P, P)
+        quantise_power(1, J - 2 * P, 2 * P, P)
         for k, (j0, n) in enumerate([(0, JT), (JT, JT), (2 * JT, JT)] + last):
             filters(j0, n, k == 3, nc.sync)

@@ -42,7 +42,7 @@ def tile_list_meltab_log_kernel(
         offsets = keep.tile([P, J // 16], U16, name="offsets")
         nc.sync.dma_start(offsets[:], offs)
 
-        scale_store = keep.tile([P, T], U8, name="scale_store", align_bytes=64)
+        scale_store = keep.tile([P, T], U8, name="scale_store", align_bytes=256)
         nc.vector.memset(scale_store[0:96, :].bitcast(I32), 0)
         nc.sync.dma_start(scale_store[96:128, :].bitcast(I32), tab_scales.rearrange("a z t -> z a t").bitcast(I32))
         gain = keep.tile([P, 2, PACK], F32, name="gain")
@@ -55,13 +55,13 @@ def tile_list_meltab_log_kernel(
 
         raw = {}
         def buffer(shape, dtype, name, where):
-            return ring.tile(shape, dtype, name=name, tag=where, align_bytes=64)
+            return ring.tile(shape, dtype, name=name, tag=where, align_bytes=256)
 
         def load_weight(c, where):
             raw[c] = buffer([P, PACK, PASS], F32, f"raw{c}", where)
             nc.sync.dma_start(raw[c][:], weight_rows(c, 0, PASS))
 
-        word_store = keep.tile([P, T], I32, name="word_store", align_bytes=64)
+        word_store = keep.tile([P, T], I32, name="word_store", align_bytes=256)
         nc.sync.dma_start(word_store[:], tab_words[0].rearrange("p t i -> p (t i)").bitcast(I32))
 
         load_weight(0, "raw0")
@@ -102,8 +102,8 @@ def tile_list_meltab_log_kernel(
             nc.vector.tensor_copy(whole(c), in_pairs(raw[c][:]))
 
         def code_tiles(c, n):
-            codes = keep.tile([P, n * PASS], U32, name=f"w_codes{c}", align_bytes=64)
-            plane = keep.tile([P, n * PASS], U8, name=f"w_plane{c}", align_bytes=64)
+            codes = keep.tile([P, n * PASS], U32, name=f"w_codes{c}", align_bytes=256)
+            plane = keep.tile([P, n * PASS], U8, name=f"w_plane{c}", align_bytes=256)
             for k in range(n):
                 w_codes[c + k], w_plane[c + k] = codes[:, k * PASS : (k + 1) * PASS], plane[:, k * PASS : (k + 1) * PASS]
                 for t in range(PACK):
@@ -119,15 +119,15 @@ def tile_list_meltab_log_kernel(
             nc.vector.quantize_mx(codes[:].bitcast(FP8X4), plane[:], values)
 
         def rounded_tile(c, n, tag):
-            tile = ring.tile([P, n * PACK * PASS], BF16, name="rounded", tag=tag, align_bytes=64)
+            tile = ring.tile([P, n * PACK * PASS], BF16, name="rounded", tag=tag, align_bytes=256)
             for k in range(n):
                 rounded[c + k] = tile[:, k * PACK * PASS : (k + 1) * PACK * PASS]
             return tile
 
         def late_pair(c, tags, between):
             values = [buffer([P, 2, 2 * PASS], BF16, "rounded", tag) for tag in tags]
-            codes = keep.tile([P, 2, 2, HALF], U32, name=f"w_codes{c}", align_bytes=64)
-            plane = keep.tile([P, 2, 2, HALF], U8, name=f"w_plane{c}", align_bytes=64)
+            codes = keep.tile([P, 2, 2, HALF], U32, name=f"w_codes{c}", align_bytes=256)
+            plane = keep.tile([P, 2, 2, HALF], U8, name=f"w_plane{c}", align_bytes=256)
             for a in range(2):
                 for u in range(2):
                     dst = values[u][:, a, :].rearrange("p (v m i) -> p m i v", v=2, i=PACK)
@@ -167,7 +167,7 @@ def tile_list_meltab_log_kernel(
 
         def square(w, b, jt, t, c0, n):
             if (w, b, jt * JT + c0) not in squares:
-                squares[w, b, jt * JT + c0] = ring.tile([P, PACK, n], F32, name=f"squares{w}", bufs=4)
+                squares[w, b, jt * JT + c0] = ring.tile([P, PACK, n], F32, name=f"squares{w}", bufs=4, align_bytes=256)
             nc.scalar.activation(
                 squares[w, b, jt * JT + c0][:, t, :], banks[w, b, jt, t][:, c0 : c0 + n], ACT.Square,
                 scale=root[:, PACK * b + t : PACK * b + t + 1],
@@ -188,8 +188,8 @@ def tile_list_meltab_log_kernel(
             start = max(j for (ww, bb, j) in squares if (ww, bb) == (w, b) and j <= j0)
             return squares[w, b, start][:, :, j0 - start : j0 - start + n].rearrange("p t (c i) -> p c t i", i=RUN)
 
-        h_codes = [keep.tile([P, J], U32, name=f"h_codes{b}", align_bytes=64) for b in range(2)]
-        h_plane = [keep.tile([P, J], U8, name=f"h_plane{b}", align_bytes=64) for b in range(2)]
+        h_codes = [keep.tile([P, J], U32, name=f"h_codes{b}", align_bytes=256) for b in range(2)]
+        h_plane = [keep.tile([P, J], U8, name=f"h_plane{b}", align_bytes=256) for b in range(2)]
         h, spans = {}, []
         def add_squares(engine, j0, n):
             b, span0, width = spans[-1]
@@ -209,7 +209,7 @@ def tile_list_meltab_log_kernel(
             )
 
         def open_span(b, j0, n, beside, first=JT):
-            h[b, j0] = ring.tile([P, n, PACK], BF16, name="h", tag=f"h{len(spans) % 2}", align_bytes=64)
+            h[b, j0] = ring.tile([P, n, PACK], BF16, name="h", tag=f"h{len(spans) % 2}", align_bytes=256)
             spans.append((b, j0, n))
             if len(spans) > 1:
                 apply_sign(*spans[-2])
@@ -245,14 +245,14 @@ def tile_list_meltab_log_kernel(
                         stop=(b == 1 and nt % per_bank == per_bank - 1),
                     )
             for n0 in range(0, N // P, per_bank):
-                result = ring.tile([P, per_bank, width], F32, name="result", bufs=9)
+                result = ring.tile([P, per_bank, width], F32, name="result", bufs=9, align_bytes=256)
                 nc.scalar.activation(result[:], y[:, n0 : n0 + per_bank, :], ACT.Ln, bias=1.0)
                 rows = out[n0 * P : (n0 + per_bank) * P, cols]
                 queue.dma_start(rows.rearrange("(n p) j -> p n j", p=P), result[:])
 
         picked, tab_planes = {}, {}
         def pick_scales(k):
-            picked[k] = keep.tile([P, 2 * JT], U8, name=f"picked{k}", align_bytes=64)
+            picked[k] = keep.tile([P, 2 * JT], U8, name=f"picked{k}", align_bytes=256)
             cols = offsets[:, 2 * k * LIST_COLS : 2 * (k + 1) * LIST_COLS]
             nc.vector.tensor_copy(picked[k][:], scale_store[:].indirect(cols))
 
@@ -267,7 +267,7 @@ def tile_list_meltab_log_kernel(
         pick_scales(0)
         move_planes(0, "planes0")
         pick_scales(1)
-        turned = ring.tile([P, P], BF16, name="turned", tag="raw2", align_bytes=64)
+        turned = ring.tile([P, P], BF16, name="turned", tag="raw2", align_bytes=256)
         sign_bank = psum.tile([P, 2, P], BF16, name="sign_bank")
         sign = sign_bank[:, 0, :]
         nc.tensor.transpose(sign_bank[:, 1, :], repeated[:].rearrange("p r e -> p (r e)"), identity[:])
@@ -281,7 +281,7 @@ def tile_list_meltab_log_kernel(
         load_weight(3, "raw3")
 
         def half_tile(tag):
-            return ring.tile([P, 2 * PASS], BF16, name="half", tag=tag, align_bytes=64)
+            return ring.tile([P, 2 * PASS], BF16, name="half", tag=tag, align_bytes=256)
 
         def by_pairs(half):
             return half[:].rearrange("p (v m i) -> p m i v", v=2, i=PACK)

@@ -71,13 +71,13 @@ def tile_list_meltab_log_kernel(
         root = keep.tile([P, 2 * PACK], F32, name="root")
         identity = keep.tile([P, P], BF16, name="identity")
         make_identity(nc, identity[:])
-        nc.vector.scalar_tensor_tensor(mag[:], g8, -1.0, g8, ALU.mult, ALU.max)
+        nc.scalar.activation(mag[:], g8, ACT.Abs)
+        repeated = keep.tile([P, P // 8, 8], BF16, name="repeated")
+        nc.scalar.activation(repeated[:], g8.unsqueeze(1).to_broadcast([P, P // 8, 8]), ACT.Sign)
         nc.scalar.activation(root[:], mag[:], ACT.Sqrt)
 
         warm = keep.tile([P, 1], F32, name="warm")
         nc.scalar.activation(warm[:], root[:, 0:1], ACT.Ln, bias=1.0)
-        repeated = buffer([P, P // 8, 8], BF16, "repeated", "mag")
-        nc.scalar.activation(repeated[:], g8.unsqueeze(1).to_broadcast([P, P // 8, 8]), ACT.Sign)
 
         pairs, frames = {}, {}
         def pick_pairs(jt, n, where):
@@ -144,7 +144,11 @@ def tile_list_meltab_log_kernel(
 
         squares, banks, taken = {}, {}, []
         def next_bank():
-            if len(taken) % 2 == 0:
+            if not banks:
+                taken.append(None)
+                first_bank = psum.tile([P, JT], F32, name="single")
+                return first_bank[:]
+            if len(taken) % 2 == 0 or taken[-1] is None:
                 pair = psum.tile([P, 2, JT], F32, name="pair", bufs=3)
             else:
                 pair = taken[-1]
@@ -252,7 +256,7 @@ def tile_list_meltab_log_kernel(
 
         picked, tab_planes = {}, {}
         def pick_scales(k):
-            picked[k] = keep.tile([P, 2 * JT], U8, name=f"picked{k}", align_bytes=256)
+            picked[k] = buffer([P, 2 * JT], U8, "picked", ("raw2", "picked1")[k])
             cols = offsets[:, 2 * k * LIST_COLS : 2 * (k + 1) * LIST_COLS]
             nc.vector.tensor_copy(picked[k][:], scale_store[:].indirect(cols))
 
@@ -267,7 +271,7 @@ def tile_list_meltab_log_kernel(
         pick_scales(0)
         move_planes(0, "planes0")
         pick_scales(1)
-        turned = ring.tile([P, P], BF16, name="turned", tag="raw2", align_bytes=256)
+        turned = keep.tile([P, P], BF16, name="turned")
         sign_bank = psum.tile([P, 2, P], BF16, name="sign_bank")
         sign = sign_bank[:, 0, :]
         nc.tensor.transpose(sign_bank[:, 1, :], repeated[:].rearrange("p r e -> p (r e)"), identity[:])
@@ -361,4 +365,4 @@ def tile_list_meltab_log_kernel(
         quantise_power(1, J - 2 * P, P)
         quantise_power(1, J - 2 * P, 2 * P, P)
         for k, (j0, n) in enumerate([(0, JT), (JT, JT), (2 * JT, JT)] + last):
-            filters(j0, n, k == 3, nc.sync)
+            filters(j0, n, k == 3, nc.scalar if j0 + n == J else nc.sync)

@@ -93,13 +93,16 @@ def tile_list_meltab_log_kernel(
 
         rounded, w_codes, w_plane, stationary = {}, {}, {}, {}
         def in_pairs(src):
-            return src.rearrange("p i (m u v) -> p u m i v", u=2, v=2)
+            return src.rearrange("p (h l) (m u v) -> p u m h v l", l=2, u=2, v=2)
 
-        def whole(c):
-            return rounded[c].rearrange("p (u v m i) -> p u m i v", u=2, v=2, i=PACK)
+        def lines_in(c):
+            return raw[c][:].rearrange("p (h l) (m t) -> p m h t l", l=2, t=PACK)
+
+        def lines_out(c):
+            return rounded[c].rearrange("p (t m h l) -> p m h t l", t=PACK, h=2, l=2)
 
         def round_weight(c):
-            nc.vector.tensor_copy(whole(c), in_pairs(raw[c][:]))
+            nc.vector.tensor_copy(lines_out(c), lines_in(c))
 
         def code_tiles(c, n):
             codes = keep.tile([P, n * PASS], U32, name=f"w_codes{c}", align_bytes=256)
@@ -130,7 +133,7 @@ def tile_list_meltab_log_kernel(
             plane = keep.tile([P, 2, 2, HALF], U8, name=f"w_plane{c}", align_bytes=256)
             for a in range(2):
                 for u in range(2):
-                    dst = values[u][:, a, :].rearrange("p (v m i) -> p m i v", v=2, i=PACK)
+                    dst = values[u][:, a, :].rearrange("p (v m h l) -> p m h v l", v=2, h=2, l=2)
                     nc.vector.tensor_copy(dst, in_pairs(raw[c + a][:])[:, u])
                     for v in range(2):
                         stationary[c + a, 2 * u + v] = codes[:, u, a, v * P : (v + 1) * P], plane[:, u, a, v * P : (v + 1) * P]
@@ -288,7 +291,7 @@ def tile_list_meltab_log_kernel(
             return ring.tile([P, 2 * PASS], BF16, name="half", tag=tag, align_bytes=256)
 
         def by_pairs(half):
-            return half[:].rearrange("p (v m i) -> p m i v", v=2, i=PACK)
+            return half[:].rearrange("p (v m h l) -> p m h v l", v=2, h=2, l=2)
 
         halves = {(0, 0): half_tile("low0"), (0, 1): half_tile("high0"), (1, 0): half_tile("low1"), (1, 1): half_tile("high1")}
         code_tiles(0, 1)
@@ -325,8 +328,8 @@ def tile_list_meltab_log_kernel(
         transform(1, 0, 1)
         round_weight(6)
         open_span(0, 0, 2 * JT, 0)
-        nc.scalar.copy(whole(7)[:, :, 0:ON_SCALAR], in_pairs(raw[7][:])[:, :, 0:ON_SCALAR])
-        nc.vector.tensor_copy(whole(7)[:, :, ON_SCALAR:P], in_pairs(raw[7][:])[:, :, ON_SCALAR:P])
+        nc.scalar.copy(lines_out(7)[:, 0:ON_SCALAR], lines_in(7)[:, 0:ON_SCALAR])
+        nc.vector.tensor_copy(lines_out(7)[:, ON_SCALAR:P], lines_in(7)[:, ON_SCALAR:P])
         close_span()
         quantise_weights(6, 2, si_late[:])
         transform(1, 0, 2)

@@ -23,7 +23,7 @@ PASS = P * PACK
 HALF = PASS // 2
 JT = 512
 LIST_COLS = JT // 16
-BESIDE = 208
+BESIDE = 240
 BESIDE_SHORT = 64
 SPACER = 96
 ON_SCALAR = 32
@@ -104,36 +104,35 @@ def tile_list_meltab_log_kernel(
         def round_weight(c):
             nc.vector.tensor_copy(lines_out(c), lines_in(c))
 
-        def code_tiles(c, n):
-            codes = keep.tile([P, n * PASS], U32, name=f"w_codes{c}", align_bytes=256)
-            plane = keep.tile([P, n * PASS], U8, name=f"w_plane{c}", align_bytes=256)
-            for k in range(n):
-                w_codes[c + k], w_plane[c + k] = codes[:, k * PASS : (k + 1) * PASS], plane[:, k * PASS : (k + 1) * PASS]
-                for t in range(PACK):
-                    stationary[c + k, t] = w_codes[c + k][:, t * P : (t + 1) * P], w_plane[c + k][:, t * P : (t + 1) * P]
+        def code_tiles(c):
+            codes = keep.tile([P, PASS], U32, name=f"w_codes{c}", align_bytes=256)
+            plane = keep.tile([P, PASS], U8, name=f"w_plane{c}", align_bytes=256)
+            w_codes[c], w_plane[c] = codes[:], plane[:]
+            for t in range(PACK):
+                stationary[c, t] = codes[:, t * P : (t + 1) * P], plane[:, t * P : (t + 1) * P]
             return codes, plane
 
         def quantise_half(c, u, values):
             cols = slice(u * HALF, (u + 1) * HALF)
             nc.vector.quantize_mx(w_codes[c][:, cols].bitcast(FP8X4), w_plane[c][:, cols], values)
 
-        def quantise_weights(c, n, values):
-            codes, plane = code_tiles(c, n)
-            nc.vector.quantize_mx(codes[:].bitcast(FP8X4), plane[:], values)
+        def quantise_weights(c):
+            codes, plane = code_tiles(c)
+            nc.vector.quantize_mx(codes[:].bitcast(FP8X4), plane[:], rounded[c])
 
-        def rounded_tile(c, n, tag):
-            tile = ring.tile([P, n * PACK * PASS], BF16, name="rounded", tag=tag, align_bytes=256)
-            for k in range(n):
-                rounded[c + k] = tile[:, k * PACK * PASS : (k + 1) * PACK * PASS]
+        def rounded_tile(c, tag):
+            tile = ring.tile([P, PACK * PASS], BF16, name="rounded", tag=tag, align_bytes=256)
+            rounded[c] = tile[:]
             return tile
 
-        def late_pair(c, tags, between):
-            values = [buffer([P, 2, 2 * PASS], BF16, "rounded", tag) for tag in tags]
+        rows16 = [keep.tile([P, 2 * JT * PACK], BF16, name=f"rows16_{k}", align_bytes=256) for k in range(2)]
+
+        def late_pair(c, values, between):
             codes = keep.tile([P, 2, 2, HALF], U32, name=f"w_codes{c}", align_bytes=256)
             plane = keep.tile([P, 2, 2, HALF], U8, name=f"w_plane{c}", align_bytes=256)
             for a in range(2):
                 for u in range(2):
-                    dst = values[u][:, a, :].rearrange("p (v m h l) -> p m h v l", v=2, h=2, l=2)
+                    dst = values[u][:, a * 2 * PASS : (a + 1) * 2 * PASS].rearrange("p (v m h l) -> p m h v l", v=2, h=2, l=2)
                     nc.vector.tensor_copy(dst, in_pairs(raw[c + a][:])[:, u])
                     for v in range(2):
                         stationary[c + a, 2 * u + v] = codes[:, u, a, v * P : (v + 1) * P], plane[:, u, a, v * P : (v + 1) * P]
@@ -142,7 +141,7 @@ def tile_list_meltab_log_kernel(
             for u in range(2):
                 nc.vector.quantize_mx(
                     codes[:, u].rearrange("p a c -> p (a c)").bitcast(FP8X4), plane[:, u].rearrange("p a c -> p (a c)"),
-                    values[u][:].rearrange("p a c -> p (a c)"),
+                    values[u],
                 )
 
         squares, banks, taken = {}, {}, []
@@ -215,8 +214,8 @@ def tile_list_meltab_log_kernel(
                 h_codes[b][:, cols].bitcast(FP8X4), h_plane[b][:, cols], h[b, j0][:, skip:n, :].rearrange("p j t -> p (j t)")
             )
 
-        def open_span(b, j0, n, beside, first=JT):
-            h[b, j0] = ring.tile([P, n, PACK], BF16, name="h", tag=f"h{len(spans) % 2}", align_bytes=256)
+        def open_span(b, j0, n, beside, first=JT, at=0):
+            h[b, j0] = rows16[len(spans) % 2][:, at * PACK : (at + n) * PACK].rearrange("p (j t) -> p j t", t=PACK)
             spans.append((b, j0, n))
             if len(spans) > 1:
                 apply_sign(*spans[-2])
@@ -229,7 +228,9 @@ def tile_list_meltab_log_kernel(
             if n > JT:
                 add_squares(nc.vector, j0 + JT, n - JT)
             if len(spans) > 1:
-                quantise_power(*spans[-2])
+                b, j0, n = spans[-2]
+                for skip in range(0, n, JT):
+                    quantise_power(b, j0, min(n, skip + JT), skip)
 
         def filters(j0, width, in_single, queue):
             cols = slice(j0, j0 + width)
@@ -294,8 +295,8 @@ def tile_list_meltab_log_kernel(
             return half[:].rearrange("p (v m h l) -> p m h v l", v=2, h=2, l=2)
 
         halves = {(0, 0): half_tile("low0"), (0, 1): half_tile("high0"), (1, 0): half_tile("low1"), (1, 1): half_tile("high1")}
-        code_tiles(0, 1)
-        code_tiles(1, 1)
+        code_tiles(0)
+        code_tiles(1)
         nc.scalar.copy(by_pairs(halves[0, 0]), in_pairs(raw[0][:])[:, 0])
         nc.scalar.copy(by_pairs(halves[0, 1]), in_pairs(raw[0][:])[:, 1])
         move_planes(1, "raw0")
@@ -311,27 +312,29 @@ def tile_list_meltab_log_kernel(
         load_weight(5, "mag")
         transform(0, 0, 0)
         transform(0, 0, 1)
-        rounded_tile(2, 1, "high")
+        rounded_tile(2, "high")
         round_weight(2)
         load_weight(6, "raw2")
         part_pairs(2, "high1")
-        quantise_weights(2, 1, rounded[2])
-        rounded_tile(3, 1, "rounded3")
+        quantise_weights(2)
+        rounded_tile(3, "rounded3")
         round_weight(3)
         load_weight(7, "raw3")
         pick_pairs(3, 1, "high")
-        quantise_weights(3, 1, rounded[3])
+        quantise_weights(3)
         transform(0, 0, 2)
         transform(1, 0, 0)
-        late_pair(4, ("h0", "rounded3"), lambda: part_pairs(3, "frames3"))
-        si_late = rounded_tile(6, 2, "h1")
+        high_pair = buffer([P, PACK * PASS], BF16, "rounded", "rounded3")
+        late_pair(4, (rows16[0][:, 0 : PACK * PASS], high_pair[:]), lambda: part_pairs(3, "frames3"))
+        rounded[6], rounded[7] = rows16[1][:, 0 : PACK * PASS], rows16[1][:, PACK * PASS : 2 * PACK * PASS]
         transform(1, 0, 1)
         round_weight(6)
         open_span(0, 0, 2 * JT, 0)
         nc.scalar.copy(lines_out(7)[:, 0:ON_SCALAR], lines_in(7)[:, 0:ON_SCALAR])
         nc.vector.tensor_copy(lines_out(7)[:, ON_SCALAR:P], lines_in(7)[:, ON_SCALAR:P])
         close_span()
-        quantise_weights(6, 2, si_late[:])
+        quantise_weights(6)
+        quantise_weights(7)
         transform(1, 0, 2)
         transform(0, 0, 3)
         transform(1, 0, 3)
@@ -359,7 +362,7 @@ def tile_list_meltab_log_kernel(
         transform(0, 1, 3)
         transform(1, 1, 3, JT // 2)
         last = [(J - JT, 2 * P), (J - 2 * P, P), (J - P, P)]
-        open_span(1, J - JT, 2 * P, BESIDE_SHORT)
+        open_span(1, J - JT, 2 * P, BESIDE_SHORT, at=JT)
         close_span()
         open_span(1, J - 2 * P, 2 * P, 0)
         close_span()
@@ -367,5 +370,5 @@ def tile_list_meltab_log_kernel(
         apply_sign(1, J - 2 * P, 2 * P, P)
         quantise_power(1, J - 2 * P, P)
         quantise_power(1, J - 2 * P, 2 * P, P)
-        for k, (j0, n) in enumerate([(0, JT), (JT, JT), (2 * JT, JT)] + last):
-            filters(j0, n, k == 3, nc.scalar if j0 + n == J else nc.sync)
+        for j0, n in [(0, JT), (JT, JT), (2 * JT, JT)] + last:
+            filters(j0, n, (j0, n) == last[0], nc.scalar if j0 + n == J else nc.sync)

@@ -22,9 +22,11 @@ PACK = 4
 PASS = P * PACK
 HALF = PASS // 2
 JT = 512
+HALF_TILE = JT // 2
 LIST_COLS = JT // 16
 BESIDE = 240
-BESIDE_SHORT = 64
+BESIDE_SHORT = 112
+BESIDE_LAST = 48
 SPACER = 96
 ON_SCALAR = 32
 RUN = 4
@@ -223,14 +225,14 @@ def tile_list_meltab_log_kernel(
                 add_squares(nc.gpsimd, j0, beside)
             add_squares(nc.vector, j0 + beside, min(n, first) - beside)
 
-        def close_span():
+        def close_span(piece=JT, add=JT):
             b, j0, n = spans[-1]
-            if n > JT:
-                add_squares(nc.vector, j0 + JT, n - JT)
+            for j in range(j0 + JT, j0 + n, add):
+                add_squares(nc.vector, j, add)
             if len(spans) > 1:
                 b, j0, n = spans[-2]
-                for skip in range(0, n, JT):
-                    quantise_power(b, j0, min(n, skip + JT), skip)
+                for skip in range(0, n, piece):
+                    quantise_power(b, j0, skip + piece, skip)
 
         def filters(j0, width, in_single, queue):
             cols = slice(j0, j0 + width)
@@ -350,22 +352,23 @@ def tile_list_meltab_log_kernel(
         close_span()
         for jt in range(2):
             transform(0, 1, jt)
-            transform(1, 1, jt)
+            transform(1, 1, jt, (JT, HALF_TILE)[jt])
         open_span(1, 0, 2 * JT, BESIDE)
-        close_span()
+        close_span(add=HALF_TILE)
         transform(0, 1, 2)
         transform(1, 1, 2, BESIDE)
         open_span(1, 2 * JT, JT, BESIDE, BESIDE + SPACER)
         quantise_power(1, 0, JT)
         add_squares(nc.vector, 2 * JT + BESIDE + SPACER, JT - BESIDE - SPACER)
-        quantise_power(1, 0, 2 * JT, JT)
+        quantise_power(1, 0, JT + HALF_TILE, JT)
+        quantise_power(1, 0, 2 * JT, JT + HALF_TILE)
         transform(0, 1, 3)
         transform(1, 1, 3, JT // 2)
         last = [(J - JT, 2 * P), (J - 2 * P, P), (J - P, P)]
-        open_span(1, J - JT, 2 * P, BESIDE_SHORT, at=JT)
-        close_span()
-        open_span(1, J - 2 * P, 2 * P, 0)
-        close_span()
+        open_span(1, J - JT, HALF_TILE, BESIDE_SHORT, at=JT)
+        close_span(HALF_TILE)
+        open_span(1, J - HALF_TILE, HALF_TILE, BESIDE_LAST)
+        close_span(HALF_TILE)
         apply_sign(1, J - 2 * P, P)
         apply_sign(1, J - 2 * P, 2 * P, P)
         quantise_power(1, J - 2 * P, P)

from contextlib import ExitStack

import concourse.mybir as mybir
from concourse.masks import make_identity

K, F, N, T, J = 1024, 1024, 256, 4096, 2048
FLOPS = 2 * (2 * K * F * J + F * N * J)

F32 = mybir.dt.float32
BF16 = mybir.dt.bfloat16
I32 = mybir.dt.int32
U32 = mybir.dt.uint32
U16 = mybir.dt.uint16
U8 = mybir.dt.uint8
FP8X4 = mybir.dt.float8_e4m3fn_x4
FP4X4 = mybir.dt.float4_e2m1fn_x4
ALU = mybir.AluOpType
ACT = mybir.ActivationFunctionType

P = 128
PACK = 4
PASS = P * PACK
HALF = PASS // 2
JT = 512
HALF_TILE = JT // 2
LIST_COLS = JT // 16
BESIDE = 240
BESIDE_SHORT = 112
BESIDE_LAST = 48
SPACER = 96
ON_SCALAR = 32
RUN = 4


def tile_list_meltab_log_kernel(
    tc, tab_words, tab_scales, co, si, gn, fb_words, fb_scales, offs, out
):
    nc = tc.nc
    with ExitStack() as ctx:
        keep = ctx.enter_context(tc.tile_pool(name="keep", bufs=1))
        ring = ctx.enter_context(tc.tile_pool(name="ring", bufs=1))
        psum = ctx.enter_context(tc.psum_pool(name="psum", bufs=1))

        offsets = keep.tile([P, J // 16], U16, name="offsets")
        nc.sync.dma_start(offsets[:], offs)

        scale_store = keep.tile([P, T], U8, name="scale_store", align_bytes=256)
        nc.vector.memset(scale_store[0:96, :].bitcast(I32), 0)
        nc.sync.dma_start(scale_store[96:128, :].bitcast(I32), tab_scales.rearrange("a z t -> z a t").bitcast(I32))
        gain = keep.tile([P, 2, PACK], F32, name="gain")
        nc.scalar.dma_start(gain[:], gn.rearrange("(b p t) -> p b t", b=2, t=PACK))

        def weight_rows(c, c0, n):
            b, w, a = c // 4, c // 2 % 2, c % 2
            rows = (co, si)[w][a * PASS : (a + 1) * PASS, b * PASS + c0 : b * PASS + c0 + n]
            return rows.rearrange("(p i) c -> p i c", i=PACK)

        raw = {}
        def buffer(shape, dtype, name, where):
            return ring.tile(shape, dtype, name=name, tag=where, align_bytes=256)

        def load_weight(c, where):
            raw[c] = buffer([P, PACK, PASS], F32, f"raw{c}", where)
            nc.sync.dma_start(raw[c][:], weight_rows(c, 0, PASS))

        word_store = keep.tile([P, T], I32, name="word_store", align_bytes=256)
        nc.sync.dma_start(word_store[:], tab_words[0].rearrange("p t i -> p (t i)").bitcast(I32))

        load_weight(0, "raw0")

        g8 = gain[:].rearrange("p b t -> p (b t)")
        mag = buffer([P, 2 * PACK], F32, "mag", "mag")
        root = keep.tile([P, 2 * PACK], F32, name="root")
        identity = keep.tile([P, P], BF16, name="identity")
        make_identity(nc, identity[:])
        nc.scalar.activation(mag[:], g8, ACT.Abs)
        repeated = keep.tile([P, P // 8, 8], BF16, name="repeated")
        nc.scalar.activation(repeated[:], g8.unsqueeze(1).to_broadcast([P, P // 8, 8]), ACT.Sign)
        nc.scalar.activation(root[:], mag[:], ACT.Sqrt)

        warm = keep.tile([P, 1], F32, name="warm")
        nc.scalar.activation(warm[:], root[:, 0:1], ACT.Ln, bias=1.0)

        pairs, frames = {}, {}
        def pick_pairs(jt, n, where):
            tile = buffer([P, n * JT], U32, f"pairs{jt}", where)
            for k in range(n):
                pairs[jt + k] = tile[:, k * JT : (k + 1) * JT]
            cols = offsets[:, jt * LIST_COLS : (jt + n) * LIST_COLS]
            nc.vector.tensor_copy(tile[:], word_store[:].bitcast(U32).indirect(cols))

        def part_pairs(jt, where):
            frames[jt] = buffer([P, 2, JT], U16, f"frames{jt}", where)
            nc.vector.tensor_copy(frames[jt][:], pairs[jt].bitcast(U16).rearrange("p (j d) -> p d j", d=2))

        rounded, w_codes, w_plane, stationary = {}, {}, {}, {}
        def in_pairs(src):
            return src.rearrange("p (h l) (m u v) -> p u m h v l", l=2, u=2, v=2)

        def lines_in(c):
            return raw[c][:].rearrange("p (h l) (m t) -> p m h t l", l=2, t=PACK)

        def lines_out(c):
            return rounded[c].rearrange("p (t m h l) -> p m h t l", t=PACK, h=2, l=2)

        def round_weight(c):
            nc.vector.tensor_copy(lines_out(c), lines_in(c))

        def code_tiles(c):
            codes = keep.tile([P, PASS], U32, name=f"w_codes{c}", align_bytes=256)
            plane = keep.tile([P, PASS], U8, name=f"w_plane{c}", align_bytes=256)
            w_codes[c], w_plane[c] = codes[:], plane[:]
            for t in range(PACK):
                stationary[c, t] = codes[:, t * P : (t + 1) * P], plane[:, t * P : (t + 1) * P]
            return codes, plane

        def quantise_half(c, u, values):
            cols = slice(u * HALF, (u + 1) * HALF)
            nc.vector.quantize_mx(w_codes[c][:, cols].bitcast(FP8X4), w_plane[c][:, cols], values)

        def quantise_weights(c):
            codes, plane = code_tiles(c)
            nc.vector.quantize_mx(codes[:].bitcast(FP8X4), plane[:], rounded[c])

        def rounded_tile(c, tag):
            tile = ring.tile([P, PACK * PASS], BF16, name="rounded", tag=tag, align_bytes=256)
            rounded[c] = tile[:]
            return tile

        rows16 = [keep.tile([P, 2 * JT * PACK], BF16, name=f"rows16_{k}", align_bytes=256) for k in range(2)]

        def late_pair(c, values, between):
            codes = keep.tile([P, 2, 2, HALF], U32, name=f"w_codes{c}", align_bytes=256)
            plane = keep.tile([P, 2, 2, HALF], U8, name=f"w_plane{c}", align_bytes=256)
            for a in range(2):
                for u in range(2):
                    dst = values[u][:, a * 2 * PASS : (a + 1) * 2 * PASS].rearrange("p (v m h l) -> p m h v l", v=2, h=2, l=2)
                    nc.vector.tensor_copy(dst, in_pairs(raw[c + a][:])[:, u])
                    for v in range(2):
                        stationary[c + a, 2 * u + v] = codes[:, u, a, v * P : (v + 1) * P], plane[:, u, a, v * P : (v + 1) * P]
                if a == 0:
                    between()
            for u in range(2):
                nc.vector.quantize_mx(
                    codes[:, u].rearrange("p a c -> p (a c)").bitcast(FP8X4), plane[:, u].rearrange("p a c -> p (a c)"),
                    values[u],
                )

        squares, banks, taken = {}, {}, []
        def next_bank():
            if not banks:
                taken.append(None)
                first_bank = psum.tile([P, JT], F32, name="single")
                return first_bank[:]
            if len(taken) % 2 == 0 or taken[-1] is None:
                pair = psum.tile([P, 2, JT], F32, name="pair", bufs=3)
            else:
                pair = taken[-1]
            taken.append(pair)
            return pair[:, (len(taken) - 1) % 2, :]

        def product(w, b, jt, t, a):
            if a == 0:
                banks[w, b, jt, t] = next_bank()
            c = 4 * b + 2 * w + a
            nc.tensor.matmul_mx(
                banks[w, b, jt, t],
                lhsT=stationary[c, t][0].bitcast(FP8X4),
                lhsT_scale=stationary[c, t][1],
                rhs=frames[jt][:, a, :].bitcast(FP4X4),
                rhs_scale=tab_planes[jt // 2][:, a, jt % 2 * JT : (jt % 2 + 1) * JT],
                start=(a == 0),
                stop=(a == 1),
            )

        def square(w, b, jt, t, c0, n):
            if (w, b, jt * JT + c0) not in squares:
                squares[w, b, jt * JT + c0] = ring.tile([P, PACK, n], F32, name=f"squares{w}", bufs=4, align_bytes=256)
            nc.scalar.activation(
                squares[w, b, jt * JT + c0][:, t, :], banks[w, b, jt, t][:, c0 : c0 + n], ACT.Square,
                scale=root[:, PACK * b + t : PACK * b + t + 1],
            )

        def transform(w, b, jt, cut=JT):
            for t0 in range(0, PACK, 2):
                for a in range(2):
                    for t in (t0, t0 + 1):
                        product(w, b, jt, t, a)
                for t in (t0, t0 + 1):
                    square(w, b, jt, t, 0, cut)
            if cut < JT:
                for t in range(PACK):
                    square(w, b, jt, t, cut, JT - cut)

        def squared(w, b, j0, n):
            start = max(j for (ww, bb, j) in squares if (ww, bb) == (w, b) and j <= j0)
            return squares[w, b, start][:, :, j0 - start : j0 - start + n].rearrange("p t (c i) -> p c t i", i=RUN)

        h_codes = [keep.tile([P, J], U32, name=f"h_codes{b}", align_bytes=256) for b in range(2)]
        h_plane = [keep.tile([P, J], U8, name=f"h_plane{b}", align_bytes=256) for b in range(2)]
        h, spans = {}, []
        def add_squares(engine, j0, n):
            b, span0, width = spans[-1]
            dst = h[b, span0][:, j0 - span0 : j0 - span0 + n, :]
            engine.tensor_tensor(
                dst.rearrange("p (c i) t -> p c t i", i=RUN), squared(0, b, j0, n), squared(1, b, j0, n), ALU.add
            )

        def apply_sign(b, j0, n, skip=0):
            signs = sign[:, PACK * b : PACK * (b + 1)].unsqueeze(1).to_broadcast([P, n - skip, PACK])
            nc.vector.tensor_tensor(h[b, j0][:, skip:n, :], h[b, j0][:, skip:n, :], signs, ALU.mult)

        def quantise_power(b, j0, n, skip=0):
            cols = slice(j0 + skip, j0 + n)
            nc.vector.quantize_mx(
                h_codes[b][:, cols].bitcast(FP8X4), h_plane[b][:, cols], h[b, j0][:, skip:n, :].rearrange("p j t -> p (j t)")
            )

        def open_span(b, j0, n, beside, first=JT, at=0):
            h[b, j0] = rows16[len(spans) % 2][:, at * PACK : (at + n) * PACK].rearrange("p (j t) -> p j t", t=PACK)
            spans.append((b, j0, n))
            if len(spans) > 1:
                apply_sign(*spans[-2])
            if beside:
                add_squares(nc.gpsimd, j0, beside)
            add_squares(nc.vector, j0 + beside, min(n, first) - beside)

        def close_span(piece=JT, add=JT):
            b, j0, n = spans[-1]
            for j in range(j0 + JT, j0 + n, add):
                add_squares(nc.vector, j, add)
            if len(spans) > 1:
                b, j0, n = spans[-2]
                for skip in range(0, n, piece):
                    quantise_power(b, j0, skip + piece, skip)

        def filters(j0, width, in_single, queue):
            cols = slice(j0, j0 + width)
            per_bank = min(N // P, JT // width)
            if in_single:
                single = psum.tile([P, 2, width], F32, name="single")
                y = single[:]
            else:
                pair = psum.tile([P, 2, JT], F32, name="pair", bufs=3)
                y = pair[:].rearrange("p k j -> p (k j)")[:, 0 : 2 * width].rearrange("p (n j) -> p n j", n=2)
            for b in range(2):
                for nt in range(N // P):
                    nc.tensor.matmul_mx(
                        y[:, nt, :],
                        lhsT=fb_codes[:, b, nt * P : (nt + 1) * P].bitcast(FP8X4),
                        lhsT_scale=fb_plane[:, b, nt * P : (nt + 1) * P],
                        rhs=h_codes[b][:, cols].bitcast(FP8X4),
                        rhs_scale=h_plane[b][:, cols],
                        start=(b == 0 and nt % per_bank == 0),
                        stop=(b == 1 and nt % per_bank == per_bank - 1),
                    )
            for n0 in range(0, N // P, per_bank):
                result = ring.tile([P, per_bank, width], F32, name="result", bufs=9, align_bytes=256)
                nc.scalar.activation(result[:], y[:, n0 : n0 + per_bank, :], ACT.Ln, bias=1.0)
                rows = out[n0 * P : (n0 + per_bank) * P, cols]
                queue.dma_start(rows.rearrange("(n p) j -> p n j", p=P), result[:])

        picked, tab_planes = {}, {}
        def pick_scales(k):
            picked[k] = buffer([P, 2 * JT], U8, "picked", ("raw2", "picked1")[k])
            cols = offsets[:, 2 * k * LIST_COLS : 2 * (k + 1) * LIST_COLS]
            nc.vector.tensor_copy(picked[k][:], scale_store[:].indirect(cols))

        def move_planes(k, where):
            tab_planes[k] = buffer([P, 2, 2 * JT], U8, f"tab_planes{k}", where)
            for q in range(4):
                nc.sync.dma_start(
                    tab_planes[k][32 * q : 32 * q + 4, :, :].bitcast(I32),
                    picked[k][96 + 8 * q : 96 + 8 * q + 8, :].bitcast(I32),
                )

        pick_scales(0)
        move_planes(0, "planes0")
        pick_scales(1)
        turned = keep.tile([P, P], BF16, name="turned")
        sign_bank = psum.tile([P, 2, P], BF16, name="sign_bank")
        sign = sign_bank[:, 0, :]
        nc.tensor.transpose(sign_bank[:, 1, :], repeated[:].rearrange("p r e -> p (r e)"), identity[:])
        load_weight(1, "mag")
        nc.scalar.copy(turned[:], sign_bank[:, 1, :])
        nc.tensor.transpose(sign, turned[:], identity[:])
        load_weight(2, "raw2")
        pick_pairs(0, 1, "raw3")
        pick_pairs(1, 1, "pairs1")
        part_pairs(0, "frames0")
        load_weight(3, "raw3")

        def half_tile(tag):
            return ring.tile([P, 2 * PASS], BF16, name="half", tag=tag, align_bytes=256)

        def by_pairs(half):
            return half[:].rearrange("p (v m h l) -> p m h v l", v=2, h=2, l=2)

        halves = {(0, 0): half_tile("low0"), (0, 1): half_tile("high0"), (1, 0): half_tile("low1"), (1, 1): half_tile("high1")}
        code_tiles(0)
        code_tiles(1)
        nc.scalar.copy(by_pairs(halves[0, 0]), in_pairs(raw[0][:])[:, 0])
        nc.scalar.copy(by_pairs(halves[0, 1]), in_pairs(raw[0][:])[:, 1])
        move_planes(1, "raw0")
        quantise_half(0, 0, halves[0, 0][:])
        nc.scalar.copy(by_pairs(halves[1, 0]), in_pairs(raw[1][:])[:, 0])
        nc.scalar.copy(by_pairs(halves[1, 1]), in_pairs(raw[1][:])[:, 1])
        pick_pairs(2, 1, "low0")
        quantise_half(0, 1, halves[0, 1][:])
        load_weight(4, "high0")
        quantise_half(1, 0, halves[1, 0][:])
        part_pairs(1, "low1")
        quantise_half(1, 1, halves[1, 1][:])
        load_weight(5, "mag")
        transform(0, 0, 0)
        transform(0, 0, 1)
        rounded_tile(2, "high")
        round_weight(2)
        load_weight(6, "raw2")
        part_pairs(2, "high1")
        quantise_weights(2)
        rounded_tile(3, "rounded3")
        round_weight(3)
        load_weight(7, "raw3")
        pick_pairs(3, 1, "high")
        quantise_weights(3)
        transform(0, 0, 2)
        transform(1, 0, 0)
        high_pair = buffer([P, PACK * PASS], BF16, "rounded", "rounded3")
        late_pair(4, (rows16[0][:, 0 : PACK * PASS], high_pair[:]), lambda: part_pairs(3, "frames3"))
        rounded[6], rounded[7] = rows16[1][:, 0 : PACK * PASS], rows16[1][:, PACK * PASS : 2 * PACK * PASS]
        transform(1, 0, 1)
        round_weight(6)
        open_span(0, 0, 2 * JT, 0)
        nc.scalar.copy(lines_out(7)[:, 0:ON_SCALAR], lines_in(7)[:, 0:ON_SCALAR])
        nc.vector.tensor_copy(lines_out(7)[:, ON_SCALAR:P], lines_in(7)[:, ON_SCALAR:P])
        close_span()
        quantise_weights(6)
        quantise_weights(7)
        transform(1, 0, 2)
        transform(0, 0, 3)
        transform(1, 0, 3)
        open_span(0, 2 * JT, 2 * JT, BESIDE)
        fb_codes = buffer([P, 2, N], I32, "fb_codes", "high0")
        nc.sync.dma_start(fb_codes[:], fb_words.rearrange("b p n i -> p b (n i)").bitcast(I32))
        fb_plane = buffer([P, 2, N], U8, "fb_plane", "mag")
        for q in range(4):
            nc.sync.dma_start(
                fb_plane[32 * q : 32 * q + 4, :, :].bitcast(I32),
                fb_scales[:, 4 * q : 4 * q + 4, :].rearrange("b r n -> r b n").bitcast(I32),
            )
        close_span()
        for jt in range(2):
            transform(0, 1, jt)
            transform(1, 1, jt, (JT, HALF_TILE)[jt])
        open_span(1, 0, 2 * JT, BESIDE)
        close_span(add=HALF_TILE)
        transform(0, 1, 2)
        transform(1, 1, 2, BESIDE)
        open_span(1, 2 * JT, JT, BESIDE, BESIDE + SPACER)
        quantise_power(1, 0, JT)
        add_squares(nc.vector, 2 * JT + BESIDE + SPACER, JT - BESIDE - SPACER)
        quantise_power(1, 0, JT + HALF_TILE, JT)
        quantise_power(1, 0, 2 * JT, JT + HALF_TILE)
        transform(0, 1, 3)
        transform(1, 1, 3, JT // 2)
        last = [(J - JT, 2 * P), (J - 2 * P, P), (J - P, P)]
        open_span(1, J - JT, HALF_TILE, BESIDE_SHORT, at=JT)
        close_span(HALF_TILE)
        open_span(1, J - HALF_TILE, HALF_TILE, BESIDE_LAST)
        close_span(HALF_TILE)
        apply_sign(1, J - 2 * P, P)
        apply_sign(1, J - 2 * P, 2 * P, P)
        quantise_power(1, J - 2 * P, P)
        quantise_power(1, J - 2 * P, 2 * P, P)
        for j0, n in [(0, JT), (JT, JT), (2 * JT, JT)] + last:
            filters(j0, n, (j0, n) == last[0], nc.scalar if j0 + n == J else nc.sync)
